import numpy as np
import ml_dtypes


def mxq(x, axis, fmt="e4m3"):
    dtype, down = {"e4m3": (ml_dtypes.float8_e4m3fn, 7), "e5m2": (ml_dtypes.float8_e5m2, 14)}[fmt]
    v = np.moveaxis(np.asarray(x, np.float32).astype(ml_dtypes.bfloat16).astype(np.float64), axis, -1)
    blocks = v.reshape(v.shape[:-1] + (-1, 32))
    amax = np.abs(blocks).max(-1, keepdims=True)
    byte = np.maximum(np.where(amax > 0, np.frexp(amax)[1] - 1 + 127, 0) - down, 1)
    scale = np.exp2(byte - 127.0)
    codes = (blocks / scale).astype(np.float32).astype(dtype).astype(np.float64)
    return np.moveaxis((codes * scale).reshape(v.shape), -1, axis)


WIDE = False


def mx_kscale(k):
    if not WIDE:
        return np.ones(k)
    levels = np.array([10, -10, 5, -5, 0])
    if k % 512:
        return np.exp2(np.random.permutation(np.resize(levels, k // 32))).repeat(32)
    a = np.empty((k // 512, 16))
    for p in range(k // 512):
        a[p, :8] = np.random.permutation(np.resize(levels, 8))
        for g in range(8):
            far = levels[np.abs(levels - a[p, g]) >= 10]
            a[p, g + 8] = far[np.random.randint(len(far))]
    return np.exp2(a.ravel()).repeat(32)


def f64(x):
    return np.asarray(x).astype(np.float64)


def striped8(idx):
    return np.asarray(idx).reshape(8, -1, 16).transpose(0, 2, 1).reshape(128, -1).astype(np.uint16)


def unstriped8(offs):
    return offs.reshape(8, 16, -1).transpose(0, 2, 1).reshape(8, -1).astype(np.int64)


def pick8(x, idx, run):
    r = np.arange(len(x))
    return x[r[:, None], idx[r % (8 * run) // run]]


E2M1 = np.array([0.0, 0.5, 1.0, 1.5, 2.0, 3.0, 4.0, 6.0, -0.0, -0.5, -1.0, -1.5, -2.0, -3.0, -4.0, -6.0])


def pack_weight(w, fmt):
    k, n = w.shape
    w = f64(np.asarray(w, np.float32).astype(ml_dtypes.bfloat16)).reshape(k // 32, 32, n)
    amax = np.abs(w).max(1)
    if fmt == "e4m3":
        byte = np.frexp(amax)[1] - 1 + 127 - 7
    else:
        mant, ex = np.frexp(amax / 6.0)
        byte = np.where(mant > 0.5, ex, ex - 1) + 127
    byte = np.clip(np.where(amax > 0, byte, 1), 1, 254)
    scaled = (w * np.exp2(127.0 - byte)[:, None, :]).reshape(k, n).astype(np.float32)
    by_word = np.ascontiguousarray(scaled.reshape(k // 512, 128, 4, n).transpose(0, 1, 3, 2))
    if fmt == "e4m3":
        words = by_word.astype(ml_dtypes.float8_e4m3fn).view(np.uint8)
    else:
        c = by_word.astype(ml_dtypes.float4_e2m1fn).view(np.uint8) & 0xF
        words = (c[..., 0::2] | (c[..., 1::2] << 4)).reshape(k // 512, 128, 2 * n)
    return np.ascontiguousarray(words), np.ascontiguousarray(byte.astype(np.uint8).reshape(k // 512, 16, n))


def unpack_weight(words, scales, fmt):
    g, _, n = scales.shape
    words = np.ascontiguousarray(words).reshape(g, 128, n, -1)
    if fmt == "e4m3":
        vals = words.view(ml_dtypes.float8_e4m3fn).astype(np.float64)
    else:
        nib = np.empty((g, 128, n, 4), np.uint8)
        nib[..., 0::2] = words & 0xF
        nib[..., 1::2] = words >> 4
        vals = E2M1[nib]
    vals = vals * np.repeat(np.exp2(scales.astype(np.float64) - 127.0), 8, axis=1)[..., None]
    return vals.transpose(0, 1, 3, 2).reshape(g * 512, n)


def sigmoid(v):
    return 1.0 / (1.0 + np.exp(-v))


def bf(x):
    return np.asarray(x, np.float32).astype(ml_dtypes.bfloat16)


def planes(Y):
    r, m = Y.shape
    b = f64(bf(Y)).reshape(r // 32, 32, m)
    amax = np.abs(b).max(1)
    byte = np.clip(np.where(amax > 0, np.frexp(amax)[1] - 1 + 127 - 7, 1), 1, 254)
    codes = (b * np.exp2(127.0 - byte)[:, None, :]).reshape(r, m).astype(np.float32).astype(ml_dtypes.float8_e4m3fn).view(np.uint8)
    words = codes.reshape(r // 512, 128, 4, m).transpose(0, 1, 3, 2)
    return np.ascontiguousarray(words), np.ascontiguousarray(byte.astype(np.uint8).reshape(r // 512, 16, m))


D, T, Q, I, E = 512, 1024, 512, 512, 512


def setup_inputs():
    n = np.random.standard_normal
    idx = np.stack([np.random.permutation(T)[:I] for _ in range(8)])
    fd = mx_kscale(D)
    ft = mx_kscale(T)
    keysp = pack_weight(n((D, T)) / fd[:, None], "e2m1")
    return {
        "query": (n((D, Q)) * 0.4 / np.sqrt(D) * fd[:, None]).astype(np.float32),
        "keys_words": keysp[0],
        "keys_scales": keysp[1],
        "th": (np.random.uniform(-0.5, 1.5, (Q, 1))).astype(np.float32),
        "fac": (np.random.uniform(0.5, 2.0, (T, 1)) * ft[:, None]).astype(np.float32),
        "vals": (n((T, E)) / ft[:, None]).astype(np.float32),
        "offs": striped8(idx),
    }


def reference(query, keys_words, keys_scales, th, fac, vals, offs):
    idx = unstriped8(offs)
    keysu = unpack_weight(keys_words, keys_scales, "e2m1")
    queryq = mxq(f64(query), 0, "e4m3")
    a = queryq.T @ keysu
    w = sigmoid(pick8(a, idx, 64) - f64(th))
    wf = np.zeros((Q, T))
    wf[np.arange(Q)[:, None], idx[np.arange(Q) % 512 // 64]] = w
    wt = wf.T
    wg = wt * f64(fac) * 0.1
    valsq = mxq(f64(vals), 0, "e4m3")
    wgq = mxq(wg, 0, "e4m3")
    o = valsq.T @ wgq
    words, scales = planes(o)
    return o, words, scales

@@ -1,0 +1,264 @@
+from contextlib import ExitStack
+
+import concourse.mybir as mybir
+from concourse.masks import make_identity
+
+D, T, Q, SLOTS, E = 512, 1024, 512, 512, 512
+FLOPS = 2 * D * Q * T + 2 * T * E * Q
+
+F32 = mybir.dt.float32
+BF16 = mybir.dt.bfloat16
+I32 = mybir.dt.int32
+U32 = mybir.dt.uint32
+U16 = mybir.dt.uint16
+U8 = mybir.dt.uint8
+FP8X4 = mybir.dt.float8_e4m3fn_x4
+FP4X4 = mybir.dt.float4_e2m1fn_x4
+MULT = mybir.AluOpType.mult
+COPY = mybir.ActivationFunctionType.Copy
+SIGMOID = mybir.ActivationFunctionType.Sigmoid
+
+P = 128
+PACK = 4
+K_PASS = P * PACK
+HEADS = 8
+GROUP = 16
+TILES = Q // P
+PASSES = T // K_PASS
+BANK = 512
+
+
+def tile_attend_mqa_ownlists_gated_kernel(tc, query, keys_words, keys_scales, th, fac, vals, offs, out_0, out_1, out_2):
+    nc = tc.nc
+    with ExitStack() as ctx:
+        keep = ctx.enter_context(tc.tile_pool(name="keep", bufs=1))
+        ring = ctx.enter_context(tc.tile_pool(name="ring", bufs=2))
+        psum = ctx.enter_context(tc.psum_pool(name="psum", bufs=2))
+
+        k_scales = keep.tile([P, T], U8, name="k_scales", align_bytes=64)
+        nc.gpsimd.memset(k_scales[:].bitcast(I32), 0)
+        th_rows = keep.tile([P, P], F32, name="th_rows", tag="v_raw1")
+        nc.gpsimd.memset(th_rows[:], 0.0)
+        offsets = keep.tile([P, SLOTS // GROUP], U16, name="offsets")
+        nc.sync.dma_start(offsets[:], offs)
+        fac_col = keep.tile([P, T // P], F32, name="fac_col", tag="v_raw0")
+        nc.sync.dma_start(fac_col[:], fac.rearrange("(p c) o -> p (c o)", p=P))
+        q_raw = keep.tile([P, PACK, Q], F32, name="q_raw")
+        nc.sync.dma_start(q_raw[:], query.rearrange("(p t) q -> p t q", t=PACK))
+        for quad in range(4):
+            nc.sync.dma_start(
+                k_scales[32 * quad : 32 * quad + 4, :].bitcast(I32),
+                keys_scales[0, 4 * quad : 4 * quad + 4, :].bitcast(I32),
+            )
+        k_words = keep.tile([P, 2 * T], U8, name="k_words", align_bytes=64)
+        nc.sync.dma_start(k_words[:].bitcast(I32), keys_words[0].bitcast(I32))
+        nc.sync.dma_start(
+            th_rows[0:TILES, :].rearrange("j (h r) -> j h r", r=GROUP),
+            th.rearrange("(h j r) o -> j h (r o)", h=HEADS, j=TILES),
+        )
+
+        ident = keep.tile([P, P], F32, name="ident")
+        make_identity(nc, ident[:])
+
+        cold = keep.tile([P, 1], F32, name="cold")
+        nc.vector.memset(cold[:], 0.0)
+        warm = keep.tile([P, 1], F32, name="warm")
+        nc.scalar.activation(warm[:], cold[:], SIGMOID)
+
+        windows = [keep.tile([P, T], F32, name="placed%d" % j) for j in range(2)]
+        for window in windows:
+            nc.vector.memset(window[:], 0.0)
+        placed = [windows[j % 2] for j in range(TILES)]
+
+        fac_row = keep.tile([P, T], F32, name="fac_row")
+        for half in range(2):
+            spread = psum.tile([P, PACK, P], F32, name="spread", tag="score%d" % half, bufs=1)
+            for c in range(PACK):
+                col = PACK * half + c
+                nc.tensor.transpose(spread[:, c, :], fac_col[:, col : col + 1].to_broadcast([P, P]), ident[:])
+            nc.scalar.activation(
+                fac_row[:].rearrange("m (n h c) -> m h n c", h=2, c=PACK)[:, half],
+                spread[:].rearrange("m c n -> m n c"),
+                COPY,
+                scale=0.1,
+            )
+        th_turned = psum.tile([P, P], F32, name="th_turned", tag="turn")
+        nc.tensor.transpose(th_turned[:], th_rows[:], ident[:])
+        neg_th = keep.tile([P, TILES], F32, name="neg_th")
+        nc.scalar.activation(neg_th[:], th_turned[:, 0:TILES], COPY, scale=-1.0)
+
+        v_raw = [keep.tile([P, PACK, E], F32, name="v_raw%d" % g, tag="v_raw%d" % g) for g in range(PASSES)]
+        for g in range(PASSES):
+            nc.sync.dma_start(v_raw[g][:], vals[g * K_PASS : (g + 1) * K_PASS, :].rearrange("(p t) e -> p t e", t=PACK))
+
+        q_codes, q_scales = [], []
+
+        def quantise_queries(j):
+            woven = keep.tile([P, P, PACK], BF16, name="q_woven%d" % j, align_bytes=64)
+            weave = nc.vector.tensor_copy if j < 2 else nc.scalar.copy
+            weave(
+                woven[:].rearrange("p (h c i) t -> p h c t i", h=HEADS, i=4),
+                q_raw[:].rearrange("p t (h j c i) -> p j h c t i", h=HEADS, j=TILES, i=4)[:, j],
+            )
+            codes = keep.tile([P, P], U32, name="q_codes%d" % j, align_bytes=64)
+            scales = keep.tile([P, P], U8, name="q_scales%d" % j, align_bytes=64)
+            nc.vector.quantize_mx(codes[:].bitcast(FP8X4), scales[:], woven[:].rearrange("p q t -> p (q t)"))
+            q_codes.append(codes)
+            q_scales.append(scales)
+
+        scores, picked, gates = {}, {}, {}
+
+        def score(j):
+            scores[j] = keep.tile([P, T], F32, name="scores%d" % j, tag="scores%d" % j, align_bytes=64)
+            for h in range(T // BANK):
+                bank = psum.tile([P, BANK], F32, name="bank", tag="score%d" % h, bufs=1)
+                nc.tensor.matmul_mx(
+                    bank[:],
+                    lhsT=q_codes[j][:].bitcast(FP8X4),
+                    lhsT_scale=q_scales[j][:],
+                    rhs=k_words[:, 2 * BANK * h : 2 * BANK * (h + 1)].bitcast(FP4X4),
+                    rhs_scale=k_scales[:, BANK * h : BANK * (h + 1)],
+                    start=True,
+                    stop=True,
+                )
+                if j == 0 and h == 1:
+                    nc.vector.tensor_copy(scores[j][:, BANK * h : BANK * (h + 1)], bank[:])
+                else:
+                    nc.scalar.copy(scores[j][:, BANK * h : BANK * (h + 1)], bank[:])
+
+        def pick(j):
+            tag = "w_woven1_1" if j == TILES - 1 else "picked%d" % j
+            picked[j] = keep.tile([P, SLOTS], F32, name="picked%d" % j, tag=tag, align_bytes=64)
+            nc.vector.tensor_copy(picked[j][:], scores[j][:].indirect(offsets[:]))
+
+        def gate(j):
+            gates[j] = keep.tile([P, SLOTS], F32, name="gate%d" % j)
+            nc.scalar.activation(gates[j][:], picked[j][:], SIGMOID, bias=neg_th[:, j : j + 1])
+
+        def place(j):
+            nc.vector.tensor_copy(placed[j][:].indirect(offsets[:]), gates[j][:])
+
+        w_woven = {}
+
+        def weigh_and_turn(j):
+            for g in range(PASSES):
+                cols = slice(g * K_PASS, (g + 1) * K_PASS)
+                weighted = ring.tile([P, K_PASS], BF16, name="weighted", tag="weighted%d" % g)
+                engine = nc.vector if j == TILES - 1 else nc.gpsimd
+                engine.tensor_tensor(weighted[:], placed[j][:, cols], fac_row[:, cols], MULT)
+                words = weighted[:].bitcast(F32)
+                turned = psum.tile([P, 2, P], F32, name="turned", tag="turn")
+                for u in range(2):
+                    nc.tensor.transpose(turned[:, u, :], words[:, u : 2 * P : 2], ident[:])
+                woven = keep.tile([P, P, PACK], BF16, name="w_woven", tag="w_woven%d_%d" % (j, g), align_bytes=64)
+                nc.scalar.copy(
+                    woven[:].rearrange("p q t -> p (q t)").bitcast(F32).rearrange("p (q u) -> p q u", u=2),
+                    turned[:].rearrange("p u q -> p q u"),
+                )
+                w_woven[j, g] = woven
+
+        w_codes, w_scales = {}, {}
+
+        def quantise_weights(j):
+            for g in range(PASSES):
+                codes = keep.tile([P, P], U32, name="w_codes%d_%d" % (j, g), align_bytes=64)
+                scales = keep.tile([P, P], U8, name="w_scales%d_%d" % (j, g), align_bytes=64)
+                nc.vector.quantize_mx(codes[:].bitcast(FP8X4), scales[:], w_woven[j, g][:].rearrange("p q t -> p (q t)"))
+                w_codes[j, g] = codes
+                w_scales[j, g] = scales
+
+        v_woven = [keep.tile([P, PACK, P, PACK], BF16, name="v_woven%d" % g, tag="v_woven%d" % g, align_bytes=64) for g in range(PASSES)]
+        v_codes = {}
+        v_scales = [keep.tile([P, E], U8, name="v_scales%d" % g, align_bytes=64) for g in range(PASSES)]
+
+        def weave_values(g, half):
+            s = slice(half * P // 2, (half + 1) * P // 2)
+            nc.scalar.copy(
+                v_woven[g][:].rearrange("p r s t -> p s t r")[:, s],
+                v_raw[g][:].rearrange("p t (s r) -> p s t r", r=PACK)[:, s],
+            )
+
+        def quantise_values(g):
+            tag = "scores%d" % (TILES - 1) if g == PASSES - 1 else "v_codes"
+            v_codes[g] = keep.tile([P, E], U32, name="v_codes%d" % g, tag=tag, align_bytes=64)
+            nc.vector.quantize_mx(v_codes[g][:].bitcast(FP8X4), v_scales[g][:], v_woven[g][:].rearrange("p r s t -> p (r s t)"))
+
+        result = keep.tile([P, PACK, Q], F32, name="result")
+        o_woven = keep.tile([P, Q, PACK], BF16, name="o_woven", align_bytes=64)
+
+        def mix_values(j):
+            mixed = psum.tile([P, PACK, P], F32, name="mixed", tag="mixed")
+            for r in range(PACK):
+                for g in range(PASSES):
+                    nc.tensor.matmul_mx(
+                        mixed[:, r, :],
+                        lhsT=v_codes[g][:, r * P : (r + 1) * P].bitcast(FP8X4),
+                        lhsT_scale=v_scales[g][:, r * P : (r + 1) * P],
+                        rhs=w_codes[j, g][:].bitcast(FP8X4),
+                        rhs_scale=w_scales[j, g][:],
+                        start=(g == 0),
+                        stop=(g == PASSES - 1),
+                    )
+            nc.scalar.copy(
+                result[:].rearrange("p r (h j i) -> p j r h i", h=HEADS, j=TILES)[:, j],
+                mixed[:].rearrange("p r (h i) -> p r h i", h=HEADS),
+            )
+            if j >= TILES - 2:
+                nc.vector.tensor_copy(
+                    o_woven[:].rearrange("p (h j c i) r -> p j h c r i", h=HEADS, j=TILES, i=4)[:, j],
+                    result[:].rearrange("p r (h j c i) -> p j h c r i", h=HEADS, j=TILES, i=4)[:, j],
+                )
+            else:
+                nc.scalar.copy(
+                    o_woven[:].rearrange("p (h j i) r -> p j h i r", h=HEADS, j=TILES)[:, j],
+                    mixed[:].rearrange("p r (h i) -> p h i r", h=HEADS),
+                )
+
+        quantise_queries(0)
+        score(0)
+        for j in range(1, TILES):
+            quantise_queries(j)
+        pick(0)
+        score(1)
+        pick(1)
+        gate(0)
+        place(0)
+        score(2)
+        pick(2)
+        gate(1)
+        place(1)
+        gate(2)
+        score(3)
+        weave_values(0, 0)
+        weave_values(0, 1)
+        weigh_and_turn(0)
+        quantise_values(0)
+        place(2)
+        weave_values(1, 0)
+        weave_values(1, 1)
+        weigh_and_turn(1)
+        quantise_weights(0)
+        quantise_weights(1)
+        pick(3)
+        quantise_values(1)
+        gate(3)
+        place(3)
+        mix_values(0)
+        weigh_and_turn(2)
+        mix_values(1)
+        weigh_and_turn(3)
+        quantise_weights(2)
+        quantise_weights(3)
+        mix_values(2)
+        mix_values(3)
+
+        nc.sync.dma_start(out_0.rearrange("(p r) q -> p r q", r=PACK), result[:])
+        o_codes = keep.tile([P, Q], U32, name="o_codes", align_bytes=64)
+        o_scales = keep.tile([P, Q], U8, name="o_scales", align_bytes=64)
+        nc.vector.quantize_mx(o_codes[:].bitcast(FP8X4), o_scales[:], o_woven[:].rearrange("p q r -> p (q r)"))
+        nc.sync.dma_start(out_1[0].rearrange("p q r -> p (q r)").bitcast(I32), o_codes[:].bitcast(I32))
+        for quad in range(4):
+            nc.scalar.dma_start(
+                out_2[0, 4 * quad : 4 * quad + 4, :].bitcast(I32),
+                o_scales[32 * quad : 32 * quad + 4, :].bitcast(I32),
+            )

@@ -24,27 +24,34 @@ K_PASS = P * PACK
 HEADS = 8
 GROUP = 16
 TILES = Q // P
+LAST = TILES - 1
 PASSES = T // K_PASS
 BANK = 512
+TURN_BANKS = (4, 6, 4, 6)
+MIX_BANKS = (0, 0, 0, 4)
 
 
 def tile_attend_mqa_ownlists_gated_kernel(tc, query, keys_words, keys_scales, th, fac, vals, offs, out_0, out_1, out_2):
     nc = tc.nc
     with ExitStack() as ctx:
         keep = ctx.enter_context(tc.tile_pool(name="keep", bufs=1))
-        ring = ctx.enter_context(tc.tile_pool(name="ring", bufs=2))
-        psum = ctx.enter_context(tc.psum_pool(name="psum", bufs=2))
+        psum = ctx.enter_context(tc.psum_pool(name="psum", bufs=1))
 
+        def bank(number, shape):
+            return psum.tile(shape, F32, name="bank%d" % number)
+
+        th_rows = keep.tile([P, P], F32, name="th_rows")
+        nc.gpsimd.memset(th_rows[:], 0.0)
         k_scales = keep.tile([P, T], U8, name="k_scales", align_bytes=64)
         nc.gpsimd.memset(k_scales[:].bitcast(I32), 0)
-        th_rows = keep.tile([P, P], F32, name="th_rows", tag="v_raw1")
-        nc.gpsimd.memset(th_rows[:], 0.0)
-        offsets = keep.tile([P, SLOTS // GROUP], U16, name="offsets")
-        nc.sync.dma_start(offsets[:], offs)
-        fac_col = keep.tile([P, T // P], F32, name="fac_col", tag="v_raw0")
+        fac_col = keep.tile([P, T // P], F32, name="fac_col")
         nc.sync.dma_start(fac_col[:], fac.rearrange("(p c) o -> p (c o)", p=P))
         q_raw = keep.tile([P, PACK, Q], F32, name="q_raw")
         nc.sync.dma_start(q_raw[:], query.rearrange("(p t) q -> p t q", t=PACK))
+        nc.sync.dma_start(
+            th_rows[0:TILES, :].rearrange("j (h r) -> j h r", r=GROUP),
+            th.rearrange("(h j r) o -> j h (r o)", h=HEADS, j=TILES),
+        )
         for quad in range(4):
             nc.sync.dma_start(
                 k_scales[32 * quad : 32 * quad + 4, :].bitcast(I32),
@@ -52,10 +59,11 @@ def tile_attend_mqa_ownlists_gated_kernel(tc, query, keys_words, keys_scales, th
             )
         k_words = keep.tile([P, 2 * T], U8, name="k_words", align_bytes=64)
         nc.sync.dma_start(k_words[:].bitcast(I32), keys_words[0].bitcast(I32))
-        nc.sync.dma_start(
-            th_rows[0:TILES, :].rearrange("j (h r) -> j h r", r=GROUP),
-            th.rearrange("(h j r) o -> j h (r o)", h=HEADS, j=TILES),
-        )
+        offsets = keep.tile([P, SLOTS // GROUP], U16, name="offsets")
+        nc.sync.dma_start(offsets[:], offs)
+        v_raw = [keep.tile([P, PACK * E], F32, name="v_raw%d" % g, tag="chain_a" if g == 1 else "v_raw", align_bytes=64) for g in range(PASSES)]
+        for g in range(PASSES):
+            nc.sync.dma_start(v_raw[g][:], vals[g * K_PASS : (g + 1) * K_PASS, :].rearrange("(p t) e -> p (t e)", t=PACK))
 
         ident = keep.tile([P, P], F32, name="ident")
         make_identity(nc, ident[:])
@@ -65,14 +73,13 @@ def tile_attend_mqa_ownlists_gated_kernel(tc, query, keys_words, keys_scales, th
         warm = keep.tile([P, 1], F32, name="warm")
         nc.scalar.activation(warm[:], cold[:], SIGMOID)
 
-        windows = [keep.tile([P, T], F32, name="placed%d" % j) for j in range(2)]
+        windows = [keep.tile([P, T], F32, name="window%d" % w) for w in range(2)]
         for window in windows:
             nc.vector.memset(window[:], 0.0)
-        placed = [windows[j % 2] for j in range(TILES)]
 
         fac_row = keep.tile([P, T], F32, name="fac_row")
         for half in range(2):
-            spread = psum.tile([P, PACK, P], F32, name="spread", tag="score%d" % half, bufs=1)
+            spread = bank(half, [P, PACK, P])
             for c in range(PACK):
                 col = PACK * half + c
                 nc.tensor.transpose(spread[:, c, :], fac_col[:, col : col + 1].to_broadcast([P, P]), ident[:])
@@ -82,38 +89,35 @@ def tile_attend_mqa_ownlists_gated_kernel(tc, query, keys_words, keys_scales, th
                 COPY,
                 scale=0.1,
             )
-        th_turned = psum.tile([P, P], F32, name="th_turned", tag="turn")
+        th_turned = bank(2, [P, P])
         nc.tensor.transpose(th_turned[:], th_rows[:], ident[:])
         neg_th = keep.tile([P, TILES], F32, name="neg_th")
         nc.scalar.activation(neg_th[:], th_turned[:, 0:TILES], COPY, scale=-1.0)
 
-        v_raw = [keep.tile([P, PACK, E], F32, name="v_raw%d" % g, tag="v_raw%d" % g) for g in range(PASSES)]
-        for g in range(PASSES):
-            nc.sync.dma_start(v_raw[g][:], vals[g * K_PASS : (g + 1) * K_PASS, :].rearrange("(p t) e -> p t e", t=PACK))
-
-        q_codes, q_scales = [], []
+        q_codes, q_scales, scores, gates, w_woven, w_codes, w_scales, v_codes, v_scales = {}, {}, {}, {}, {}, {}, {}, {}, {}
+        v_woven = [keep.tile([P, PACK * E], BF16, name="v_woven%d" % g, align_bytes=64) for g in range(PASSES)]
+        gates[0] = keep.tile([P, SLOTS], F32, name="gate0")
+        last_picked = keep.tile([P, SLOTS], F32, name="last_picked")
+        picked = [v_woven[0][:].bitcast(F32)[:, :SLOTS], v_woven[1][:].bitcast(F32)[:, :SLOTS], gates[0][:], last_picked[:]]
+        result = keep.tile([P, PACK, Q], F32, name="result")
+        o_woven = keep.tile([P, Q, PACK], BF16, name="o_woven", align_bytes=64)
 
         def quantise_queries(j):
             woven = keep.tile([P, P, PACK], BF16, name="q_woven%d" % j, align_bytes=64)
-            weave = nc.vector.tensor_copy if j < 2 else nc.scalar.copy
-            weave(
+            nc.vector.tensor_copy(
                 woven[:].rearrange("p (h c i) t -> p h c t i", h=HEADS, i=4),
                 q_raw[:].rearrange("p t (h j c i) -> p j h c t i", h=HEADS, j=TILES, i=4)[:, j],
             )
-            codes = keep.tile([P, P], U32, name="q_codes%d" % j, align_bytes=64)
-            scales = keep.tile([P, P], U8, name="q_scales%d" % j, align_bytes=64)
-            nc.vector.quantize_mx(codes[:].bitcast(FP8X4), scales[:], woven[:].rearrange("p q t -> p (q t)"))
-            q_codes.append(codes)
-            q_scales.append(scales)
-
-        scores, picked, gates = {}, {}, {}
+            q_codes[j] = keep.tile([P, P], U32, name="q_codes%d" % j, align_bytes=64)
+            q_scales[j] = keep.tile([P, P], U8, name="q_scales%d" % j, align_bytes=64)
+            nc.vector.quantize_mx(q_codes[j][:].bitcast(FP8X4), q_scales[j][:], woven[:].rearrange("p q t -> p (q t)"))
 
         def score(j):
-            scores[j] = keep.tile([P, T], F32, name="scores%d" % j, tag="scores%d" % j, align_bytes=64)
+            scores[j] = keep.tile([P, T], F32, name="scores%d" % j, align_bytes=64)
             for h in range(T // BANK):
-                bank = psum.tile([P, BANK], F32, name="bank", tag="score%d" % h, bufs=1)
+                sums = bank((2 * j + h) % 3, [P, BANK])
                 nc.tensor.matmul_mx(
-                    bank[:],
+                    sums[:],
                     lhsT=q_codes[j][:].bitcast(FP8X4),
                     lhsT_scale=q_scales[j][:],
                     rhs=k_words[:, 2 * BANK * h : 2 * BANK * (h + 1)].bitcast(FP4X4),
@@ -121,129 +125,120 @@ def tile_attend_mqa_ownlists_gated_kernel(tc, query, keys_words, keys_scales, th
                     start=True,
                     stop=True,
                 )
-                if j == 0 and h == 1:
-                    nc.vector.tensor_copy(scores[j][:, BANK * h : BANK * (h + 1)], bank[:])
-                else:
-                    nc.scalar.copy(scores[j][:, BANK * h : BANK * (h + 1)], bank[:])
+                empty = nc.vector.tensor_copy if (j, h) == (0, 1) else nc.scalar.copy
+                empty(scores[j][:, BANK * h : BANK * (h + 1)], sums[:])
 
         def pick(j):
-            tag = "w_woven1_1" if j == TILES - 1 else "picked%d" % j
-            picked[j] = keep.tile([P, SLOTS], F32, name="picked%d" % j, tag=tag, align_bytes=64)
-            nc.vector.tensor_copy(picked[j][:], scores[j][:].indirect(offsets[:]))
+            nc.vector.tensor_copy(picked[j], scores[j][:].indirect(offsets[:]))
 
         def gate(j):
-            gates[j] = keep.tile([P, SLOTS], F32, name="gate%d" % j)
-            nc.scalar.activation(gates[j][:], picked[j][:], SIGMOID, bias=neg_th[:, j : j + 1])
+            if j not in gates:
+                gates[j] = keep.tile([P, SLOTS], F32, name="gate%d" % j, tag="chain_a" if j == LAST else "gate%d" % j, align_bytes=64)
+            nc.scalar.activation(gates[j][:], picked[j], SIGMOID, bias=neg_th[:, j : j + 1])
 
         def place(j):
-            nc.vector.tensor_copy(placed[j][:].indirect(offsets[:]), gates[j][:])
-
-        w_woven = {}
+            nc.vector.tensor_copy(windows[j % 2][:].indirect(offsets[:]), gates[j][:])
 
         def weigh_and_turn(j):
+            engine = nc.vector if j == LAST else nc.gpsimd
+            weighted = keep.tile([P, T], BF16, name="weighted", tag=("weighted", "chain_a", "chain_b", "chain_b")[j], align_bytes=64)
             for g in range(PASSES):
                 cols = slice(g * K_PASS, (g + 1) * K_PASS)
-                weighted = ring.tile([P, K_PASS], BF16, name="weighted", tag="weighted%d" % g)
-                engine = nc.vector if j == TILES - 1 else nc.gpsimd
-                engine.tensor_tensor(weighted[:], placed[j][:, cols], fac_row[:, cols], MULT)
-                words = weighted[:].bitcast(F32)
-                turned = psum.tile([P, 2, P], F32, name="turned", tag="turn")
+                engine.tensor_tensor(weighted[:, cols], windows[j % 2][:, cols], fac_row[:, cols], MULT)
+            w_woven[j] = keep.tile([P, SLOTS], F32, name="w_woven", tag=("chain_a", "chain_b", "w_woven2", "w_woven3")[j], align_bytes=64)
+            for g in range(PASSES):
+                words = weighted[:, g * K_PASS : (g + 1) * K_PASS].bitcast(F32)
+                turned = bank(TURN_BANKS[j] + g, [P, 2, P])
                 for u in range(2):
                     nc.tensor.transpose(turned[:, u, :], words[:, u : 2 * P : 2], ident[:])
-                woven = keep.tile([P, P, PACK], BF16, name="w_woven", tag="w_woven%d_%d" % (j, g), align_bytes=64)
                 nc.scalar.copy(
-                    woven[:].rearrange("p q t -> p (q t)").bitcast(F32).rearrange("p (q u) -> p q u", u=2),
+                    w_woven[j][:, 2 * P * g : 2 * P * (g + 1)].rearrange("p (q u) -> p q u", u=2),
                     turned[:].rearrange("p u q -> p q u"),
                 )
-                w_woven[j, g] = woven
-
-        w_codes, w_scales = {}, {}
 
         def quantise_weights(j):
+            w_codes[j] = keep.tile([P, PASSES * P], U32, name="w_codes%d" % j, align_bytes=64)
+            w_scales[j] = keep.tile([P, PASSES * P], U8, name="w_scales%d" % j, align_bytes=64)
             for g in range(PASSES):
-                codes = keep.tile([P, P], U32, name="w_codes%d_%d" % (j, g), align_bytes=64)
-                scales = keep.tile([P, P], U8, name="w_scales%d_%d" % (j, g), align_bytes=64)
-                nc.vector.quantize_mx(codes[:].bitcast(FP8X4), scales[:], w_woven[j, g][:].rearrange("p q t -> p (q t)"))
-                w_codes[j, g] = codes
-                w_scales[j, g] = scales
-
-        v_woven = [keep.tile([P, PACK, P, PACK], BF16, name="v_woven%d" % g, tag="v_woven%d" % g, align_bytes=64) for g in range(PASSES)]
-        v_codes = {}
-        v_scales = [keep.tile([P, E], U8, name="v_scales%d" % g, align_bytes=64) for g in range(PASSES)]
+                cols = slice(g * P, (g + 1) * P)
+                nc.vector.quantize_mx(
+                    w_codes[j][:, cols].bitcast(FP8X4),
+                    w_scales[j][:, cols],
+                    w_woven[j][:, 2 * P * g : 2 * P * (g + 1)].bitcast(BF16),
+                )
 
         def weave_values(g, half):
             s = slice(half * P // 2, (half + 1) * P // 2)
             nc.scalar.copy(
-                v_woven[g][:].rearrange("p r s t -> p s t r")[:, s],
-                v_raw[g][:].rearrange("p t (s r) -> p s t r", r=PACK)[:, s],
+                v_woven[g][:].rearrange("p (r s t) -> p s t r", r=PACK, t=PACK)[:, s],
+                v_raw[g][:].rearrange("p (t s r) -> p s t r", t=PACK, r=PACK)[:, s],
             )
 
         def quantise_values(g):
-            tag = "scores%d" % (TILES - 1) if g == PASSES - 1 else "v_codes"
-            v_codes[g] = keep.tile([P, E], U32, name="v_codes%d" % g, tag=tag, align_bytes=64)
-            nc.vector.quantize_mx(v_codes[g][:].bitcast(FP8X4), v_scales[g][:], v_woven[g][:].rearrange("p r s t -> p (r s t)"))
-
-        result = keep.tile([P, PACK, Q], F32, name="result")
-        o_woven = keep.tile([P, Q, PACK], BF16, name="o_woven", align_bytes=64)
+            v_codes[g] = keep.tile([P, E], U32, name="v_codes%d" % g, align_bytes=64)
+            v_scales[g] = keep.tile([P, E], U8, name="v_scales%d" % g, align_bytes=64)
+            nc.vector.quantize_mx(v_codes[g][:].bitcast(FP8X4), v_scales[g][:], v_woven[g][:])
 
         def mix_values(j):
-            mixed = psum.tile([P, PACK, P], F32, name="mixed", tag="mixed")
-            for r in range(PACK):
-                for g in range(PASSES):
+            mixed = [bank(MIX_BANKS[j] + r, [P, P]) for r in range(PACK)]
+            for g in range(PASSES):
+                for r in range(PACK):
                     nc.tensor.matmul_mx(
-                        mixed[:, r, :],
+                        mixed[r][:],
                         lhsT=v_codes[g][:, r * P : (r + 1) * P].bitcast(FP8X4),
                         lhsT_scale=v_scales[g][:, r * P : (r + 1) * P],
-                        rhs=w_codes[j, g][:].bitcast(FP8X4),
-                        rhs_scale=w_scales[j, g][:],
+                        rhs=w_codes[j][:, g * P : (g + 1) * P].bitcast(FP8X4),
+                        rhs_scale=w_scales[j][:, g * P : (g + 1) * P],
                         start=(g == 0),
                         stop=(g == PASSES - 1),
                     )
-            nc.scalar.copy(
-                result[:].rearrange("p r (h j i) -> p j r h i", h=HEADS, j=TILES)[:, j],
-                mixed[:].rearrange("p r (h i) -> p r h i", h=HEADS),
-            )
-            if j >= TILES - 2:
-                nc.vector.tensor_copy(
-                    o_woven[:].rearrange("p (h j c i) r -> p j h c r i", h=HEADS, j=TILES, i=4)[:, j],
-                    result[:].rearrange("p r (h j c i) -> p j h c r i", h=HEADS, j=TILES, i=4)[:, j],
+            for r in range(PACK):
+                on_vector = j == LAST and r % 2 == 1
+                empty = nc.vector.tensor_copy if on_vector else nc.scalar.copy
+                empty(
+                    result[:, r, :].rearrange("p (h j i) -> p j h i", h=HEADS, j=TILES)[:, j],
+                    mixed[r][:].rearrange("p (h i) -> p h i", h=HEADS),
                 )
-            else:
-                nc.scalar.copy(
-                    o_woven[:].rearrange("p (h j i) r -> p j h i r", h=HEADS, j=TILES)[:, j],
-                    mixed[:].rearrange("p r (h i) -> p h i r", h=HEADS),
+            weave = nc.vector.tensor_copy if j >= LAST - 1 else nc.scalar.copy
+            parts = 2 if j == LAST else 1
+            for part in range(parts):
+                heads = slice(part * HEADS // parts, (part + 1) * HEADS // parts)
+                weave(
+                    o_woven[:].rearrange("p (h j c i) r -> p j h c r i", h=HEADS, j=TILES, i=4)[:, j, heads],
+                    result[:].rearrange("p r (h j c i) -> p j h c r i", h=HEADS, j=TILES, i=4)[:, j, heads],
                 )
 
         quantise_queries(0)
         score(0)
-        for j in range(1, TILES):
-            quantise_queries(j)
-        pick(0)
+        quantise_queries(1)
+        quantise_queries(2)
+        quantise_queries(3)
         score(1)
+        pick(0)
         pick(1)
         gate(0)
         place(0)
         score(2)
-        pick(2)
         gate(1)
+        pick(2)
         place(1)
-        gate(2)
-        score(3)
         weave_values(0, 0)
         weave_values(0, 1)
-        weigh_and_turn(0)
-        quantise_values(0)
-        place(2)
         weave_values(1, 0)
         weave_values(1, 1)
-        weigh_and_turn(1)
-        quantise_weights(0)
-        quantise_weights(1)
-        pick(3)
+        weigh_and_turn(0)
+        score(3)
+        gate(2)
+        quantise_values(0)
         quantise_values(1)
+        quantise_weights(0)
+        pick(3)
+        place(2)
+        weigh_and_turn(1)
+        mix_values(0)
+        quantise_weights(1)
         gate(3)
         place(3)
-        mix_values(0)
         weigh_and_turn(2)
         mix_values(1)
         weigh_and_turn(3)
@@ -252,11 +247,15 @@ def tile_attend_mqa_ownlists_gated_kernel(tc, query, keys_words, keys_scales, th
         mix_values(2)
         mix_values(3)
 
-        nc.sync.dma_start(out_0.rearrange("(p r) q -> p r q", r=PACK), result[:])
+        for half in range(2):
+            rows = slice(2 * half, 2 * half + 2)
+            nc.sync.dma_start(out_0.rearrange("(p r) q -> p r q", r=PACK)[:, rows], result[:, rows])
         o_codes = keep.tile([P, Q], U32, name="o_codes", align_bytes=64)
         o_scales = keep.tile([P, Q], U8, name="o_scales", align_bytes=64)
-        nc.vector.quantize_mx(o_codes[:].bitcast(FP8X4), o_scales[:], o_woven[:].rearrange("p q r -> p (q r)"))
-        nc.sync.dma_start(out_1[0].rearrange("p q r -> p (q r)").bitcast(I32), o_codes[:].bitcast(I32))
+        for half in range(2):
+            cols = slice(half * Q // 2, (half + 1) * Q // 2)
+            nc.vector.quantize_mx(o_codes[:, cols].bitcast(FP8X4), o_scales[:, cols], o_woven[:, cols].rearrange("p q r -> p (q r)"))
+            nc.sync.dma_start(out_1[0, :, cols].rearrange("p q r -> p (q r)").bitcast(I32), o_codes[:, cols].bitcast(I32))
         for quad in range(4):
             nc.scalar.dma_start(
                 out_2[0, 4 * quad : 4 * quad + 4, :].bitcast(I32),

@@ -1,7 +1,6 @@
 from contextlib import ExitStack
 
 import concourse.mybir as mybir
-from concourse.masks import make_identity
 
 D, T, Q, SLOTS, E = 512, 1024, 512, 512, 512
 FLOPS = 2 * D * Q * T + 2 * T * E * Q
@@ -15,10 +14,13 @@ U8 = mybir.dt.uint8
 FP8X4 = mybir.dt.float8_e4m3fn_x4
 FP4X4 = mybir.dt.float4_e2m1fn_x4
 MULT = mybir.AluOpType.mult
+ADD = mybir.AluOpType.add
+EQUAL = mybir.AluOpType.is_equal
 COPY = mybir.ActivationFunctionType.Copy
 SIGMOID = mybir.ActivationFunctionType.Sigmoid
 
 P = 128
+QUAD = 32
 PACK = 4
 K_PASS = P * PACK
 HEADS = 8
@@ -66,14 +68,20 @@ def tile_attend_mqa_ownlists_gated_kernel(tc, query, keys_words, keys_scales, th
             nc.sync.dma_start(v_raw[g][:], vals[g * K_PASS : (g + 1) * K_PASS, :].rearrange("(p t) e -> p (t e)", t=PACK))
 
         ident = keep.tile([P, P], F32, name="ident")
-        make_identity(nc, ident[:])
-
-        cold = keep.tile([P, 1], F32, name="cold")
-        nc.vector.memset(cold[:], 0.0)
+        nc.gpsimd.memset(ident[:], 0.0)
+        ones = keep.tile([P, QUAD], F32, name="ones")
+        nc.vector.memset(ones[:], 1.0)
         warm = keep.tile([P, 1], F32, name="warm")
-        nc.scalar.activation(warm[:], cold[:], SIGMOID)
+        nc.scalar.activation(warm[:], ones[:, 0:1], SIGMOID)
+        column_number = keep.tile([P, QUAD], F32, name="column_number", tag="window0", align_bytes=64)
+        nc.vector.tensor_tensor_scan(column_number[:], ones[:], ones[:], 0.0, MULT, ADD)
+        row_number = keep.tile([P, QUAD], F32, name="row_number", tag="window1", align_bytes=64)
+        nc.vector.transpose(row_number[:], column_number[:])
+        for quad in range(4):
+            rows = slice(QUAD * quad, QUAD * (quad + 1))
+            nc.vector.tensor_tensor(ident[rows, rows], column_number[rows, :], row_number[rows, :], EQUAL)
 
-        windows = [keep.tile([P, T], F32, name="window%d" % w) for w in range(2)]
+        windows = [keep.tile([P, T], F32, name="window%d" % w, tag="window%d" % w, align_bytes=64) for w in range(2)]
         for window in windows:
             nc.vector.memset(window[:], 0.0)
 

@@ -29,8 +29,8 @@ TILES = Q // P
 LAST = TILES - 1
 PASSES = T // K_PASS
 BANK = 512
+SCORE_BANKS = (0, 4, 0, 2)
 TURN_BANKS = (4, 6, 4, 6)
-MIX_BANKS = (0, 0, 0, 4)
 
 
 def tile_attend_mqa_ownlists_gated_kernel(tc, query, keys_words, keys_scales, th, fac, vals, offs, out_0, out_1, out_2):
@@ -42,12 +42,15 @@ def tile_attend_mqa_ownlists_gated_kernel(tc, query, keys_words, keys_scales, th
         def bank(number, shape):
             return psum.tile(shape, F32, name="bank%d" % number)
 
-        th_rows = keep.tile([P, P], F32, name="th_rows")
-        nc.gpsimd.memset(th_rows[:], 0.0)
         k_scales = keep.tile([P, T], U8, name="k_scales", align_bytes=64)
         nc.gpsimd.memset(k_scales[:].bitcast(I32), 0)
-        fac_col = keep.tile([P, T // P], F32, name="fac_col")
-        nc.sync.dma_start(fac_col[:], fac.rearrange("(p c) o -> p (c o)", p=P))
+        th_rows = keep.tile([P, P], F32, name="th_rows")
+        nc.gpsimd.memset(th_rows[:], 0.0)
+        ident = keep.tile([P, P], F32, name="ident")
+        nc.gpsimd.memset(ident[:], 0.0)
+
+        fac_col = keep.tile([P, PASSES, PACK], F32, name="fac_col")
+        nc.sync.dma_start(fac_col[:], fac.rearrange("(g p r) o -> p g (r o)", g=PASSES, r=PACK))
         q_raw = keep.tile([P, PACK, Q], F32, name="q_raw")
         nc.sync.dma_start(q_raw[:], query.rearrange("(p t) q -> p t q", t=PACK))
         nc.sync.dma_start(
@@ -56,19 +59,17 @@ def tile_attend_mqa_ownlists_gated_kernel(tc, query, keys_words, keys_scales, th
         )
         for quad in range(4):
             nc.sync.dma_start(
-                k_scales[32 * quad : 32 * quad + 4, :].bitcast(I32),
+                k_scales[QUAD * quad : QUAD * quad + 4, :].bitcast(I32),
                 keys_scales[0, 4 * quad : 4 * quad + 4, :].bitcast(I32),
             )
         k_words = keep.tile([P, 2 * T], U8, name="k_words", align_bytes=64)
         nc.sync.dma_start(k_words[:].bitcast(I32), keys_words[0].bitcast(I32))
         offsets = keep.tile([P, SLOTS // GROUP], U16, name="offsets")
         nc.sync.dma_start(offsets[:], offs)
-        v_raw = [keep.tile([P, PACK * E], F32, name="v_raw%d" % g, tag="chain_a" if g == 1 else "v_raw", align_bytes=64) for g in range(PASSES)]
+        v_raw = [keep.tile([P, PACK * E], F32, name="v_raw%d" % g, align_bytes=64) for g in range(PASSES)]
         for g in range(PASSES):
             nc.sync.dma_start(v_raw[g][:], vals[g * K_PASS : (g + 1) * K_PASS, :].rearrange("(p t) e -> p (t e)", t=PACK))
 
-        ident = keep.tile([P, P], F32, name="ident")
-        nc.gpsimd.memset(ident[:], 0.0)
         ones = keep.tile([P, QUAD], F32, name="ones")
         nc.vector.memset(ones[:], 1.0)
         warm = keep.tile([P, 1], F32, name="warm")
@@ -80,34 +81,29 @@ def tile_attend_mqa_ownlists_gated_kernel(tc, query, keys_words, keys_scales, th
         for quad in range(4):
             rows = slice(QUAD * quad, QUAD * (quad + 1))
             nc.vector.tensor_tensor(ident[rows, rows], column_number[rows, :], row_number[rows, :], EQUAL)
-
         windows = [keep.tile([P, T], F32, name="window%d" % w, tag="window%d" % w, align_bytes=64) for w in range(2)]
         for window in windows:
             nc.vector.memset(window[:], 0.0)
 
-        fac_row = keep.tile([P, T], F32, name="fac_row")
-        for half in range(2):
-            spread = bank(half, [P, PACK, P])
-            for c in range(PACK):
-                col = PACK * half + c
-                nc.tensor.transpose(spread[:, c, :], fac_col[:, col : col + 1].to_broadcast([P, P]), ident[:])
-            nc.scalar.activation(
-                fac_row[:].rearrange("m (n h c) -> m h n c", h=2, c=PACK)[:, half],
-                spread[:].rearrange("m c n -> m n c"),
-                COPY,
-                scale=0.1,
-            )
-        th_turned = bank(2, [P, P])
-        nc.tensor.transpose(th_turned[:], th_rows[:], ident[:])
-        neg_th = keep.tile([P, TILES], F32, name="neg_th")
-        nc.scalar.activation(neg_th[:], th_turned[:, 0:TILES], COPY, scale=-1.0)
+        def part(tile, number):
+            return tile[:, number * SLOTS : (number + 1) * SLOTS]
 
-        q_codes, q_scales, scores, gates, w_woven, w_codes, w_scales, v_codes, v_scales = {}, {}, {}, {}, {}, {}, {}, {}, {}
+        def own(name):
+            return keep.tile([P, SLOTS], F32, name=name, align_bytes=64)[:]
+
+        q_codes, q_scales, scores, w_codes, w_scales, v_codes, v_scales = {}, {}, {}, {}, {}, {}, {}
         v_woven = [keep.tile([P, PACK * E], BF16, name="v_woven%d" % g, align_bytes=64) for g in range(PASSES)]
-        gates[0] = keep.tile([P, SLOTS], F32, name="gate0")
-        last_picked = keep.tile([P, SLOTS], F32, name="last_picked")
-        picked = [v_woven[0][:].bitcast(F32)[:, :SLOTS], v_woven[1][:].bitcast(F32)[:, :SLOTS], gates[0][:], last_picked[:]]
+        middle = slice(SLOTS // 2, SLOTS // 2 + SLOTS)
+        picked = [own("picked0"), v_woven[0][:].bitcast(F32)[:, middle], own("picked2"), own("picked3")]
+        gates = [own("gates0"), own("gates1"), part(v_raw[1], 3), part(v_raw[1], 0)]
+        weighted = [part(v_raw[1], 1), part(v_raw[0], 1), own("weighted2"), own("weighted3")]
+        w_woven = [part(v_raw[0], 2), part(v_raw[1], 2), own("w_woven2"), own("w_woven3")]
+        fac_row = keep.tile([P, T], F32, name="fac_row")
+        fac_tenth = keep.tile([P, PASSES, PACK], F32, name="fac_tenth")
+        nc.scalar.activation(fac_tenth[:], fac_col[:], COPY, scale=0.1)
+        neg_th = keep.tile([P, TILES], F32, name="neg_th")
         result = keep.tile([P, PACK, Q], F32, name="result")
+        result_by_tile = result[:].rearrange("p r (h j i) -> p j r h i", h=HEADS, j=TILES)
         o_woven = keep.tile([P, Q, PACK], BF16, name="o_woven", align_bytes=64)
 
         def quantise_queries(j):
@@ -120,42 +116,55 @@ def tile_attend_mqa_ownlists_gated_kernel(tc, query, keys_words, keys_scales, th
             q_scales[j] = keep.tile([P, P], U8, name="q_scales%d" % j, align_bytes=64)
             nc.vector.quantize_mx(q_codes[j][:].bitcast(FP8X4), q_scales[j][:], woven[:].rearrange("p q t -> p (q t)"))
 
+        def turn_thresholds():
+            turned = bank(7, [P, P])
+            nc.tensor.transpose(turned[:], th_rows[:], ident[:])
+            nc.scalar.activation(neg_th[:], turned[:, 0:TILES], COPY, scale=-1.0)
+
+        def spread_factors():
+            for g in range(PASSES):
+                spread = bank(SCORE_BANKS[2] + g, [P, PACK, P])
+                for r in range(PACK):
+                    nc.tensor.transpose(spread[:, r, :], fac_col[:, g, r : r + 1].to_broadcast([P, P]), ident[:])
+                nc.scalar.activation(
+                    fac_row[:, g * K_PASS : (g + 1) * K_PASS].rearrange("m (n r) -> m n r", r=PACK),
+                    spread[:].rearrange("m r n -> m n r"),
+                    COPY,
+                    scale=0.1,
+                )
+
         def score(j):
             scores[j] = keep.tile([P, T], F32, name="scores%d" % j, align_bytes=64)
-            for h in range(T // BANK):
-                sums = bank((2 * j + h) % 3, [P, BANK])
+            width = BANK // 2 if j < 2 else BANK
+            for h in range(T // width):
+                sums = bank(SCORE_BANKS[j] + h, [P, width])
                 nc.tensor.matmul_mx(
                     sums[:],
                     lhsT=q_codes[j][:].bitcast(FP8X4),
                     lhsT_scale=q_scales[j][:],
-                    rhs=k_words[:, 2 * BANK * h : 2 * BANK * (h + 1)].bitcast(FP4X4),
-                    rhs_scale=k_scales[:, BANK * h : BANK * (h + 1)],
+                    rhs=k_words[:, 2 * width * h : 2 * width * (h + 1)].bitcast(FP4X4),
+                    rhs_scale=k_scales[:, width * h : width * (h + 1)],
                     start=True,
                     stop=True,
                 )
-                empty = nc.vector.tensor_copy if (j, h) == (0, 1) else nc.scalar.copy
-                empty(scores[j][:, BANK * h : BANK * (h + 1)], sums[:])
+                empty = nc.vector.tensor_copy if j == 0 and h % 2 == 1 else nc.scalar.copy
+                empty(scores[j][:, width * h : width * (h + 1)], sums[:])
 
         def pick(j):
             nc.vector.tensor_copy(picked[j], scores[j][:].indirect(offsets[:]))
 
         def gate(j):
-            if j not in gates:
-                gates[j] = keep.tile([P, SLOTS], F32, name="gate%d" % j, tag="chain_a" if j == LAST else "gate%d" % j, align_bytes=64)
-            nc.scalar.activation(gates[j][:], picked[j], SIGMOID, bias=neg_th[:, j : j + 1])
+            nc.scalar.activation(gates[j], picked[j], SIGMOID, bias=neg_th[:, j : j + 1])
 
         def place(j):
-            nc.vector.tensor_copy(windows[j % 2][:].indirect(offsets[:]), gates[j][:])
+            nc.vector.tensor_copy(windows[j % 2][:].indirect(offsets[:]), gates[j])
 
-        def weigh_and_turn(j):
-            engine = nc.vector if j == LAST else nc.gpsimd
-            weighted = keep.tile([P, T], BF16, name="weighted", tag=("weighted", "chain_a", "chain_b", "chain_b")[j], align_bytes=64)
-            for g in range(PASSES):
+        def weigh_and_turn(j, passes):
+            for g in range(passes.start, passes.stop):
                 cols = slice(g * K_PASS, (g + 1) * K_PASS)
-                engine.tensor_tensor(weighted[:, cols], windows[j % 2][:, cols], fac_row[:, cols], MULT)
-            w_woven[j] = keep.tile([P, SLOTS], F32, name="w_woven", tag=("chain_a", "chain_b", "w_woven2", "w_woven3")[j], align_bytes=64)
-            for g in range(PASSES):
-                words = weighted[:, g * K_PASS : (g + 1) * K_PASS].bitcast(F32)
+                nc.vector.tensor_tensor(weighted[j].bitcast(BF16)[:, cols], windows[j % 2][:, cols], fac_row[:, cols], MULT)
+            for g in range(passes.start, passes.stop):
+                words = weighted[j][:, 2 * P * g : 2 * P * (g + 1)]
                 turned = bank(TURN_BANKS[j] + g, [P, 2, P])
                 for u in range(2):
                     nc.tensor.transpose(turned[:, u, :], words[:, u : 2 * P : 2], ident[:])
@@ -164,108 +173,132 @@ def tile_attend_mqa_ownlists_gated_kernel(tc, query, keys_words, keys_scales, th
                     turned[:].rearrange("p u q -> p q u"),
                 )
 
-        def quantise_weights(j):
-            w_codes[j] = keep.tile([P, PASSES * P], U32, name="w_codes%d" % j, align_bytes=64)
-            w_scales[j] = keep.tile([P, PASSES * P], U8, name="w_scales%d" % j, align_bytes=64)
-            for g in range(PASSES):
-                cols = slice(g * P, (g + 1) * P)
-                nc.vector.quantize_mx(
-                    w_codes[j][:, cols].bitcast(FP8X4),
-                    w_scales[j][:, cols],
-                    w_woven[j][:, 2 * P * g : 2 * P * (g + 1)].bitcast(BF16),
+        def turn_and_weigh(j, passes):
+            for g in range(passes.start, passes.stop):
+                turned = bank(TURN_BANKS[j] + g, [P, PACK, P])
+                planes = weighted[j].bitcast(BF16)[:, g * K_PASS : (g + 1) * K_PASS].rearrange("p (r q) -> p r q", r=PACK)
+                for r in range(PACK):
+                    nc.tensor.transpose(turned[:, r, :], windows[j % 2][:, g * K_PASS + r : (g + 1) * K_PASS : PACK], ident[:])
+                for r in range(PACK):
+                    nc.scalar.activation(planes[:, r, :], turned[:, r, :], COPY, scale=fac_tenth[:, g, r : r + 1])
+                nc.scalar.copy(
+                    w_woven[j].bitcast(BF16)[:, g * K_PASS : (g + 1) * K_PASS].rearrange("p (c i r) -> p c r i", i=4, r=PACK),
+                    planes.rearrange("p r (c i) -> p c r i", i=4),
                 )
 
-        def weave_values(g, half):
-            s = slice(half * P // 2, (half + 1) * P // 2)
-            nc.scalar.copy(
-                v_woven[g][:].rearrange("p (r s t) -> p s t r", r=PACK, t=PACK)[:, s],
-                v_raw[g][:].rearrange("p (t s r) -> p s t r", t=PACK, r=PACK)[:, s],
+        def quantise_weights(j, passes):
+            if passes.start == 0:
+                w_codes[j] = keep.tile([P, PASSES * P], U32, name="w_codes%d" % j, align_bytes=64)
+                w_scales[j] = keep.tile([P, PASSES * P], U8, name="w_scales%d" % j, align_bytes=64)
+            cols = slice(passes.start * P, passes.stop * P)
+            nc.vector.quantize_mx(
+                w_codes[j][:, cols].bitcast(FP8X4),
+                w_scales[j][:, cols],
+                w_woven[j][:, 2 * cols.start : 2 * cols.stop].bitcast(BF16),
             )
+
+        def weave_values(g):
+            for half in range(2):
+                pair = slice(2 * half, 2 * half + 2)
+                nc.scalar.copy(
+                    v_woven[g][:].rearrange("p (r s t) -> p s t r", r=PACK, t=PACK)[:, :, :, pair],
+                    v_raw[g][:].rearrange("p (t s r) -> p s t r", t=PACK, r=PACK)[:, :, :, pair],
+                )
 
         def quantise_values(g):
             v_codes[g] = keep.tile([P, E], U32, name="v_codes%d" % g, align_bytes=64)
             v_scales[g] = keep.tile([P, E], U8, name="v_scales%d" % g, align_bytes=64)
             nc.vector.quantize_mx(v_codes[g][:].bitcast(FP8X4), v_scales[g][:], v_woven[g][:])
 
-        def mix_values(j):
-            mixed = [bank(MIX_BANKS[j] + r, [P, P]) for r in range(PACK)]
+        def mix(sums, j, r, g):
+            nc.tensor.matmul_mx(
+                sums,
+                lhsT=v_codes[g][:, r * P : (r + 1) * P].bitcast(FP8X4),
+                lhsT_scale=v_scales[g][:, r * P : (r + 1) * P],
+                rhs=w_codes[j][:, g * P : (g + 1) * P].bitcast(FP8X4),
+                rhs_scale=w_scales[j][:, g * P : (g + 1) * P],
+                start=(g == 0),
+                stop=(g == PASSES - 1),
+            )
+
+        def weave_result(weave, j, heads):
+            weave(
+                o_woven[:].rearrange("p (h j c i) r -> p j h c r i", h=HEADS, j=TILES, i=4)[:, j, heads],
+                result[:].rearrange("p r (h j c i) -> p j h c r i", h=HEADS, j=TILES, i=4)[:, j, heads],
+            )
+
+        def mix_early_tile(j):
+            mixed = bank(j, [P, PACK, P])
+            for r in range(PACK):
+                for g in range(PASSES):
+                    mix(mixed[:, r, :], j, r, g)
+            nc.scalar.copy(result_by_tile[:, j], mixed[:].rearrange("p r (h i) -> p r h i", h=HEADS))
+            weave_result(nc.scalar.copy, j, slice(0, HEADS))
+
+        def mix_late_tile(j):
+            mixed = [bank(PACK * (j - 2) + r, [P, P]) for r in range(PACK)]
             for g in range(PASSES):
                 for r in range(PACK):
-                    nc.tensor.matmul_mx(
-                        mixed[r][:],
-                        lhsT=v_codes[g][:, r * P : (r + 1) * P].bitcast(FP8X4),
-                        lhsT_scale=v_scales[g][:, r * P : (r + 1) * P],
-                        rhs=w_codes[j][:, g * P : (g + 1) * P].bitcast(FP8X4),
-                        rhs_scale=w_scales[j][:, g * P : (g + 1) * P],
-                        start=(g == 0),
-                        stop=(g == PASSES - 1),
-                    )
+                    mix(mixed[r][:], j, r, g)
             for r in range(PACK):
-                on_vector = j == LAST and r % 2 == 1
-                empty = nc.vector.tensor_copy if on_vector else nc.scalar.copy
-                empty(
-                    result[:, r, :].rearrange("p (h j i) -> p j h i", h=HEADS, j=TILES)[:, j],
-                    mixed[r][:].rearrange("p (h i) -> p h i", h=HEADS),
-                )
-            weave = nc.vector.tensor_copy if j >= LAST - 1 else nc.scalar.copy
+                empty = nc.vector.tensor_copy if j == LAST and r % 2 == 0 else nc.scalar.copy
+                empty(result_by_tile[:, j, r], mixed[r][:].rearrange("p (h i) -> p h i", h=HEADS))
             parts = 2 if j == LAST else 1
-            for part in range(parts):
-                heads = slice(part * HEADS // parts, (part + 1) * HEADS // parts)
-                weave(
-                    o_woven[:].rearrange("p (h j c i) r -> p j h c r i", h=HEADS, j=TILES, i=4)[:, j, heads],
-                    result[:].rearrange("p r (h j c i) -> p j h c r i", h=HEADS, j=TILES, i=4)[:, j, heads],
-                )
+            for number in range(parts):
+                weave_result(nc.vector.tensor_copy, j, slice(number * HEADS // parts, (number + 1) * HEADS // parts))
 
-        quantise_queries(0)
+        both, first, second = slice(0, 2), slice(0, 1), slice(1, 2)
+        spread_factors()
+        turn_thresholds()
+        for j in range(TILES):
+            quantise_queries(j)
         score(0)
-        quantise_queries(1)
-        quantise_queries(2)
-        quantise_queries(3)
         score(1)
         pick(0)
         pick(1)
         gate(0)
         place(0)
         score(2)
-        gate(1)
         pick(2)
+        gate(1)
         place(1)
-        weave_values(0, 0)
-        weave_values(0, 1)
-        weave_values(1, 0)
-        weave_values(1, 1)
-        weigh_and_turn(0)
         score(3)
+        pick(3)
+        weave_values(0)
+        weave_values(1)
         gate(2)
         quantise_values(0)
         quantise_values(1)
-        quantise_weights(0)
-        pick(3)
+        turn_and_weigh(0, both)
         place(2)
-        weigh_and_turn(1)
-        mix_values(0)
-        quantise_weights(1)
+        turn_and_weigh(1, both)
         gate(3)
+        quantise_weights(0, both)
+        weigh_and_turn(2, first)
+        turn_and_weigh(2, second)
+        quantise_weights(1, both)
         place(3)
-        weigh_and_turn(2)
-        mix_values(1)
-        weigh_and_turn(3)
-        quantise_weights(2)
-        quantise_weights(3)
-        mix_values(2)
-        mix_values(3)
+        mix_early_tile(0)
+        mix_early_tile(1)
+        quantise_weights(2, first)
+        weigh_and_turn(3, both)
+        quantise_weights(2, second)
+        quantise_weights(3, first)
+        quantise_weights(3, second)
+        mix_late_tile(2)
+        mix_late_tile(3)
 
-        for half in range(2):
-            rows = slice(2 * half, 2 * half + 2)
-            nc.sync.dma_start(out_0.rearrange("(p r) q -> p r q", r=PACK)[:, rows], result[:, rows])
+        out_rows = out_0.rearrange("(p r) q -> p r q", r=PACK)
+        for rows in (slice(0, 1), slice(1, 2), slice(2, PACK)):
+            nc.sync.dma_start(out_rows[:, rows], result[:, rows])
         o_codes = keep.tile([P, Q], U32, name="o_codes", align_bytes=64)
         o_scales = keep.tile([P, Q], U8, name="o_scales", align_bytes=64)
         for half in range(2):
             cols = slice(half * Q // 2, (half + 1) * Q // 2)
             nc.vector.quantize_mx(o_codes[:, cols].bitcast(FP8X4), o_scales[:, cols], o_woven[:, cols].rearrange("p q r -> p (q r)"))
-            nc.sync.dma_start(out_1[0, :, cols].rearrange("p q r -> p (q r)").bitcast(I32), o_codes[:, cols].bitcast(I32))
+        nc.sync.dma_start(out_1[0].rearrange("p q r -> p (q r)").bitcast(I32), o_codes[:].bitcast(I32))
         for quad in range(4):
             nc.scalar.dma_start(
                 out_2[0, 4 * quad : 4 * quad + 4, :].bitcast(I32),
-                o_scales[32 * quad : 32 * quad + 4, :].bitcast(I32),
+                o_scales[QUAD * quad : QUAD * quad + 4, :].bitcast(I32),
             )

@@ -29,8 +29,10 @@ TILES = Q // P
 LAST = TILES - 1
 PASSES = T // K_PASS
 BANK = 512
+QUERY_WEAVERS = (("vector",), ("vector",), ("vector",), ("scalar",))
 SCORE_BANKS = (0, 4, 0, 2)
 TURN_BANKS = (4, 6, 4, 6)
+EARLY_MIX_BANKS = (4, 0)
 
 
 def tile_attend_mqa_ownlists_gated_kernel(tc, query, keys_words, keys_scales, th, fac, vals, offs, out_0, out_1, out_2):
@@ -108,10 +110,14 @@ def tile_attend_mqa_ownlists_gated_kernel(tc, query, keys_words, keys_scales, th
 
         def quantise_queries(j):
             woven = keep.tile([P, P, PACK], BF16, name="q_woven%d" % j, align_bytes=64)
-            nc.vector.tensor_copy(
-                woven[:].rearrange("p (h c i) t -> p h c t i", h=HEADS, i=4),
-                q_raw[:].rearrange("p t (h j c i) -> p j h c t i", h=HEADS, j=TILES, i=4)[:, j],
-            )
+            shares = QUERY_WEAVERS[j]
+            for number, engine in enumerate(shares):
+                heads = slice(number * HEADS // len(shares), (number + 1) * HEADS // len(shares))
+                weave = nc.vector.tensor_copy if engine == "vector" else nc.scalar.copy
+                weave(
+                    woven[:].rearrange("p (h c i) t -> p h c t i", h=HEADS, i=4)[:, heads],
+                    q_raw[:].rearrange("p t (h j c i) -> p j h c t i", h=HEADS, j=TILES, i=4)[:, j, heads],
+                )
             q_codes[j] = keep.tile([P, P], U32, name="q_codes%d" % j, align_bytes=64)
             q_scales[j] = keep.tile([P, P], U8, name="q_scales%d" % j, align_bytes=64)
             nc.vector.quantize_mx(q_codes[j][:].bitcast(FP8X4), q_scales[j][:], woven[:].rearrange("p q t -> p (q t)"))
@@ -123,12 +129,12 @@ def tile_attend_mqa_ownlists_gated_kernel(tc, query, keys_words, keys_scales, th
 
         def spread_factors():
             for g in range(PASSES):
-                spread = bank(SCORE_BANKS[2] + g, [P, PACK, P])
+                spread = bank(SCORE_BANKS[1] + g, [P, PACK, P])
                 for r in range(PACK):
                     nc.tensor.transpose(spread[:, r, :], fac_col[:, g, r : r + 1].to_broadcast([P, P]), ident[:])
                 nc.scalar.activation(
-                    fac_row[:, g * K_PASS : (g + 1) * K_PASS].rearrange("m (n r) -> m n r", r=PACK),
-                    spread[:].rearrange("m r n -> m n r"),
+                    fac_row[:, g * K_PASS : (g + 1) * K_PASS].rearrange("m (u n e) -> m u n e", u=2, e=2),
+                    spread[:].rearrange("m (u e) n -> m u n e", u=2),
                     COPY,
                     scale=0.1,
                 )
@@ -159,28 +165,39 @@ def tile_attend_mqa_ownlists_gated_kernel(tc, query, keys_words, keys_scales, th
         def place(j):
             nc.vector.tensor_copy(windows[j % 2][:].indirect(offsets[:]), gates[j])
 
-        def weigh_and_turn(j, passes):
-            for g in range(passes.start, passes.stop):
+        def weigh_and_turn(j):
+            for g, parts in enumerate(([slice(0, 2)], [slice(0, 1), slice(1, 2)])):
                 cols = slice(g * K_PASS, (g + 1) * K_PASS)
-                nc.vector.tensor_tensor(weighted[j].bitcast(BF16)[:, cols], windows[j % 2][:, cols], fac_row[:, cols], MULT)
-            for g in range(passes.start, passes.stop):
+                for u in parts:
+                    nc.vector.tensor_tensor(
+                        weighted[j].bitcast(BF16)[:, cols].rearrange("q (u p e) -> q u p e", u=2, e=2)[:, u],
+                        windows[j % 2][:, cols].rearrange("q (p u e) -> q u p e", u=2, e=2)[:, u],
+                        fac_row[:, cols].rearrange("q (u p e) -> q u p e", u=2, e=2)[:, u],
+                        MULT,
+                    )
+            for g in range(PASSES):
                 words = weighted[j][:, 2 * P * g : 2 * P * (g + 1)]
                 turned = bank(TURN_BANKS[j] + g, [P, 2, P])
                 for u in range(2):
-                    nc.tensor.transpose(turned[:, u, :], words[:, u : 2 * P : 2], ident[:])
+                    nc.tensor.transpose(turned[:, u, :], words[:, u * P : (u + 1) * P], ident[:])
                 nc.scalar.copy(
                     w_woven[j][:, 2 * P * g : 2 * P * (g + 1)].rearrange("p (q u) -> p q u", u=2),
                     turned[:].rearrange("p u q -> p q u"),
                 )
 
-        def turn_and_weigh(j, passes):
-            for g in range(passes.start, passes.stop):
-                turned = bank(TURN_BANKS[j] + g, [P, PACK, P])
+        def turn_and_weigh(j):
+            for g in range(PASSES):
+                if (j, g) == (2, 0):
+                    halves = [bank(number, [P, 2, P]) for number in EARLY_MIX_BANKS]
+                    turned = [halves[r // 2][:, r % 2, :] for r in range(PACK)]
+                else:
+                    whole = bank(TURN_BANKS[j] + g, [P, PACK, P])
+                    turned = [whole[:, r, :] for r in range(PACK)]
                 planes = weighted[j].bitcast(BF16)[:, g * K_PASS : (g + 1) * K_PASS].rearrange("p (r q) -> p r q", r=PACK)
                 for r in range(PACK):
-                    nc.tensor.transpose(turned[:, r, :], windows[j % 2][:, g * K_PASS + r : (g + 1) * K_PASS : PACK], ident[:])
+                    nc.tensor.transpose(turned[r], windows[j % 2][:, g * K_PASS + r : (g + 1) * K_PASS : PACK], ident[:])
                 for r in range(PACK):
-                    nc.scalar.activation(planes[:, r, :], turned[:, r, :], COPY, scale=fac_tenth[:, g, r : r + 1])
+                    nc.scalar.activation(planes[:, r, :], turned[r], COPY, scale=fac_tenth[:, g, r : r + 1])
                 nc.scalar.copy(
                     w_woven[j].bitcast(BF16)[:, g * K_PASS : (g + 1) * K_PASS].rearrange("p (c i r) -> p c r i", i=4, r=PACK),
                     planes.rearrange("p r (c i) -> p c r i", i=4),
@@ -221,19 +238,19 @@ def tile_attend_mqa_ownlists_gated_kernel(tc, query, keys_words, keys_scales, th
                 stop=(g == PASSES - 1),
             )
 
-        def weave_result(weave, j, heads):
-            weave(
+        def weave_result(j, heads):
+            nc.vector.tensor_copy(
                 o_woven[:].rearrange("p (h j c i) r -> p j h c r i", h=HEADS, j=TILES, i=4)[:, j, heads],
                 result[:].rearrange("p r (h j c i) -> p j h c r i", h=HEADS, j=TILES, i=4)[:, j, heads],
             )
 
         def mix_early_tile(j):
-            mixed = bank(j, [P, PACK, P])
+            mixed = bank(EARLY_MIX_BANKS[j], [P, PACK, P])
             for r in range(PACK):
                 for g in range(PASSES):
                     mix(mixed[:, r, :], j, r, g)
             nc.scalar.copy(result_by_tile[:, j], mixed[:].rearrange("p r (h i) -> p r h i", h=HEADS))
-            weave_result(nc.scalar.copy, j, slice(0, HEADS))
+            weave_result(j, slice(0, HEADS))
 
         def mix_late_tile(j):
             mixed = [bank(PACK * (j - 2) + r, [P, P]) for r in range(PACK)]
@@ -245,7 +262,7 @@ def tile_attend_mqa_ownlists_gated_kernel(tc, query, keys_words, keys_scales, th
                 empty(result_by_tile[:, j, r], mixed[r][:].rearrange("p (h i) -> p h i", h=HEADS))
             parts = 2 if j == LAST else 1
             for number in range(parts):
-                weave_result(nc.vector.tensor_copy, j, slice(number * HEADS // parts, (number + 1) * HEADS // parts))
+                weave_result(j, slice(number * HEADS // parts, (number + 1) * HEADS // parts))
 
         both, first, second = slice(0, 2), slice(0, 1), slice(1, 2)
         spread_factors()
@@ -269,20 +286,18 @@ def tile_attend_mqa_ownlists_gated_kernel(tc, query, keys_words, keys_scales, th
         gate(2)
         quantise_values(0)
         quantise_values(1)
-        turn_and_weigh(0, both)
+        turn_and_weigh(0)
         place(2)
-        turn_and_weigh(1, both)
+        turn_and_weigh(1)
         gate(3)
         quantise_weights(0, both)
-        weigh_and_turn(2, first)
-        turn_and_weigh(2, second)
+        turn_and_weigh(2)
         quantise_weights(1, both)
         place(3)
         mix_early_tile(0)
         mix_early_tile(1)
-        quantise_weights(2, first)
-        weigh_and_turn(3, both)
-        quantise_weights(2, second)
+        weigh_and_turn(3)
+        quantise_weights(2, both)
         quantise_weights(3, first)
         quantise_weights(3, second)
         mix_late_tile(2)

@@ -29,10 +29,11 @@ TILES = Q // P
 LAST = TILES - 1
 PASSES = T // K_PASS
 BANK = 512
-QUERY_WEAVERS = (("vector",), ("vector",), ("vector",), ("scalar",))
+QUERY_WEAVERS = (("vector", "vector"), ("vector",), ("vector",), ("scalar",))
 SCORE_BANKS = (0, 4, 0, 2)
 TURN_BANKS = (4, 6, 4, 6)
-EARLY_MIX_BANKS = (4, 0)
+MIX_BANKS = (4, 0, 1)
+LAST_MIX_BANKS = (2, 3, 4, 5)
 
 
 def tile_attend_mqa_ownlists_gated_kernel(tc, query, keys_words, keys_scales, th, fac, vals, offs, out_0, out_1, out_2):
@@ -98,7 +99,8 @@ def tile_attend_mqa_ownlists_gated_kernel(tc, query, keys_words, keys_scales, th
         middle = slice(SLOTS // 2, SLOTS // 2 + SLOTS)
         picked = [own("picked0"), v_woven[0][:].bitcast(F32)[:, middle], own("picked2"), own("picked3")]
         gates = [own("gates0"), own("gates1"), part(v_raw[1], 3), part(v_raw[1], 0)]
-        weighted = [part(v_raw[1], 1), part(v_raw[0], 1), own("weighted2"), own("weighted3")]
+        late_weighted = own("late_weighted")
+        weighted = [part(v_raw[1], 1), part(v_raw[0], 1), late_weighted, late_weighted]
         w_woven = [part(v_raw[0], 2), part(v_raw[1], 2), own("w_woven2"), own("w_woven3")]
         fac_row = keep.tile([P, T], F32, name="fac_row")
         fac_tenth = keep.tile([P, PASSES, PACK], F32, name="fac_tenth")
@@ -120,7 +122,9 @@ def tile_attend_mqa_ownlists_gated_kernel(tc, query, keys_words, keys_scales, th
                 )
             q_codes[j] = keep.tile([P, P], U32, name="q_codes%d" % j, align_bytes=64)
             q_scales[j] = keep.tile([P, P], U8, name="q_scales%d" % j, align_bytes=64)
-            nc.vector.quantize_mx(q_codes[j][:].bitcast(FP8X4), q_scales[j][:], woven[:].rearrange("p q t -> p (q t)"))
+            for number in range(len(shares)):
+                cols = slice(number * P // len(shares), (number + 1) * P // len(shares))
+                nc.vector.quantize_mx(q_codes[j][:, cols].bitcast(FP8X4), q_scales[j][:, cols], woven[:, cols].rearrange("p q t -> p (q t)"))
 
         def turn_thresholds():
             turned = bank(7, [P, P])
@@ -153,7 +157,7 @@ def tile_attend_mqa_ownlists_gated_kernel(tc, query, keys_words, keys_scales, th
                     start=True,
                     stop=True,
                 )
-                empty = nc.vector.tensor_copy if j == 0 and h % 2 == 1 else nc.scalar.copy
+                empty = nc.vector.tensor_copy if j == 0 and h % 2 == 0 else nc.scalar.copy
                 empty(scores[j][:, width * h : width * (h + 1)], sums[:])
 
         def pick(j):
@@ -188,7 +192,7 @@ def tile_attend_mqa_ownlists_gated_kernel(tc, query, keys_words, keys_scales, th
         def turn_and_weigh(j):
             for g in range(PASSES):
                 if (j, g) == (2, 0):
-                    halves = [bank(number, [P, 2, P]) for number in EARLY_MIX_BANKS]
+                    halves = [bank(number, [P, 2, P]) for number in MIX_BANKS[:2]]
                     turned = [halves[r // 2][:, r % 2, :] for r in range(PACK)]
                 else:
                     whole = bank(TURN_BANKS[j] + g, [P, PACK, P])
@@ -238,31 +242,46 @@ def tile_attend_mqa_ownlists_gated_kernel(tc, query, keys_words, keys_scales, th
                 stop=(g == PASSES - 1),
             )
 
-        def weave_result(j, heads):
-            nc.vector.tensor_copy(
-                o_woven[:].rearrange("p (h j c i) r -> p j h c r i", h=HEADS, j=TILES, i=4)[:, j, heads],
-                result[:].rearrange("p r (h j c i) -> p j h c r i", h=HEADS, j=TILES, i=4)[:, j, heads],
+        def weave_result(weave, tiles, heads):
+            chunks = slice(PACK * tiles.start, PACK * tiles.stop)
+            weave(
+                o_woven[:].rearrange("p (h c i) r -> p h c r i", h=HEADS, i=4)[:, heads, chunks],
+                result[:].rearrange("p r (h c i) -> p h c r i", h=HEADS, i=4)[:, heads, chunks],
             )
 
-        def mix_early_tile(j):
-            mixed = bank(EARLY_MIX_BANKS[j], [P, PACK, P])
+        def mix_tile(j):
+            mixed = bank(MIX_BANKS[j], [P, PACK, P])
             for r in range(PACK):
                 for g in range(PASSES):
                     mix(mixed[:, r, :], j, r, g)
-            nc.scalar.copy(result_by_tile[:, j], mixed[:].rearrange("p r (h i) -> p r h i", h=HEADS))
-            weave_result(j, slice(0, HEADS))
+            return mixed
 
-        def mix_late_tile(j):
-            mixed = [bank(PACK * (j - 2) + r, [P, P]) for r in range(PACK)]
+        def keep_tile(j, mixed):
+            nc.scalar.copy(result_by_tile[:, j], mixed[:].rearrange("p r (h i) -> p r h i", h=HEADS))
+            if j < 2:
+                weave_result(nc.vector.tensor_copy, slice(j, j + 1), slice(0, HEADS))
+
+        def mix_last_tile():
+            mixed = [bank(LAST_MIX_BANKS[r], [P, P]) for r in range(PACK)]
             for g in range(PASSES):
                 for r in range(PACK):
-                    mix(mixed[r][:], j, r, g)
+                    mix(mixed[r][:], LAST, r, g)
             for r in range(PACK):
-                empty = nc.vector.tensor_copy if j == LAST and r % 2 == 0 else nc.scalar.copy
-                empty(result_by_tile[:, j, r], mixed[r][:].rearrange("p (h i) -> p h i", h=HEADS))
-            parts = 2 if j == LAST else 1
-            for number in range(parts):
-                weave_result(j, slice(number * HEADS // parts, (number + 1) * HEADS // parts))
+                empty = nc.vector.tensor_copy if r % 2 == 0 else nc.scalar.copy
+                empty(result_by_tile[:, LAST, r], mixed[r][:].rearrange("p (h i) -> p h i", h=HEADS))
+
+        def warm_tensor_engine():
+            idle = bank(MIX_BANKS[1], [P, BANK])
+            for h in range(T // BANK):
+                nc.tensor.matmul_mx(
+                    idle[:],
+                    lhsT=q_codes[LAST][:].bitcast(FP8X4),
+                    lhsT_scale=q_scales[LAST][:],
+                    rhs=k_words[:, 2 * BANK * h : 2 * BANK * (h + 1)].bitcast(FP4X4),
+                    rhs_scale=k_scales[:, BANK * h : BANK * (h + 1)],
+                    start=True,
+                    stop=True,
+                )
 
         both, first, second = slice(0, 2), slice(0, 1), slice(1, 2)
         spread_factors()
@@ -294,14 +313,18 @@ def tile_attend_mqa_ownlists_gated_kernel(tc, query, keys_words, keys_scales, th
         turn_and_weigh(2)
         quantise_weights(1, both)
         place(3)
-        mix_early_tile(0)
-        mix_early_tile(1)
+        keep_tile(0, mix_tile(0))
+        warm_tensor_engine()
+        mixed = mix_tile(1)
         weigh_and_turn(3)
         quantise_weights(2, both)
         quantise_weights(3, first)
         quantise_weights(3, second)
-        mix_late_tile(2)
-        mix_late_tile(3)
+        keep_tile(1, mixed)
+        keep_tile(2, mix_tile(2))
+        mix_last_tile()
+        weave_result(nc.vector.tensor_copy, slice(2, TILES), slice(0, HEADS // 2))
+        weave_result(nc.scalar.copy, slice(2, TILES), slice(HEADS // 2, HEADS))
 
         out_rows = out_0.rearrange("(p r) q -> p r q", r=PACK)
         for rows in (slice(0, 1), slice(1, 2), slice(2, PACK)):

@@ -102,7 +102,7 @@ def tile_attend_mqa_ownlists_gated_kernel(tc, query, keys_words, keys_scales, th
         late_weighted = own("late_weighted")
         weighted = [part(v_raw[1], 1), part(v_raw[0], 1), late_weighted, late_weighted]
         w_woven = [part(v_raw[0], 2), part(v_raw[1], 2), own("w_woven2"), own("w_woven3")]
-        fac_row = keep.tile([P, T], F32, name="fac_row")
+        fac_row = keep.tile([P, P, 2], F32, name="fac_row")
         fac_tenth = keep.tile([P, PASSES, PACK], F32, name="fac_tenth")
         nc.scalar.activation(fac_tenth[:], fac_col[:], COPY, scale=0.1)
         neg_th = keep.tile([P, TILES], F32, name="neg_th")
@@ -131,17 +131,11 @@ def tile_attend_mqa_ownlists_gated_kernel(tc, query, keys_words, keys_scales, th
             nc.tensor.transpose(turned[:], th_rows[:], ident[:])
             nc.scalar.activation(neg_th[:], turned[:, 0:TILES], COPY, scale=-1.0)
 
-        def spread_factors():
-            for g in range(PASSES):
-                spread = bank(SCORE_BANKS[1] + g, [P, PACK, P])
-                for r in range(PACK):
-                    nc.tensor.transpose(spread[:, r, :], fac_col[:, g, r : r + 1].to_broadcast([P, P]), ident[:])
-                nc.scalar.activation(
-                    fac_row[:, g * K_PASS : (g + 1) * K_PASS].rearrange("m (u n e) -> m u n e", u=2, e=2),
-                    spread[:].rearrange("m (u e) n -> m u n e", u=2),
-                    COPY,
-                    scale=0.1,
-                )
+        def spread_factors(number, g, places):
+            spread = bank(number, [P, PACK, P])
+            for r in range(places.start, places.stop):
+                nc.tensor.transpose(spread[:, r, :], fac_tenth[:, g, r : r + 1].to_broadcast([P, P]), ident[:])
+            return spread[:].rearrange("m (u e) n -> m u n e", u=2)
 
         def score(j):
             scores[j] = keep.tile([P, T], F32, name="scores%d" % j, align_bytes=64)
@@ -170,20 +164,17 @@ def tile_attend_mqa_ownlists_gated_kernel(tc, query, keys_words, keys_scales, th
             nc.vector.tensor_copy(windows[j % 2][:].indirect(offsets[:]), gates[j])
 
         def weigh_and_turn(j):
-            for g, parts in enumerate(([slice(0, 2)], [slice(0, 1), slice(1, 2)])):
-                cols = slice(g * K_PASS, (g + 1) * K_PASS)
-                for u in parts:
-                    nc.vector.tensor_tensor(
-                        weighted[j].bitcast(BF16)[:, cols].rearrange("q (u p e) -> q u p e", u=2, e=2)[:, u],
-                        windows[j % 2][:, cols].rearrange("q (p u e) -> q u p e", u=2, e=2)[:, u],
-                        fac_row[:, cols].rearrange("q (u p e) -> q u p e", u=2, e=2)[:, u],
-                        MULT,
-                    )
+            ordered = weighted[j].bitcast(BF16).rearrange("q (g u p e) -> q g u p e", g=PASSES, u=2, e=2)
+            placed = windows[j % 2][:].rearrange("q (g p u e) -> q g u p e", g=PASSES, u=2, e=2)
+            nc.vector.tensor_tensor(ordered[:, 0], placed[:, 0], spread[0], MULT)
+            nc.vector.tensor_tensor(ordered[:, 1, 0], placed[:, 1, 0], spread[1][:, 0], MULT)
+            last_quarter = keep.tile([P, P], F32, name="last_quarter", align_bytes=64)
+            nc.gpsimd.tensor_tensor(last_quarter[:].bitcast(BF16).rearrange("q (p e) -> q p e", e=2), placed[:, 1, 1], fac_row[:], MULT)
             for g in range(PASSES):
                 words = weighted[j][:, 2 * P * g : 2 * P * (g + 1)]
                 turned = bank(TURN_BANKS[j] + g, [P, 2, P])
                 for u in range(2):
-                    nc.tensor.transpose(turned[:, u, :], words[:, u * P : (u + 1) * P], ident[:])
+                    nc.tensor.transpose(turned[:, u, :], last_quarter[:] if (g, u) == (1, 1) else words[:, u * P : (u + 1) * P], ident[:])
                 nc.scalar.copy(
                     w_woven[j][:, 2 * P * g : 2 * P * (g + 1)].rearrange("p (q u) -> p q u", u=2),
                     turned[:].rearrange("p u q -> p q u"),
@@ -284,7 +275,7 @@ def tile_attend_mqa_ownlists_gated_kernel(tc, query, keys_words, keys_scales, th
                 )
 
         both, first, second = slice(0, 2), slice(0, 1), slice(1, 2)
-        spread_factors()
+        nc.scalar.copy(fac_row[:], spread_factors(SCORE_BANKS[1], 1, slice(2, PACK))[:, 1])
         turn_thresholds()
         for j in range(TILES):
             quantise_queries(j)
@@ -300,6 +291,7 @@ def tile_attend_mqa_ownlists_gated_kernel(tc, query, keys_words, keys_scales, th
         place(1)
         score(3)
         pick(3)
+        spread = [spread_factors(SCORE_BANKS[3], 0, slice(0, PACK)), spread_factors(SCORE_BANKS[3] + 1, 1, slice(0, 2))]
         weave_values(0)
         weave_values(1)
         gate(2)

@@ -52,8 +52,6 @@ def tile_attend_mqa_ownlists_gated_kernel(tc, query, keys_words, keys_scales, th
         ident = keep.tile([P, P], F32, name="ident")
         nc.gpsimd.memset(ident[:], 0.0)
 
-        fac_col = keep.tile([P, PASSES, PACK], F32, name="fac_col")
-        nc.sync.dma_start(fac_col[:], fac.rearrange("(g p r) o -> p g (r o)", g=PASSES, r=PACK))
         q_raw = keep.tile([P, PACK, Q], F32, name="q_raw")
         nc.sync.dma_start(q_raw[:], query.rearrange("(p t) q -> p t q", t=PACK))
         nc.sync.dma_start(
@@ -69,6 +67,8 @@ def tile_attend_mqa_ownlists_gated_kernel(tc, query, keys_words, keys_scales, th
         nc.sync.dma_start(k_words[:].bitcast(I32), keys_words[0].bitcast(I32))
         offsets = keep.tile([P, SLOTS // GROUP], U16, name="offsets")
         nc.sync.dma_start(offsets[:], offs)
+        fac_col = keep.tile([P, PASSES, PACK], F32, name="fac_col")
+        nc.sync.dma_start(fac_col[:], fac.rearrange("(g p r) o -> p g (r o)", g=PASSES, r=PACK))
         v_raw = [keep.tile([P, PACK * E], F32, name="v_raw%d" % g, align_bytes=64) for g in range(PASSES)]
         for g in range(PASSES):
             nc.sync.dma_start(v_raw[g][:], vals[g * K_PASS : (g + 1) * K_PASS, :].rearrange("(p t) e -> p (t e)", t=PACK))
@@ -102,9 +102,8 @@ def tile_attend_mqa_ownlists_gated_kernel(tc, query, keys_words, keys_scales, th
         late_weighted = own("late_weighted")
         weighted = [part(v_raw[1], 1), part(v_raw[0], 1), late_weighted, late_weighted]
         w_woven = [part(v_raw[0], 2), part(v_raw[1], 2), own("w_woven2"), own("w_woven3")]
-        fac_row = keep.tile([P, P, 2], F32, name="fac_row")
+        fac_row = part(v_raw[0], 3)[:, : 2 * P].rearrange("m (n e) -> m n e", e=2)
         fac_tenth = keep.tile([P, PASSES, PACK], F32, name="fac_tenth")
-        nc.scalar.activation(fac_tenth[:], fac_col[:], COPY, scale=0.1)
         neg_th = keep.tile([P, TILES], F32, name="neg_th")
         result = keep.tile([P, PACK, Q], F32, name="result")
         result_by_tile = result[:].rearrange("p r (h j i) -> p j r h i", h=HEADS, j=TILES)
@@ -131,9 +130,9 @@ def tile_attend_mqa_ownlists_gated_kernel(tc, query, keys_words, keys_scales, th
             nc.tensor.transpose(turned[:], th_rows[:], ident[:])
             nc.scalar.activation(neg_th[:], turned[:, 0:TILES], COPY, scale=-1.0)
 
-        def spread_factors(number, g, places):
-            spread = bank(number, [P, PACK, P])
-            for r in range(places.start, places.stop):
+        def spread_factors(g):
+            spread = bank(SCORE_BANKS[LAST] + g, [P, PACK, P])
+            for r in range(PACK):
                 nc.tensor.transpose(spread[:, r, :], fac_tenth[:, g, r : r + 1].to_broadcast([P, P]), ident[:])
             return spread[:].rearrange("m (u e) n -> m u n e", u=2)
 
@@ -169,7 +168,7 @@ def tile_attend_mqa_ownlists_gated_kernel(tc, query, keys_words, keys_scales, th
             nc.vector.tensor_tensor(ordered[:, 0], placed[:, 0], spread[0], MULT)
             nc.vector.tensor_tensor(ordered[:, 1, 0], placed[:, 1, 0], spread[1][:, 0], MULT)
             last_quarter = keep.tile([P, P], F32, name="last_quarter", align_bytes=64)
-            nc.gpsimd.tensor_tensor(last_quarter[:].bitcast(BF16).rearrange("q (p e) -> q p e", e=2), placed[:, 1, 1], fac_row[:], MULT)
+            nc.gpsimd.tensor_tensor(last_quarter[:].bitcast(BF16).rearrange("q (p e) -> q p e", e=2), placed[:, 1, 1], fac_row, MULT)
             for g in range(PASSES):
                 words = weighted[j][:, 2 * P * g : 2 * P * (g + 1)]
                 turned = bank(TURN_BANKS[j] + g, [P, 2, P])
@@ -275,7 +274,6 @@ def tile_attend_mqa_ownlists_gated_kernel(tc, query, keys_words, keys_scales, th
                 )
 
         both, first, second = slice(0, 2), slice(0, 1), slice(1, 2)
-        nc.scalar.copy(fac_row[:], spread_factors(SCORE_BANKS[1], 1, slice(2, PACK))[:, 1])
         turn_thresholds()
         for j in range(TILES):
             quantise_queries(j)
@@ -291,13 +289,15 @@ def tile_attend_mqa_ownlists_gated_kernel(tc, query, keys_words, keys_scales, th
         place(1)
         score(3)
         pick(3)
-        spread = [spread_factors(SCORE_BANKS[3], 0, slice(0, PACK)), spread_factors(SCORE_BANKS[3] + 1, 1, slice(0, 2))]
+        nc.gpsimd.tensor_scalar(fac_tenth[:], fac_col[:], 0.1, 0.0, MULT, ADD)
+        spread = [spread_factors(g) for g in range(PASSES)]
         weave_values(0)
         weave_values(1)
         gate(2)
         quantise_values(0)
         quantise_values(1)
         turn_and_weigh(0)
+        nc.scalar.copy(fac_row, spread[1][:, 1])
         place(2)
         turn_and_weigh(1)
         gate(3)

@@ -326,9 +326,9 @@ def tile_attend_mqa_ownlists_gated_kernel(tc, query, keys_words, keys_scales, th
         for half in range(2):
             cols = slice(half * Q // 2, (half + 1) * Q // 2)
             nc.vector.quantize_mx(o_codes[:, cols].bitcast(FP8X4), o_scales[:, cols], o_woven[:, cols].rearrange("p q r -> p (q r)"))
-        nc.sync.dma_start(out_1[0].rearrange("p q r -> p (q r)").bitcast(I32), o_codes[:].bitcast(I32))
         for quad in range(4):
-            nc.scalar.dma_start(
+            nc.sync.dma_start(
                 out_2[0, 4 * quad : 4 * quad + 4, :].bitcast(I32),
                 o_scales[QUAD * quad : QUAD * quad + 4, :].bitcast(I32),
             )
+        nc.sync.dma_start(out_1[0].rearrange("p q r -> p (q r)").bitcast(I32), o_codes[:].bitcast(I32))

@@ -29,11 +29,11 @@ TILES = Q // P
 LAST = TILES - 1
 PASSES = T // K_PASS
 BANK = 512
-QUERY_WEAVERS = (("vector", "vector"), ("vector",), ("vector",), ("scalar",))
-SCORE_BANKS = (0, 4, 0, 2)
-TURN_BANKS = (4, 6, 4, 6)
-MIX_BANKS = (4, 0, 1)
-LAST_MIX_BANKS = (2, 3, 4, 5)
+SCORE_BANKS = (0, 4, 6, 0)
+TURN_BANKS = (2, 4, 6, 2)
+FACTOR_BANKS = 4
+MIX_BANKS = (6, 7, 0)
+LAST_MIX_BANKS = (1, 4, 5, 2)
 
 
 def tile_attend_mqa_ownlists_gated_kernel(tc, query, keys_words, keys_scales, th, fac, vals, offs, out_0, out_1, out_2):
@@ -88,61 +88,62 @@ def tile_attend_mqa_ownlists_gated_kernel(tc, query, keys_words, keys_scales, th
         for window in windows:
             nc.vector.memset(window[:], 0.0)
 
-        def part(tile, number):
-            return tile[:, number * SLOTS : (number + 1) * SLOTS]
+        def own(name, width=SLOTS):
+            return keep.tile([P, width], F32, name=name, align_bytes=64)[:]
 
-        def own(name):
-            return keep.tile([P, SLOTS], F32, name=name, align_bytes=64)[:]
-
-        q_codes, q_scales, scores, w_codes, w_scales, v_codes, v_scales = {}, {}, {}, {}, {}, {}, {}
+        HALF = SLOTS // 2
+        q_woven, q_codes, q_scales, scores, v_codes, v_scales = {}, {}, {}, {}, {}, {}
         v_woven = [keep.tile([P, PACK * E], BF16, name="v_woven%d" % g, align_bytes=64) for g in range(PASSES)]
-        middle = slice(SLOTS // 2, SLOTS // 2 + SLOTS)
-        picked = [own("picked0"), v_woven[0][:].bitcast(F32)[:, middle], own("picked2"), own("picked3")]
-        gates = [own("gates0"), own("gates1"), part(v_raw[1], 3), part(v_raw[1], 0)]
-        late_weighted = own("late_weighted")
-        weighted = [part(v_raw[1], 1), part(v_raw[0], 1), late_weighted, late_weighted]
-        w_woven = [part(v_raw[0], 2), part(v_raw[1], 2), own("w_woven2"), own("w_woven3")]
-        fac_row = part(v_raw[0], 3)[:, : 2 * P].rearrange("m (n e) -> m n e", e=2)
+        middle = slice(HALF, HALF + SLOTS)
+        early_woven = own("early_woven", 2 * SLOTS)
+        gates = [v_woven[0][:].bitcast(F32)[:, middle], v_woven[1][:].bitcast(F32)[:, middle], early_woven[:, HALF // 2 : HALF // 2 + SLOTS], own("gates3")]
+        o_words = own("o_words", 2 * Q)
+        o_woven = o_words.bitcast(BF16).rearrange("p (q r) -> p q r", r=PACK)
+        late_planes = own("late_planes")
+        planes = {(1, 1): own("planes1", HALF), (2, 0): late_planes[:, :HALF], (2, 1): late_planes[:, HALF:]}
+        woven2 = own("woven2")
+        w_woven = {(j, g): early_woven[:, (2 * j + g) * HALF : (2 * j + g + 1) * HALF] for j in range(2) for g in range(PASSES)}
+        w_woven.update({(2, g): woven2[:, g * HALF : (g + 1) * HALF] for g in range(PASSES)})
+        w_woven.update({(LAST, g): o_words[:, g * HALF : (g + 1) * HALF] for g in range(PASSES)})
+        last_weighted = late_planes
+        w_codes = keep.tile([P, TILES * PASSES * P], U32, name="w_codes", align_bytes=64)
+        w_scales = keep.tile([P, TILES * PASSES * P], U8, name="w_scales", align_bytes=64)
         fac_tenth = keep.tile([P, PASSES, PACK], F32, name="fac_tenth")
         neg_th = keep.tile([P, TILES], F32, name="neg_th")
         result = keep.tile([P, PACK, Q], F32, name="result")
         result_by_tile = result[:].rearrange("p r (h j i) -> p j r h i", h=HEADS, j=TILES)
-        o_woven = keep.tile([P, Q, PACK], BF16, name="o_woven", align_bytes=64)
+        turned, summed, mixed = {}, {}, {}
+
+        def weave_queries(j, weave):
+            q_woven[j] = keep.tile([P, P, PACK], BF16, name="q_woven%d" % j, align_bytes=64)
+            weave(
+                q_woven[j][:].rearrange("p (h c i) t -> p h c t i", h=HEADS, i=4),
+                q_raw[:].rearrange("p t (h j c i) -> p j h c t i", h=HEADS, j=TILES, i=4)[:, j],
+            )
 
         def quantise_queries(j):
-            woven = keep.tile([P, P, PACK], BF16, name="q_woven%d" % j, align_bytes=64)
-            shares = QUERY_WEAVERS[j]
-            for number, engine in enumerate(shares):
-                heads = slice(number * HEADS // len(shares), (number + 1) * HEADS // len(shares))
-                weave = nc.vector.tensor_copy if engine == "vector" else nc.scalar.copy
-                weave(
-                    woven[:].rearrange("p (h c i) t -> p h c t i", h=HEADS, i=4)[:, heads],
-                    q_raw[:].rearrange("p t (h j c i) -> p j h c t i", h=HEADS, j=TILES, i=4)[:, j, heads],
-                )
             q_codes[j] = keep.tile([P, P], U32, name="q_codes%d" % j, align_bytes=64)
             q_scales[j] = keep.tile([P, P], U8, name="q_scales%d" % j, align_bytes=64)
-            for number in range(len(shares)):
-                cols = slice(number * P // len(shares), (number + 1) * P // len(shares))
-                nc.vector.quantize_mx(q_codes[j][:, cols].bitcast(FP8X4), q_scales[j][:, cols], woven[:, cols].rearrange("p q t -> p (q t)"))
+            nc.vector.quantize_mx(q_codes[j][:].bitcast(FP8X4), q_scales[j][:], q_woven[j][:].rearrange("p q t -> p (q t)"))
 
         def turn_thresholds():
-            turned = bank(7, [P, P])
-            nc.tensor.transpose(turned[:], th_rows[:], ident[:])
-            nc.scalar.activation(neg_th[:], turned[:, 0:TILES], COPY, scale=-1.0)
+            rows = bank(7, [P, P])
+            nc.tensor.transpose(rows[:], th_rows[:], ident[:])
+            nc.scalar.activation(neg_th[:], rows[:, 0:TILES], COPY, scale=-1.0)
 
         def spread_factors(g):
-            spread = bank(SCORE_BANKS[LAST] + g, [P, PACK, P])
+            spread = bank(FACTOR_BANKS + g, [P, PACK, P])
             for r in range(PACK):
                 nc.tensor.transpose(spread[:, r, :], fac_tenth[:, g, r : r + 1].to_broadcast([P, P]), ident[:])
             return spread[:].rearrange("m (u e) n -> m u n e", u=2)
 
         def score(j):
             scores[j] = keep.tile([P, T], F32, name="scores%d" % j, align_bytes=64)
-            width = BANK // 2 if j < 2 else BANK
+            width = BANK // 2 if j == 0 else BANK
             for h in range(T // width):
-                sums = bank(SCORE_BANKS[j] + h, [P, width])
+                summed[j, h] = bank(SCORE_BANKS[j] + h, [P, width])
                 nc.tensor.matmul_mx(
-                    sums[:],
+                    summed[j, h][:],
                     lhsT=q_codes[j][:].bitcast(FP8X4),
                     lhsT_scale=q_scales[j][:],
                     rhs=k_words[:, 2 * width * h : 2 * width * (h + 1)].bitcast(FP4X4),
@@ -150,71 +151,68 @@ def tile_attend_mqa_ownlists_gated_kernel(tc, query, keys_words, keys_scales, th
                     start=True,
                     stop=True,
                 )
-                empty = nc.vector.tensor_copy if j == 0 and h % 2 == 0 else nc.scalar.copy
-                empty(scores[j][:, width * h : width * (h + 1)], sums[:])
 
-        def pick(j):
-            nc.vector.tensor_copy(picked[j], scores[j][:].indirect(offsets[:]))
+        def keep_scores(j, h, copy):
+            width = summed[j, h].shape[1]
+            copy(scores[j][:, width * h : width * (h + 1)], summed[j, h][:])
 
-        def gate(j):
-            nc.scalar.activation(gates[j], picked[j], SIGMOID, bias=neg_th[:, j : j + 1])
+        def gate(j, part=slice(0, SLOTS)):
+            listed = offsets[:, part.start // GROUP : part.stop // GROUP]
+            nc.scalar.activation(gates[j][:, part], scores[j][:].indirect(listed), SIGMOID, bias=neg_th[:, j : j + 1])
 
-        def place(j):
-            nc.vector.tensor_copy(windows[j % 2][:].indirect(offsets[:]), gates[j])
+        def place(j, part=slice(0, SLOTS)):
+            listed = offsets[:, part.start // GROUP : part.stop // GROUP]
+            nc.vector.tensor_copy(windows[j % 2][:].indirect(listed), gates[j][:, part])
 
-        def weigh_and_turn(j):
-            ordered = weighted[j].bitcast(BF16).rearrange("q (g u p e) -> q g u p e", g=PASSES, u=2, e=2)
-            placed = windows[j % 2][:].rearrange("q (g p u e) -> q g u p e", g=PASSES, u=2, e=2)
-            nc.vector.tensor_tensor(ordered[:, 0], placed[:, 0], spread[0], MULT)
-            nc.vector.tensor_tensor(ordered[:, 1, 0], placed[:, 1, 0], spread[1][:, 0], MULT)
-            last_quarter = keep.tile([P, P], F32, name="last_quarter", align_bytes=64)
-            nc.gpsimd.tensor_tensor(last_quarter[:].bitcast(BF16).rearrange("q (p e) -> q p e", e=2), placed[:, 1, 1], fac_row, MULT)
+        def turn(j):
             for g in range(PASSES):
-                words = weighted[j][:, 2 * P * g : 2 * P * (g + 1)]
-                turned = bank(TURN_BANKS[j] + g, [P, 2, P])
-                for u in range(2):
-                    nc.tensor.transpose(turned[:, u, :], last_quarter[:] if (g, u) == (1, 1) else words[:, u * P : (u + 1) * P], ident[:])
-                nc.scalar.copy(
-                    w_woven[j][:, 2 * P * g : 2 * P * (g + 1)].rearrange("p (q u) -> p q u", u=2),
-                    turned[:].rearrange("p u q -> p q u"),
-                )
-
-        def turn_and_weigh(j):
-            for g in range(PASSES):
-                if (j, g) == (2, 0):
-                    halves = [bank(number, [P, 2, P]) for number in MIX_BANKS[:2]]
-                    turned = [halves[r // 2][:, r % 2, :] for r in range(PACK)]
-                else:
-                    whole = bank(TURN_BANKS[j] + g, [P, PACK, P])
-                    turned = [whole[:, r, :] for r in range(PACK)]
-                planes = weighted[j].bitcast(BF16)[:, g * K_PASS : (g + 1) * K_PASS].rearrange("p (r q) -> p r q", r=PACK)
+                turned[j, g] = bank(TURN_BANKS[j] + g, [P, PACK, P])
                 for r in range(PACK):
-                    nc.tensor.transpose(turned[r], windows[j % 2][:, g * K_PASS + r : (g + 1) * K_PASS : PACK], ident[:])
-                for r in range(PACK):
-                    nc.scalar.activation(planes[:, r, :], turned[r], COPY, scale=fac_tenth[:, g, r : r + 1])
-                nc.scalar.copy(
-                    w_woven[j].bitcast(BF16)[:, g * K_PASS : (g + 1) * K_PASS].rearrange("p (c i r) -> p c r i", i=4, r=PACK),
-                    planes.rearrange("p r (c i) -> p c r i", i=4),
-                )
+                    nc.tensor.transpose(turned[j, g][:, r, :], windows[j % 2][:, g * K_PASS + r : (g + 1) * K_PASS : PACK], ident[:])
 
-        def quantise_weights(j, passes):
-            if passes.start == 0:
-                w_codes[j] = keep.tile([P, PASSES * P], U32, name="w_codes%d" % j, align_bytes=64)
-                w_scales[j] = keep.tile([P, PASSES * P], U8, name="w_scales%d" % j, align_bytes=64)
-            cols = slice(passes.start * P, passes.stop * P)
-            nc.vector.quantize_mx(
-                w_codes[j][:, cols].bitcast(FP8X4),
-                w_scales[j][:, cols],
-                w_woven[j][:, 2 * cols.start : 2 * cols.stop].bitcast(BF16),
+        def weigh_on_vector(j, g):
+            nc.vector.tensor_tensor(
+                w_woven[j, g].bitcast(BF16).rearrange("p (q r) -> p q r", r=PACK),
+                turned[j, g][:].rearrange("p r q -> p q r"),
+                fac_tenth[:, g : g + 1, :].to_broadcast([P, P, PACK]),
+                MULT,
             )
 
-        def weave_values(g):
-            for half in range(2):
-                pair = slice(2 * half, 2 * half + 2)
-                nc.scalar.copy(
-                    v_woven[g][:].rearrange("p (r s t) -> p s t r", r=PACK, t=PACK)[:, :, :, pair],
-                    v_raw[g][:].rearrange("p (t s r) -> p s t r", t=PACK, r=PACK)[:, :, :, pair],
-                )
+        def weigh_on_scalar(j, g, places=range(PACK)):
+            rows = planes[j, g].bitcast(BF16).rearrange("p (r q) -> p r q", r=PACK)
+            for r in places:
+                nc.scalar.activation(rows[:, r, :], turned[j, g][:, r, :], COPY, scale=fac_tenth[:, g, r : r + 1])
+
+        def weave_weights(j, g):
+            nc.scalar.copy(
+                w_woven[j, g].bitcast(BF16).rearrange("p (c i r) -> p c r i", i=4, r=PACK),
+                planes[j, g].bitcast(BF16).rearrange("p (r c i) -> p c r i", r=PACK, i=4),
+            )
+
+        def weigh_last(spread):
+            ordered = last_weighted.bitcast(BF16).rearrange("q (g u p e) -> q g u p e", g=PASSES, u=2, e=2)
+            placed = windows[LAST % 2][:].rearrange("q (g p u e) -> q g u p e", g=PASSES, u=2, e=2)
+            nc.vector.tensor_tensor(ordered[:, 0], placed[:, 0], spread[0], MULT)
+            for u in range(2):
+                nc.vector.tensor_tensor(ordered[:, 1, u], placed[:, 1, u], spread[1][:, u], MULT)
+
+        def turn_last():
+            for g in range(PASSES):
+                pairs = bank(TURN_BANKS[LAST] + g, [P, 2, P])
+                for u in range(2):
+                    nc.tensor.transpose(pairs[:, u, :], last_weighted[:, (2 * g + u) * P : (2 * g + u + 1) * P], ident[:])
+                nc.scalar.copy(w_woven[LAST, g].rearrange("p (q u) -> p q u", u=2), pairs[:].rearrange("p u q -> p q u"))
+
+        def quantise_weights(first, woven):
+            cols = slice(first * P, first * P + woven.shape[1] // 2)
+            nc.vector.quantize_mx(w_codes[:, cols].bitcast(FP8X4), w_scales[:, cols], woven.bitcast(BF16))
+
+        def weave_values(g, half):
+            pair = slice(2 * half, 2 * half + 2)
+            nc.scalar.copy(
+                v_woven[g][:].rearrange("p (r s t) -> p s t r", r=PACK, t=PACK)[:, :, :, pair],
+                v_raw[g][:].rearrange("p (t s r) -> p s t r", t=PACK, r=PACK)[:, :, :, pair],
+            )
 
         def quantise_values(g):
             v_codes[g] = keep.tile([P, E], U32, name="v_codes%d" % g, align_bytes=64)
@@ -222,12 +220,13 @@ def tile_attend_mqa_ownlists_gated_kernel(tc, query, keys_words, keys_scales, th
             nc.vector.quantize_mx(v_codes[g][:].bitcast(FP8X4), v_scales[g][:], v_woven[g][:])
 
         def mix(sums, j, r, g):
+            cols = slice((PASSES * j + g) * P, (PASSES * j + g + 1) * P)
             nc.tensor.matmul_mx(
                 sums,
                 lhsT=v_codes[g][:, r * P : (r + 1) * P].bitcast(FP8X4),
                 lhsT_scale=v_scales[g][:, r * P : (r + 1) * P],
-                rhs=w_codes[j][:, g * P : (g + 1) * P].bitcast(FP8X4),
-                rhs_scale=w_scales[j][:, g * P : (g + 1) * P],
+                rhs=w_codes[:, cols].bitcast(FP8X4),
+                rhs_scale=w_scales[:, cols],
                 start=(g == 0),
                 stop=(g == PASSES - 1),
             )
@@ -235,88 +234,95 @@ def tile_attend_mqa_ownlists_gated_kernel(tc, query, keys_words, keys_scales, th
         def weave_result(weave, tiles, heads):
             chunks = slice(PACK * tiles.start, PACK * tiles.stop)
             weave(
-                o_woven[:].rearrange("p (h c i) r -> p h c r i", h=HEADS, i=4)[:, heads, chunks],
+                o_woven.rearrange("p (h c i) r -> p h c r i", h=HEADS, i=4)[:, heads, chunks],
                 result[:].rearrange("p r (h c i) -> p h c r i", h=HEADS, i=4)[:, heads, chunks],
             )
 
         def mix_tile(j):
-            mixed = bank(MIX_BANKS[j], [P, PACK, P])
+            mixed[j] = bank(MIX_BANKS[j], [P, PACK, P])
             for r in range(PACK):
                 for g in range(PASSES):
-                    mix(mixed[:, r, :], j, r, g)
-            return mixed
+                    mix(mixed[j][:, r, :], j, r, g)
 
-        def keep_tile(j, mixed):
-            nc.scalar.copy(result_by_tile[:, j], mixed[:].rearrange("p r (h i) -> p r h i", h=HEADS))
-            if j < 2:
-                weave_result(nc.vector.tensor_copy, slice(j, j + 1), slice(0, HEADS))
+        def keep_tile(j):
+            nc.scalar.copy(result_by_tile[:, j], mixed[j][:].rearrange("p r (h i) -> p r h i", h=HEADS))
 
         def mix_last_tile():
-            mixed = [bank(LAST_MIX_BANKS[r], [P, P]) for r in range(PACK)]
+            sums = [bank(LAST_MIX_BANKS[r], [P, P]) for r in range(PACK)]
             for g in range(PASSES):
                 for r in range(PACK):
-                    mix(mixed[r][:], LAST, r, g)
+                    mix(sums[r][:], LAST, r, g)
             for r in range(PACK):
                 empty = nc.vector.tensor_copy if r % 2 == 0 else nc.scalar.copy
-                empty(result_by_tile[:, LAST, r], mixed[r][:].rearrange("p (h i) -> p h i", h=HEADS))
+                empty(result_by_tile[:, LAST, r], sums[r][:].rearrange("p (h i) -> p h i", h=HEADS))
 
-        def warm_tensor_engine():
-            idle = bank(MIX_BANKS[1], [P, BANK])
-            for h in range(T // BANK):
-                nc.tensor.matmul_mx(
-                    idle[:],
-                    lhsT=q_codes[LAST][:].bitcast(FP8X4),
-                    lhsT_scale=q_scales[LAST][:],
-                    rhs=k_words[:, 2 * BANK * h : 2 * BANK * (h + 1)].bitcast(FP4X4),
-                    rhs_scale=k_scales[:, BANK * h : BANK * (h + 1)],
-                    start=True,
-                    stop=True,
-                )
-
-        both, first, second = slice(0, 2), slice(0, 1), slice(1, 2)
+        on_vector, on_scalar = nc.vector.tensor_copy, nc.scalar.copy
+        halves = (slice(0, HALF), slice(HALF, SLOTS))
         turn_thresholds()
+        weave_queries(0, on_vector)
+        weave_queries(1, on_vector)
+        weave_queries(2, on_scalar)
+        weave_queries(3, on_scalar)
         for j in range(TILES):
             quantise_queries(j)
         score(0)
+        for h in range(4):
+            keep_scores(0, h, on_scalar if h % 2 == 0 else on_vector)
         score(1)
-        pick(0)
-        pick(1)
-        gate(0)
-        place(0)
         score(2)
-        pick(2)
+        score(3)
+        keep_scores(1, 0, on_vector)
+        for half in halves:
+            gate(0, half)
+            place(0, half)
+        nc.gpsimd.tensor_scalar(fac_tenth[:], fac_col[:], 0.1, 0.0, MULT, ADD)
+        keep_scores(1, 1, on_scalar)
+        keep_scores(2, 0, on_scalar)
         gate(1)
         place(1)
-        score(3)
-        pick(3)
-        nc.gpsimd.tensor_scalar(fac_tenth[:], fac_col[:], 0.1, 0.0, MULT, ADD)
-        spread = [spread_factors(g) for g in range(PASSES)]
-        weave_values(0)
-        weave_values(1)
+        turn(0)
+        keep_scores(2, 1, on_scalar)
+        weave_values(0, 0)
         gate(2)
+        place(2)
+        turn(1)
+        weave_values(0, 1)
+        weave_values(1, 0)
+        weave_values(1, 1)
+        weigh_on_vector(0, 0)
+        weigh_on_vector(0, 1)
+        weigh_on_vector(1, 0)
+        turn(2)
         quantise_values(0)
         quantise_values(1)
-        turn_and_weigh(0)
-        nc.scalar.copy(fac_row, spread[1][:, 1])
-        place(2)
-        turn_and_weigh(1)
+        weigh_on_scalar(1, 1)
+        keep_scores(3, 0, on_scalar)
+        weave_weights(1, 1)
+        keep_scores(3, 1, on_scalar)
+        quantise_weights(0, early_woven)
         gate(3)
-        quantise_weights(0, both)
-        turn_and_weigh(2)
-        quantise_weights(1, both)
         place(3)
-        keep_tile(0, mix_tile(0))
-        warm_tensor_engine()
-        mixed = mix_tile(1)
-        weigh_and_turn(3)
-        quantise_weights(2, both)
-        quantise_weights(3, first)
-        quantise_weights(3, second)
-        keep_tile(1, mixed)
-        keep_tile(2, mix_tile(2))
+        spread = [spread_factors(g) for g in range(PASSES)]
+        weigh_on_scalar(2, 1, range(PACK - 1))
+        weigh_on_scalar(2, 0)
+        weigh_on_scalar(2, 1, range(PACK - 1, PACK))
+        weave_weights(2, 0)
+        weave_weights(2, 1)
+        mix_tile(0)
+        mix_tile(1)
+        keep_tile(0)
+        keep_tile(1)
+        weigh_last(spread)
+        quantise_weights(2 * PASSES, woven2)
+        mix_tile(2)
+        turn_last()
+        for g in range(PASSES):
+            quantise_weights(LAST * PASSES + g, w_woven[LAST, g])
+        weave_result(on_vector, slice(0, 2), slice(0, HEADS))
+        keep_tile(2)
         mix_last_tile()
-        weave_result(nc.vector.tensor_copy, slice(2, TILES), slice(0, HEADS // 2))
-        weave_result(nc.scalar.copy, slice(2, TILES), slice(HEADS // 2, HEADS))
+        weave_result(on_vector, slice(2, TILES), slice(0, HEADS // 2))
+        weave_result(on_scalar, slice(2, TILES), slice(HEADS // 2, HEADS))
 
         out_rows = out_0.rearrange("(p r) q -> p r q", r=PACK)
         for rows in (slice(0, 1), slice(1, 2), slice(2, PACK)):

@@ -91,16 +91,20 @@ def tile_attend_mqa_ownlists_gated_kernel(tc, query, keys_words, keys_scales, th
         def own(name, width=SLOTS):
             return keep.tile([P, width], F32, name=name, align_bytes=64)[:]
 
+        def tagged(tag, dtype):
+            return keep.tile([P, SLOTS], dtype, name="%s_%d" % (tag, dtype == F32), tag=tag, align_bytes=64)[:]
+
         HALF = SLOTS // 2
         q_woven, q_codes, q_scales, scores, v_codes, v_scales = {}, {}, {}, {}, {}, {}
         v_woven = [keep.tile([P, PACK * E], BF16, name="v_woven%d" % g, align_bytes=64) for g in range(PASSES)]
-        middle = slice(HALF, HALF + SLOTS)
-        early_woven = own("early_woven", 2 * SLOTS)
-        gates = [v_woven[0][:].bitcast(F32)[:, middle], v_woven[1][:].bitcast(F32)[:, middle], early_woven[:, HALF // 2 : HALF // 2 + SLOTS], own("gates3")]
+        early = own("early", 2 * SLOTS + HALF)
+        early_woven = early[:, HALF:]
+        early_planes = own("early_planes", 3 * HALF)
+        gates = [tagged("gates0", F32), early[:, :SLOTS], tagged("gates2", F32), early_planes[:, :SLOTS]]
         o_words = own("o_words", 2 * Q)
         o_woven = o_words.bitcast(BF16).rearrange("p (q r) -> p q r", r=PACK)
         late_planes = own("late_planes")
-        planes = {(1, 1): own("planes1", HALF), (2, 0): late_planes[:, :HALF], (2, 1): late_planes[:, HALF:]}
+        planes = {(0, 1): early_planes[:, :HALF], (1, 0): early_planes[:, HALF:SLOTS], (1, 1): early_planes[:, SLOTS:], (2, 0): late_planes[:, :HALF], (2, 1): late_planes[:, HALF:]}
         woven2 = own("woven2")
         w_woven = {(j, g): early_woven[:, (2 * j + g) * HALF : (2 * j + g + 1) * HALF] for j in range(2) for g in range(PASSES)}
         w_woven.update({(2, g): woven2[:, g * HALF : (g + 1) * HALF] for g in range(PASSES)})
@@ -207,17 +211,21 @@ def tile_attend_mqa_ownlists_gated_kernel(tc, query, keys_words, keys_scales, th
             cols = slice(first * P, first * P + woven.shape[1] // 2)
             nc.vector.quantize_mx(w_codes[:, cols].bitcast(FP8X4), w_scales[:, cols], woven.bitcast(BF16))
 
-        def weave_values(g, half):
-            pair = slice(2 * half, 2 * half + 2)
-            nc.scalar.copy(
-                v_woven[g][:].rearrange("p (r s t) -> p s t r", r=PACK, t=PACK)[:, :, :, pair],
-                v_raw[g][:].rearrange("p (t s r) -> p s t r", t=PACK, r=PACK)[:, :, :, pair],
-            )
+        def weave_values(g):
+            for r in range(PACK):
+                nc.gpsimd.tensor_scalar(
+                    v_woven[g][:].rearrange("p (r s t) -> p r s t", r=PACK, t=PACK)[:, r],
+                    v_raw[g][:].rearrange("p (t s r) -> p r s t", t=PACK, r=PACK)[:, r],
+                    1.0,
+                    0.0,
+                    MULT,
+                    ADD,
+                )
 
         def quantise_values(g):
-            v_codes[g] = keep.tile([P, E], U32, name="v_codes%d" % g, align_bytes=64)
+            v_codes[g] = tagged("gates%d" % (2 * g), U32)
             v_scales[g] = keep.tile([P, E], U8, name="v_scales%d" % g, align_bytes=64)
-            nc.vector.quantize_mx(v_codes[g][:].bitcast(FP8X4), v_scales[g][:], v_woven[g][:])
+            nc.vector.quantize_mx(v_codes[g].bitcast(FP8X4), v_scales[g][:], v_woven[g][:])
 
         def mix(sums, j, r, g):
             cols = slice((PASSES * j + g) * P, (PASSES * j + g + 1) * P)
@@ -276,29 +284,29 @@ def tile_attend_mqa_ownlists_gated_kernel(tc, query, keys_words, keys_scales, th
             gate(0, half)
             place(0, half)
         nc.gpsimd.tensor_scalar(fac_tenth[:], fac_col[:], 0.1, 0.0, MULT, ADD)
+        weave_values(0)
+        weave_values(1)
         keep_scores(1, 1, on_scalar)
         keep_scores(2, 0, on_scalar)
         gate(1)
         place(1)
         turn(0)
         keep_scores(2, 1, on_scalar)
-        weave_values(0, 0)
+        keep_scores(3, 0, on_scalar)
         gate(2)
+        quantise_values(0)
         place(2)
         turn(1)
-        weave_values(0, 1)
-        weave_values(1, 0)
-        weave_values(1, 1)
-        weigh_on_vector(0, 0)
-        weigh_on_vector(0, 1)
-        weigh_on_vector(1, 0)
-        turn(2)
-        quantise_values(0)
-        quantise_values(1)
-        weigh_on_scalar(1, 1)
-        keep_scores(3, 0, on_scalar)
-        weave_weights(1, 1)
         keep_scores(3, 1, on_scalar)
+        weigh_on_vector(0, 0)
+        turn(2)
+        quantise_values(1)
+        weigh_on_scalar(0, 1)
+        weigh_on_scalar(1, 0)
+        weave_weights(0, 1)
+        weigh_on_scalar(1, 1)
+        weave_weights(1, 0)
+        weave_weights(1, 1)
         quantise_weights(0, early_woven)
         gate(3)
         place(3)

@@ -30,10 +30,10 @@ LAST = TILES - 1
 PASSES = T // K_PASS
 BANK = 512
 SCORE_BANKS = (0, 4, 6, 0)
-TURN_BANKS = (2, 4, 6, 2)
+TURN_BANKS = (2, 4, 6, 6)
 FACTOR_BANKS = 4
-MIX_BANKS = (6, 7, 0)
-LAST_MIX_BANKS = (1, 4, 5, 2)
+MIX_BANKS = (2, 3, 0)
+LAST_MIX_BANKS = (1, 4, 5, 6)
 
 
 def tile_attend_mqa_ownlists_gated_kernel(tc, query, keys_words, keys_scales, th, fac, vals, offs, out_0, out_1, out_2):
@@ -69,9 +69,11 @@ def tile_attend_mqa_ownlists_gated_kernel(tc, query, keys_words, keys_scales, th
         nc.sync.dma_start(offsets[:], offs)
         fac_col = keep.tile([P, PASSES, PACK], F32, name="fac_col")
         nc.sync.dma_start(fac_col[:], fac.rearrange("(g p r) o -> p g (r o)", g=PASSES, r=PACK))
-        v_raw = [keep.tile([P, PACK * E], F32, name="v_raw%d" % g, align_bytes=64) for g in range(PASSES)]
+        first_values = keep.tile([P, PACK * E], F32, name="first_values", align_bytes=64)
+        second_values = keep.tile([P, SLOTS // 2 + PACK * E], F32, name="second_values", align_bytes=64)
+        v_raw = [first_values[:], second_values[:, SLOTS // 2 :]]
         for g in range(PASSES):
-            nc.sync.dma_start(v_raw[g][:], vals[g * K_PASS : (g + 1) * K_PASS, :].rearrange("(p t) e -> p (t e)", t=PACK))
+            nc.sync.dma_start(v_raw[g], vals[g * K_PASS : (g + 1) * K_PASS, :].rearrange("(p t) e -> p (t e)", t=PACK))
 
         ones = keep.tile([P, QUAD], F32, name="ones")
         nc.vector.memset(ones[:], 1.0)
@@ -91,23 +93,17 @@ def tile_attend_mqa_ownlists_gated_kernel(tc, query, keys_words, keys_scales, th
         def own(name, width=SLOTS):
             return keep.tile([P, width], F32, name=name, align_bytes=64)[:]
 
-        def tagged(tag, dtype):
-            return keep.tile([P, SLOTS], dtype, name="%s_%d" % (tag, dtype == F32), tag=tag, align_bytes=64)[:]
-
         HALF = SLOTS // 2
-        q_woven, q_codes, q_scales, scores, v_codes, v_scales = {}, {}, {}, {}, {}, {}
-        v_woven = [keep.tile([P, PACK * E], BF16, name="v_woven%d" % g, align_bytes=64) for g in range(PASSES)]
-        early = own("early", 2 * SLOTS + HALF)
-        early_woven = early[:, HALF:]
-        early_planes = own("early_planes", 3 * HALF)
-        gates = [tagged("gates0", F32), early[:, :SLOTS], tagged("gates2", F32), early_planes[:, :SLOTS]]
-        o_words = own("o_words", 2 * Q)
-        o_woven = o_words.bitcast(BF16).rearrange("p (q r) -> p q r", r=PACK)
+        q_woven, q_codes, q_scales, scores = {}, {}, {}, {}
+        v_woven = keep.tile([P, PASSES * PACK * E], BF16, name="v_woven", align_bytes=64)
+        early_planes = own("early_planes", SLOTS + HALF)
+        gates = [own("gates0"), own("gates1"), own("gates2"), second_values[:, :SLOTS]]
         late_planes = own("late_planes")
         planes = {(0, 1): early_planes[:, :HALF], (1, 0): early_planes[:, HALF:SLOTS], (1, 1): early_planes[:, SLOTS:], (2, 0): late_planes[:, :HALF], (2, 1): late_planes[:, HALF:]}
         woven2 = own("woven2")
-        w_woven = {(j, g): early_woven[:, (2 * j + g) * HALF : (2 * j + g + 1) * HALF] for j in range(2) for g in range(PASSES)}
-        w_woven.update({(2, g): woven2[:, g * HALF : (g + 1) * HALF] for g in range(PASSES)})
+        o_words = own("o_words", 2 * Q)
+        o_woven = o_words.bitcast(BF16).rearrange("p (q r) -> p q r", r=PACK)
+        w_woven = {(2, g): woven2[:, g * HALF : (g + 1) * HALF] for g in range(PASSES)}
         w_woven.update({(LAST, g): o_words[:, g * HALF : (g + 1) * HALF] for g in range(PASSES)})
         last_weighted = late_planes
         w_codes = keep.tile([P, TILES * PASSES * P], U32, name="w_codes", align_bytes=64)
@@ -142,7 +138,7 @@ def tile_attend_mqa_ownlists_gated_kernel(tc, query, keys_words, keys_scales, th
             return spread[:].rearrange("m (u e) n -> m u n e", u=2)
 
         def score(j):
-            scores[j] = keep.tile([P, T], F32, name="scores%d" % j, align_bytes=64)
+            scores[j] = keep.tile([P, T], F32, name="scores%d" % j, tag="scores%d" % j, align_bytes=64)
             width = BANK // 2 if j == 0 else BANK
             for h in range(T // width):
                 summed[j, h] = bank(SCORE_BANKS[j] + h, [P, width])
@@ -182,9 +178,9 @@ def tile_attend_mqa_ownlists_gated_kernel(tc, query, keys_words, keys_scales, th
                 MULT,
             )
 
-        def weigh_on_scalar(j, g, places=range(PACK)):
+        def weigh_on_scalar(j, g):
             rows = planes[j, g].bitcast(BF16).rearrange("p (r q) -> p r q", r=PACK)
-            for r in places:
+            for r in range(PACK):
                 nc.scalar.activation(rows[:, r, :], turned[j, g][:, r, :], COPY, scale=fac_tenth[:, g, r : r + 1])
 
         def weave_weights(j, g):
@@ -212,27 +208,17 @@ def tile_attend_mqa_ownlists_gated_kernel(tc, query, keys_words, keys_scales, th
             nc.vector.quantize_mx(w_codes[:, cols].bitcast(FP8X4), w_scales[:, cols], woven.bitcast(BF16))
 
         def weave_values(g):
+            woven = v_woven[:, g * PACK * E : (g + 1) * PACK * E].rearrange("p (r s t) -> p r s t", r=PACK, t=PACK)
+            raw = v_raw[g].rearrange("p (t s r) -> p r s t", t=PACK, r=PACK)
             for r in range(PACK):
-                nc.gpsimd.tensor_scalar(
-                    v_woven[g][:].rearrange("p (r s t) -> p r s t", r=PACK, t=PACK)[:, r],
-                    v_raw[g][:].rearrange("p (t s r) -> p r s t", t=PACK, r=PACK)[:, r],
-                    1.0,
-                    0.0,
-                    MULT,
-                    ADD,
-                )
-
-        def quantise_values(g):
-            v_codes[g] = tagged("gates%d" % (2 * g), U32)
-            v_scales[g] = keep.tile([P, E], U8, name="v_scales%d" % g, align_bytes=64)
-            nc.vector.quantize_mx(v_codes[g].bitcast(FP8X4), v_scales[g][:], v_woven[g][:])
+                nc.gpsimd.tensor_scalar(woven[:, r], raw[:, r], 1.0, 0.0, MULT, ADD)
 
         def mix(sums, j, r, g):
             cols = slice((PASSES * j + g) * P, (PASSES * j + g + 1) * P)
             nc.tensor.matmul_mx(
                 sums,
-                lhsT=v_codes[g][:, r * P : (r + 1) * P].bitcast(FP8X4),
-                lhsT_scale=v_scales[g][:, r * P : (r + 1) * P],
+                lhsT=v_codes[:, g * E + r * P : g * E + (r + 1) * P].bitcast(FP8X4),
+                lhsT_scale=v_scales[:, g * E + r * P : g * E + (r + 1) * P],
                 rhs=w_codes[:, cols].bitcast(FP8X4),
                 rhs_scale=w_scales[:, cols],
                 start=(g == 0),
@@ -280,40 +266,44 @@ def tile_attend_mqa_ownlists_gated_kernel(tc, query, keys_words, keys_scales, th
         score(2)
         score(3)
         keep_scores(1, 0, on_vector)
+        keep_scores(1, 1, on_vector)
         for half in halves:
             gate(0, half)
             place(0, half)
         nc.gpsimd.tensor_scalar(fac_tenth[:], fac_col[:], 0.1, 0.0, MULT, ADD)
         weave_values(0)
         weave_values(1)
-        keep_scores(1, 1, on_scalar)
-        keep_scores(2, 0, on_scalar)
         gate(1)
+        early_woven = keep.tile([P, 2 * SLOTS], F32, name="early_woven", tag="scores1", align_bytes=64)[:]
+        w_woven.update({(j, g): early_woven[:, (2 * j + g) * HALF : (2 * j + g + 1) * HALF] for j in range(2) for g in range(PASSES)})
         place(1)
         turn(0)
+        keep_scores(2, 0, on_scalar)
         keep_scores(2, 1, on_scalar)
         keep_scores(3, 0, on_scalar)
         gate(2)
-        quantise_values(0)
+        weigh_on_vector(0, 0)
         place(2)
         turn(1)
         keep_scores(3, 1, on_scalar)
-        weigh_on_vector(0, 0)
         turn(2)
-        quantise_values(1)
         weigh_on_scalar(0, 1)
-        weigh_on_scalar(1, 0)
+        gate(3, halves[0])
+        place(3, halves[0])
         weave_weights(0, 1)
+        weigh_on_scalar(1, 0)
         weigh_on_scalar(1, 1)
         weave_weights(1, 0)
         weave_weights(1, 1)
+        gate(3, halves[1])
+        v_codes = keep.tile([P, PASSES * E], U32, name="v_codes", align_bytes=64)
+        v_scales = keep.tile([P, PASSES * E], U8, name="v_scales", align_bytes=64)
+        nc.vector.quantize_mx(v_codes[:].bitcast(FP8X4), v_scales[:], v_woven[:])
         quantise_weights(0, early_woven)
-        gate(3)
-        place(3)
+        place(3, halves[1])
         spread = [spread_factors(g) for g in range(PASSES)]
-        weigh_on_scalar(2, 1, range(PACK - 1))
         weigh_on_scalar(2, 0)
-        weigh_on_scalar(2, 1, range(PACK - 1, PACK))
+        weigh_on_scalar(2, 1)
         weave_weights(2, 0)
         weave_weights(2, 1)
         mix_tile(0)

@@ -30,10 +30,10 @@ LAST = TILES - 1
 PASSES = T // K_PASS
 BANK = 512
 SCORE_BANKS = (0, 4, 6, 0)
-TURN_BANKS = (2, 4, 6, 6)
-FACTOR_BANKS = 4
-MIX_BANKS = (2, 3, 0)
-LAST_MIX_BANKS = (1, 4, 5, 6)
+TURN_BANKS = (2, 4, 6, 3)
+FACTOR_BANKS = 0
+MIX_BANKS = (2, 6, 5)
+LAST_MIX_BANKS = (0, 1, 7, 2)
 
 
 def tile_attend_mqa_ownlists_gated_kernel(tc, query, keys_words, keys_scales, th, fac, vals, offs, out_0, out_1, out_2):
@@ -96,16 +96,15 @@ def tile_attend_mqa_ownlists_gated_kernel(tc, query, keys_words, keys_scales, th
         HALF = SLOTS // 2
         q_woven, q_codes, q_scales, scores = {}, {}, {}, {}
         v_woven = keep.tile([P, PASSES * PACK * E], BF16, name="v_woven", align_bytes=64)
-        early_planes = own("early_planes", SLOTS + HALF)
+        early_planes = own("early_planes", 2 * SLOTS)
         gates = [own("gates0"), own("gates1"), own("gates2"), second_values[:, :SLOTS]]
-        late_planes = own("late_planes")
-        planes = {(0, 1): early_planes[:, :HALF], (1, 0): early_planes[:, HALF:SLOTS], (1, 1): early_planes[:, SLOTS:], (2, 0): late_planes[:, :HALF], (2, 1): late_planes[:, HALF:]}
+        last_weighted = own("last_weighted")
+        planes = {(0, 1): early_planes[:, :HALF], (1, 0): early_planes[:, HALF:SLOTS], (1, 1): early_planes[:, SLOTS : SLOTS + HALF], (2, 0): last_weighted[:, HALF - 5 * GROUP : SLOTS - 5 * GROUP], (2, 1): own("late_planes", HALF), (0, 0): early_planes[:, SLOTS + HALF :]}
         woven2 = own("woven2")
         o_words = own("o_words", 2 * Q)
         o_woven = o_words.bitcast(BF16).rearrange("p (q r) -> p q r", r=PACK)
         w_woven = {(2, g): woven2[:, g * HALF : (g + 1) * HALF] for g in range(PASSES)}
         w_woven.update({(LAST, g): o_words[:, g * HALF : (g + 1) * HALF] for g in range(PASSES)})
-        last_weighted = late_planes
         w_codes = keep.tile([P, TILES * PASSES * P], U32, name="w_codes", align_bytes=64)
         w_scales = keep.tile([P, TILES * PASSES * P], U8, name="w_scales", align_bytes=64)
         fac_tenth = keep.tile([P, PASSES, PACK], F32, name="fac_tenth")
@@ -115,7 +114,7 @@ def tile_attend_mqa_ownlists_gated_kernel(tc, query, keys_words, keys_scales, th
         turned, summed, mixed = {}, {}, {}
 
         def weave_queries(j, weave):
-            q_woven[j] = keep.tile([P, P, PACK], BF16, name="q_woven%d" % j, align_bytes=64)
+            q_woven[j] = keep.tile([P, P, PACK], BF16, name="q_woven%d" % j, tag="q_woven%d" % (j // 2 * j), align_bytes=64)
             weave(
                 q_woven[j][:].rearrange("p (h c i) t -> p h c t i", h=HEADS, i=4),
                 q_raw[:].rearrange("p t (h j c i) -> p j h c t i", h=HEADS, j=TILES, i=4)[:, j],
@@ -170,17 +169,9 @@ def tile_attend_mqa_ownlists_gated_kernel(tc, query, keys_words, keys_scales, th
                 for r in range(PACK):
                     nc.tensor.transpose(turned[j, g][:, r, :], windows[j % 2][:, g * K_PASS + r : (g + 1) * K_PASS : PACK], ident[:])
 
-        def weigh_on_vector(j, g):
-            nc.vector.tensor_tensor(
-                w_woven[j, g].bitcast(BF16).rearrange("p (q r) -> p q r", r=PACK),
-                turned[j, g][:].rearrange("p r q -> p q r"),
-                fac_tenth[:, g : g + 1, :].to_broadcast([P, P, PACK]),
-                MULT,
-            )
-
-        def weigh_on_scalar(j, g):
+        def weigh_on_scalar(j, g, places=range(PACK)):
             rows = planes[j, g].bitcast(BF16).rearrange("p (r q) -> p r q", r=PACK)
-            for r in range(PACK):
+            for r in places:
                 nc.scalar.activation(rows[:, r, :], turned[j, g][:, r, :], COPY, scale=fac_tenth[:, g, r : r + 1])
 
         def weave_weights(j, g):
@@ -238,8 +229,8 @@ def tile_attend_mqa_ownlists_gated_kernel(tc, query, keys_words, keys_scales, th
                 for g in range(PASSES):
                     mix(mixed[j][:, r, :], j, r, g)
 
-        def keep_tile(j):
-            nc.scalar.copy(result_by_tile[:, j], mixed[j][:].rearrange("p r (h i) -> p r h i", h=HEADS))
+        def keep_tile(j, copy):
+            copy(result_by_tile[:, j], mixed[j][:].rearrange("p r (h i) -> p r h i", h=HEADS))
 
         def mix_last_tile():
             sums = [bank(LAST_MIX_BANKS[r], [P, P]) for r in range(PACK)]
@@ -247,17 +238,18 @@ def tile_attend_mqa_ownlists_gated_kernel(tc, query, keys_words, keys_scales, th
                 for r in range(PACK):
                     mix(sums[r][:], LAST, r, g)
             for r in range(PACK):
-                empty = nc.vector.tensor_copy if r % 2 == 0 else nc.scalar.copy
+                empty = nc.scalar.copy if r % 2 == 0 else nc.vector.tensor_copy
                 empty(result_by_tile[:, LAST, r], sums[r][:].rearrange("p (h i) -> p h i", h=HEADS))
 
         on_vector, on_scalar = nc.vector.tensor_copy, nc.scalar.copy
         halves = (slice(0, HALF), slice(HALF, SLOTS))
         turn_thresholds()
         weave_queries(0, on_vector)
+        quantise_queries(0)
         weave_queries(1, on_vector)
         weave_queries(2, on_scalar)
         weave_queries(3, on_scalar)
-        for j in range(TILES):
+        for j in range(1, TILES):
             quantise_queries(j)
         score(0)
         for h in range(4):
@@ -282,14 +274,16 @@ def tile_attend_mqa_ownlists_gated_kernel(tc, query, keys_words, keys_scales, th
         keep_scores(2, 1, on_scalar)
         keep_scores(3, 0, on_scalar)
         gate(2)
-        weigh_on_vector(0, 0)
         place(2)
         turn(1)
         keep_scores(3, 1, on_scalar)
         turn(2)
-        weigh_on_scalar(0, 1)
+        spread = [spread_factors(g) for g in range(PASSES)]
+        weigh_on_scalar(0, 0)
         gate(3, halves[0])
         place(3, halves[0])
+        weigh_on_scalar(0, 1)
+        weave_weights(0, 0)
         weave_weights(0, 1)
         weigh_on_scalar(1, 0)
         weigh_on_scalar(1, 1)
@@ -301,23 +295,23 @@ def tile_attend_mqa_ownlists_gated_kernel(tc, query, keys_words, keys_scales, th
         nc.vector.quantize_mx(v_codes[:].bitcast(FP8X4), v_scales[:], v_woven[:])
         quantise_weights(0, early_woven)
         place(3, halves[1])
-        spread = [spread_factors(g) for g in range(PASSES)]
+        weigh_on_scalar(2, 1, range(PACK - 1))
         weigh_on_scalar(2, 0)
-        weigh_on_scalar(2, 1)
+        weigh_on_scalar(2, 1, range(PACK - 1, PACK))
         weave_weights(2, 0)
         weave_weights(2, 1)
         mix_tile(0)
         mix_tile(1)
-        keep_tile(0)
-        keep_tile(1)
+        keep_tile(0, on_scalar)
         weigh_last(spread)
         quantise_weights(2 * PASSES, woven2)
-        mix_tile(2)
+        keep_tile(1, on_vector)
         turn_last()
+        mix_tile(2)
         for g in range(PASSES):
             quantise_weights(LAST * PASSES + g, w_woven[LAST, g])
         weave_result(on_vector, slice(0, 2), slice(0, HEADS))
-        keep_tile(2)
+        keep_tile(2, on_scalar)
         mix_last_tile()
         weave_result(on_vector, slice(2, TILES), slice(0, HEADS // 2))
         weave_result(on_scalar, slice(2, TILES), slice(HEADS // 2, HEADS))

@@ -29,11 +29,13 @@ TILES = Q // P
 LAST = TILES - 1
 PASSES = T // K_PASS
 BANK = 512
+WINDOWS = 3
 SCORE_BANKS = (0, 4, 6, 0)
-TURN_BANKS = (2, 4, 6, 3)
-FACTOR_BANKS = 0
-MIX_BANKS = (2, 6, 5)
-LAST_MIX_BANKS = (0, 1, 7, 2)
+TURN_BANKS = (2, 4, 6, 4)
+FACTOR_BANKS = 2
+MIX_BANKS = (0, 1)
+LATE_MIX_BANKS = (7, 2, 3, 6)
+OVERLAP_START = 11 * GROUP
 
 
 def tile_attend_mqa_ownlists_gated_kernel(tc, query, keys_words, keys_scales, th, fac, vals, offs, out_0, out_1, out_2):
@@ -86,7 +88,7 @@ def tile_attend_mqa_ownlists_gated_kernel(tc, query, keys_words, keys_scales, th
         for quad in range(4):
             rows = slice(QUAD * quad, QUAD * (quad + 1))
             nc.vector.tensor_tensor(ident[rows, rows], column_number[rows, :], row_number[rows, :], EQUAL)
-        windows = [keep.tile([P, T], F32, name="window%d" % w, tag="window%d" % w, align_bytes=64) for w in range(2)]
+        windows = [keep.tile([P, T], F32, name="window%d" % w, tag="window%d" % w, align_bytes=64) for w in range(WINDOWS)]
         for window in windows:
             nc.vector.memset(window[:], 0.0)
 
@@ -96,14 +98,21 @@ def tile_attend_mqa_ownlists_gated_kernel(tc, query, keys_words, keys_scales, th
         HALF = SLOTS // 2
         q_woven, q_codes, q_scales, scores = {}, {}, {}, {}
         v_woven = keep.tile([P, PASSES * PACK * E], BF16, name="v_woven", align_bytes=64)
-        early_planes = own("early_planes", 2 * SLOTS)
         gates = [own("gates0"), own("gates1"), own("gates2"), second_values[:, :SLOTS]]
-        last_weighted = own("last_weighted")
-        planes = {(0, 1): early_planes[:, :HALF], (1, 0): early_planes[:, HALF:SLOTS], (1, 1): early_planes[:, SLOTS : SLOTS + HALF], (2, 0): last_weighted[:, HALF - 5 * GROUP : SLOTS - 5 * GROUP], (2, 1): own("late_planes", HALF), (0, 0): early_planes[:, SLOTS + HALF :]}
-        woven2 = own("woven2")
+        last_weighted = second_values[:, SLOTS : 2 * SLOTS]
+        first_planes = own("first_planes")
+        planes = {
+            (0, 0): first_planes[:, :HALF],
+            (0, 1): first_planes[:, HALF:],
+            (1, 0): second_values[:, 2 * SLOTS : 2 * SLOTS + HALF],
+            (1, 1): last_weighted[:, OVERLAP_START : OVERLAP_START + HALF],
+            (2, 1): second_values[:, 2 * SLOTS + HALF : 3 * SLOTS],
+        }
+        early_woven = [own("woven0"), own("woven1")]
         o_words = own("o_words", 2 * Q)
         o_woven = o_words.bitcast(BF16).rearrange("p (q r) -> p q r", r=PACK)
-        w_woven = {(2, g): woven2[:, g * HALF : (g + 1) * HALF] for g in range(PASSES)}
+        w_woven = {(j, g): early_woven[j][:, g * HALF : (g + 1) * HALF] for j in range(2) for g in range(PASSES)}
+        w_woven.update({(2, 0): early_woven[1][:, :HALF], (2, 1): own("woven2", HALF)})
         w_woven.update({(LAST, g): o_words[:, g * HALF : (g + 1) * HALF] for g in range(PASSES)})
         w_codes = keep.tile([P, TILES * PASSES * P], U32, name="w_codes", align_bytes=64)
         w_scales = keep.tile([P, TILES * PASSES * P], U8, name="w_scales", align_bytes=64)
@@ -161,13 +170,13 @@ def tile_attend_mqa_ownlists_gated_kernel(tc, query, keys_words, keys_scales, th
 
         def place(j, part=slice(0, SLOTS)):
             listed = offsets[:, part.start // GROUP : part.stop // GROUP]
-            nc.vector.tensor_copy(windows[j % 2][:].indirect(listed), gates[j][:, part])
+            nc.vector.tensor_copy(windows[j % WINDOWS][:].indirect(listed), gates[j][:, part])
 
         def turn(j):
             for g in range(PASSES):
                 turned[j, g] = bank(TURN_BANKS[j] + g, [P, PACK, P])
                 for r in range(PACK):
-                    nc.tensor.transpose(turned[j, g][:, r, :], windows[j % 2][:, g * K_PASS + r : (g + 1) * K_PASS : PACK], ident[:])
+                    nc.tensor.transpose(turned[j, g][:, r, :], windows[j % WINDOWS][:, g * K_PASS + r : (g + 1) * K_PASS : PACK], ident[:])
 
         def weigh_on_scalar(j, g, places=range(PACK)):
             rows = planes[j, g].bitcast(BF16).rearrange("p (r q) -> p r q", r=PACK)
@@ -180,9 +189,17 @@ def tile_attend_mqa_ownlists_gated_kernel(tc, query, keys_words, keys_scales, th
                 planes[j, g].bitcast(BF16).rearrange("p (r c i) -> p c r i", r=PACK, i=4),
             )
 
+        def weigh_on_vector(j, g):
+            nc.vector.tensor_tensor(
+                w_woven[j, g].bitcast(BF16).rearrange("p (q r) -> p q r", r=PACK),
+                turned[j, g][:].rearrange("p r q -> p q r"),
+                fac_tenth[:, g : g + 1, :].to_broadcast([P, P, PACK]),
+                MULT,
+            )
+
         def weigh_last(spread):
             ordered = last_weighted.bitcast(BF16).rearrange("q (g u p e) -> q g u p e", g=PASSES, u=2, e=2)
-            placed = windows[LAST % 2][:].rearrange("q (g p u e) -> q g u p e", g=PASSES, u=2, e=2)
+            placed = windows[LAST % WINDOWS][:].rearrange("q (g p u e) -> q g u p e", g=PASSES, u=2, e=2)
             nc.vector.tensor_tensor(ordered[:, 0], placed[:, 0], spread[0], MULT)
             for u in range(2):
                 nc.vector.tensor_tensor(ordered[:, 1, u], placed[:, 1, u], spread[1][:, u], MULT)
@@ -232,14 +249,17 @@ def tile_attend_mqa_ownlists_gated_kernel(tc, query, keys_words, keys_scales, th
         def keep_tile(j, copy):
             copy(result_by_tile[:, j], mixed[j][:].rearrange("p r (h i) -> p r h i", h=HEADS))
 
-        def mix_last_tile():
-            sums = [bank(LAST_MIX_BANKS[r], [P, P]) for r in range(PACK)]
-            for g in range(PASSES):
-                for r in range(PACK):
-                    mix(sums[r][:], LAST, r, g)
+        def mix_late_tiles():
+            late_columns = result[:].rearrange("p r (h j i) -> p r j h i", h=HEADS, j=TILES)
+            sums = [bank(LATE_MIX_BANKS[r], [P, 2, P]) for r in range(PACK)]
+            for pair in ((0, 1), (2,), (3,)):
+                for j in (2, LAST):
+                    for r in pair:
+                        for g in range(PASSES):
+                            mix(sums[r][:, j - 2, :], j, r, g)
             for r in range(PACK):
                 empty = nc.scalar.copy if r % 2 == 0 else nc.vector.tensor_copy
-                empty(result_by_tile[:, LAST, r], sums[r][:].rearrange("p (h i) -> p h i", h=HEADS))
+                empty(late_columns[:, r, 2:TILES], sums[r][:].rearrange("p j (h i) -> p j h i", h=HEADS))
 
         on_vector, on_scalar = nc.vector.tensor_copy, nc.scalar.copy
         halves = (slice(0, HALF), slice(HALF, SLOTS))
@@ -266,53 +286,50 @@ def tile_attend_mqa_ownlists_gated_kernel(tc, query, keys_words, keys_scales, th
         weave_values(0)
         weave_values(1)
         gate(1)
-        early_woven = keep.tile([P, 2 * SLOTS], F32, name="early_woven", tag="scores1", align_bytes=64)[:]
-        w_woven.update({(j, g): early_woven[:, (2 * j + g) * HALF : (2 * j + g + 1) * HALF] for j in range(2) for g in range(PASSES)})
         place(1)
         turn(0)
         keep_scores(2, 0, on_scalar)
         keep_scores(2, 1, on_scalar)
-        keep_scores(3, 0, on_scalar)
         gate(2)
         place(2)
         turn(1)
+        keep_scores(3, 0, on_scalar)
         keep_scores(3, 1, on_scalar)
-        turn(2)
-        spread = [spread_factors(g) for g in range(PASSES)]
-        weigh_on_scalar(0, 0)
         gate(3, halves[0])
         place(3, halves[0])
-        weigh_on_scalar(0, 1)
-        weave_weights(0, 0)
-        weave_weights(0, 1)
-        weigh_on_scalar(1, 0)
-        weigh_on_scalar(1, 1)
-        weave_weights(1, 0)
-        weave_weights(1, 1)
-        gate(3, halves[1])
+        turn(2)
+        for g in range(PASSES):
+            weigh_on_scalar(0, g)
+        for g in range(PASSES):
+            weave_weights(0, g)
+        spread = [spread_factors(g) for g in range(PASSES)]
+        quantise_weights(0, early_woven[0])
         v_codes = keep.tile([P, PASSES * E], U32, name="v_codes", align_bytes=64)
         v_scales = keep.tile([P, PASSES * E], U8, name="v_scales", align_bytes=64)
         nc.vector.quantize_mx(v_codes[:].bitcast(FP8X4), v_scales[:], v_woven[:])
-        quantise_weights(0, early_woven)
+        gate(3, halves[1])
         place(3, halves[1])
-        weigh_on_scalar(2, 1, range(PACK - 1))
-        weigh_on_scalar(2, 0)
-        weigh_on_scalar(2, 1, range(PACK - 1, PACK))
-        weave_weights(2, 0)
-        weave_weights(2, 1)
         mix_tile(0)
-        mix_tile(1)
-        keep_tile(0, on_scalar)
+        for g in range(PASSES):
+            weigh_on_scalar(1, g)
+        for g in range(PASSES):
+            weave_weights(1, g)
+        quantise_weights(PASSES, early_woven[1])
+        weigh_on_scalar(2, 1)
+        weave_weights(2, 1)
         weigh_last(spread)
-        quantise_weights(2 * PASSES, woven2)
-        keep_tile(1, on_vector)
+        weigh_on_vector(2, 0)
+        keep_tile(0, on_scalar)
         turn_last()
-        mix_tile(2)
+        mix_tile(1)
+        quantise_weights(2 * PASSES + 1, w_woven[2, 1])
+        quantise_weights(2 * PASSES, w_woven[2, 0])
         for g in range(PASSES):
             quantise_weights(LAST * PASSES + g, w_woven[LAST, g])
-        weave_result(on_vector, slice(0, 2), slice(0, HEADS))
-        keep_tile(2, on_scalar)
-        mix_last_tile()
+        keep_tile(1, on_scalar)
+        for j in range(2):
+            weave_result(on_vector, slice(j, j + 1), slice(0, HEADS))
+        mix_late_tiles()
         weave_result(on_vector, slice(2, TILES), slice(0, HEADS // 2))
         weave_result(on_scalar, slice(2, TILES), slice(HEADS // 2, HEADS))
 
@@ -324,9 +341,9 @@ def tile_attend_mqa_ownlists_gated_kernel(tc, query, keys_words, keys_scales, th
         for half in range(2):
             cols = slice(half * Q // 2, (half + 1) * Q // 2)
             nc.vector.quantize_mx(o_codes[:, cols].bitcast(FP8X4), o_scales[:, cols], o_woven[:, cols].rearrange("p q r -> p (q r)"))
+        nc.sync.dma_start(out_1[0].rearrange("p q r -> p (q r)").bitcast(I32), o_codes[:].bitcast(I32))
         for quad in range(4):
             nc.sync.dma_start(
                 out_2[0, 4 * quad : 4 * quad + 4, :].bitcast(I32),
                 o_scales[QUAD * quad : QUAD * quad + 4, :].bitcast(I32),
             )
-        nc.sync.dma_start(out_1[0].rearrange("p q r -> p (q r)").bitcast(I32), o_codes[:].bitcast(I32))

@@ -30,7 +30,12 @@ LAST = TILES - 1
 PASSES = T // K_PASS
 BANK = 512
 WINDOWS = 3
-SCORE_BANKS = (0, 4, 6, 0)
+SCORE_PIECES = (
+    ((0, 256, 0), (256, 256, 1), (512, 256, 2), (768, 128, 3), (896, 128, 7)),
+    ((0, BANK, 4), (BANK, BANK, 5)),
+    ((0, BANK, 6), (BANK, BANK, 7)),
+    ((0, BANK, 0), (BANK, BANK, 1)),
+)
 TURN_BANKS = (2, 4, 6, 4)
 FACTOR_BANKS = 2
 MIX_BANKS = (0, 1)
@@ -62,8 +67,8 @@ def tile_attend_mqa_ownlists_gated_kernel(tc, query, keys_words, keys_scales, th
         )
         for quad in range(4):
             nc.sync.dma_start(
-                k_scales[QUAD * quad : QUAD * quad + 4, :].bitcast(I32),
-                keys_scales[0, 4 * quad : 4 * quad + 4, :].bitcast(I32),
+                k_scales[quad:P:QUAD, :].bitcast(I32),
+                keys_scales[0, quad:16:4, :].bitcast(I32),
             )
         k_words = keep.tile([P, 2 * T], U8, name="k_words", align_bytes=64)
         nc.sync.dma_start(k_words[:].bitcast(I32), keys_words[0].bitcast(I32))
@@ -120,7 +125,7 @@ def tile_attend_mqa_ownlists_gated_kernel(tc, query, keys_words, keys_scales, th
         neg_th = keep.tile([P, TILES], F32, name="neg_th")
         result = keep.tile([P, PACK, Q], F32, name="result")
         result_by_tile = result[:].rearrange("p r (h j i) -> p j r h i", h=HEADS, j=TILES)
-        turned, summed, mixed = {}, {}, {}
+        turned, summed, columns, mixed = {}, {}, {}, {}
 
         def weave_queries(j, weave):
             q_woven[j] = keep.tile([P, P, PACK], BF16, name="q_woven%d" % j, tag="q_woven%d" % (j // 2 * j), align_bytes=64)
@@ -147,22 +152,21 @@ def tile_attend_mqa_ownlists_gated_kernel(tc, query, keys_words, keys_scales, th
 
         def score(j):
             scores[j] = keep.tile([P, T], F32, name="scores%d" % j, tag="scores%d" % j, align_bytes=64)
-            width = BANK // 2 if j == 0 else BANK
-            for h in range(T // width):
-                summed[j, h] = bank(SCORE_BANKS[j] + h, [P, width])
+            for h, (first, width, number) in enumerate(SCORE_PIECES[j]):
+                summed[j, h] = bank(number, [P, width])
+                columns[j, h] = slice(first, first + width)
                 nc.tensor.matmul_mx(
                     summed[j, h][:],
                     lhsT=q_codes[j][:].bitcast(FP8X4),
                     lhsT_scale=q_scales[j][:],
-                    rhs=k_words[:, 2 * width * h : 2 * width * (h + 1)].bitcast(FP4X4),
-                    rhs_scale=k_scales[:, width * h : width * (h + 1)],
+                    rhs=k_words[:, 2 * first : 2 * (first + width)].bitcast(FP4X4),
+                    rhs_scale=k_scales[:, columns[j, h]],
                     start=True,
                     stop=True,
                 )
 
         def keep_scores(j, h, copy):
-            width = summed[j, h].shape[1]
-            copy(scores[j][:, width * h : width * (h + 1)], summed[j, h][:])
+            copy(scores[j][:, columns[j, h]], summed[j, h][:])
 
         def gate(j, part=slice(0, SLOTS)):
             listed = offsets[:, part.start // GROUP : part.stop // GROUP]
@@ -272,19 +276,19 @@ def tile_attend_mqa_ownlists_gated_kernel(tc, query, keys_words, keys_scales, th
         for j in range(1, TILES):
             quantise_queries(j)
         score(0)
-        for h in range(4):
+        for h in range(len(SCORE_PIECES[0])):
             keep_scores(0, h, on_scalar if h % 2 == 0 else on_vector)
         score(1)
         score(2)
         score(3)
         keep_scores(1, 0, on_vector)
-        keep_scores(1, 1, on_vector)
         for half in halves:
             gate(0, half)
             place(0, half)
         nc.gpsimd.tensor_scalar(fac_tenth[:], fac_col[:], 0.1, 0.0, MULT, ADD)
         weave_values(0)
         weave_values(1)
+        keep_scores(1, 1, on_scalar)
         gate(1)
         place(1)
         turn(0)
@@ -344,6 +348,6 @@ def tile_attend_mqa_ownlists_gated_kernel(tc, query, keys_words, keys_scales, th
         nc.sync.dma_start(out_1[0].rearrange("p q r -> p (q r)").bitcast(I32), o_codes[:].bitcast(I32))
         for quad in range(4):
             nc.sync.dma_start(
-                out_2[0, 4 * quad : 4 * quad + 4, :].bitcast(I32),
-                o_scales[QUAD * quad : QUAD * quad + 4, :].bitcast(I32),
+                out_2[0, quad:16:4, :].bitcast(I32),
+                o_scales[quad:P:QUAD, :].bitcast(I32),
             )

@@ -30,6 +30,7 @@ LAST = TILES - 1
 PASSES = T // K_PASS
 BANK = 512
 WINDOWS = 3
+SHARED = 96
 SCORE_PIECES = (
     ((0, 256, 0), (256, 256, 1), (512, 256, 2), (768, 128, 3), (896, 128, 7)),
     ((0, BANK, 4), (BANK, BANK, 5)),
@@ -74,13 +75,14 @@ def tile_attend_mqa_ownlists_gated_kernel(tc, query, keys_words, keys_scales, th
         nc.sync.dma_start(k_words[:].bitcast(I32), keys_words[0].bitcast(I32))
         offsets = keep.tile([P, SLOTS // GROUP], U16, name="offsets")
         nc.sync.dma_start(offsets[:], offs)
-        fac_col = keep.tile([P, PASSES, PACK], F32, name="fac_col")
-        nc.sync.dma_start(fac_col[:], fac.rearrange("(g p r) o -> p g (r o)", g=PASSES, r=PACK))
         first_values = keep.tile([P, PACK * E], F32, name="first_values", align_bytes=64)
         second_values = keep.tile([P, SLOTS // 2 + PACK * E], F32, name="second_values", align_bytes=64)
         v_raw = [first_values[:], second_values[:, SLOTS // 2 :]]
         for g in range(PASSES):
             nc.sync.dma_start(v_raw[g], vals[g * K_PASS : (g + 1) * K_PASS, :].rearrange("(p t) e -> p (t e)", t=PACK))
+
+        fac_col = keep.tile([P, PASSES, PACK], F32, name="fac_col")
+        nc.sync.dma_start(fac_col[:], fac.rearrange("(g p r) o -> p g (r o)", g=PASSES, r=PACK))
 
         ones = keep.tile([P, QUAD], F32, name="ones")
         nc.vector.memset(ones[:], 1.0)
@@ -104,16 +106,16 @@ def tile_attend_mqa_ownlists_gated_kernel(tc, query, keys_words, keys_scales, th
         q_woven, q_codes, q_scales, scores = {}, {}, {}, {}
         v_woven = keep.tile([P, PASSES * PACK * E], BF16, name="v_woven", align_bytes=64)
         gates = [own("gates0"), own("gates1"), own("gates2"), second_values[:, :SLOTS]]
-        last_weighted = second_values[:, SLOTS : 2 * SLOTS]
+        last_weighted = own("last_weighted")
         first_planes = own("first_planes")
         planes = {
             (0, 0): first_planes[:, :HALF],
             (0, 1): first_planes[:, HALF:],
-            (1, 0): second_values[:, 2 * SLOTS : 2 * SLOTS + HALF],
+            (1, 0): own("second_planes", HALF),
             (1, 1): last_weighted[:, OVERLAP_START : OVERLAP_START + HALF],
             (2, 1): second_values[:, 2 * SLOTS + HALF : 3 * SLOTS],
         }
-        early_woven = [own("woven0"), own("woven1")]
+        early_woven = [own("woven0"), second_values[:, SLOTS : 2 * SLOTS]]
         o_words = own("o_words", 2 * Q)
         o_woven = o_words.bitcast(BF16).rearrange("p (q r) -> p q r", r=PACK)
         w_woven = {(j, g): early_woven[j][:, g * HALF : (g + 1) * HALF] for j in range(2) for g in range(PASSES)}
@@ -219,11 +221,13 @@ def tile_attend_mqa_ownlists_gated_kernel(tc, query, keys_words, keys_scales, th
             cols = slice(first * P, first * P + woven.shape[1] // 2)
             nc.vector.quantize_mx(w_codes[:, cols].bitcast(FP8X4), w_scales[:, cols], woven.bitcast(BF16))
 
-        def weave_values(g):
-            woven = v_woven[:, g * PACK * E : (g + 1) * PACK * E].rearrange("p (r s t) -> p r s t", r=PACK, t=PACK)
-            raw = v_raw[g].rearrange("p (t s r) -> p r s t", t=PACK, r=PACK)
-            for r in range(PACK):
-                nc.gpsimd.tensor_scalar(woven[:, r], raw[:, r], 1.0, 0.0, MULT, ADD)
+        def weave_values(g, groups, weave):
+            woven = v_woven[:, g * PACK * E : (g + 1) * PACK * E].rearrange("p (r s t) -> p s r t", r=PACK, t=PACK)
+            raw = v_raw[g].rearrange("p (t s r) -> p s r t", t=PACK, r=PACK)
+            weave(woven[:, groups], raw[:, groups])
+
+        def on_gpsimd(out, in_):
+            nc.gpsimd.tensor_scalar(out, in_, 1.0, 0.0, MULT, ADD)
 
         def mix(sums, j, r, g):
             cols = slice((PASSES * j + g) * P, (PASSES * j + g + 1) * P)
@@ -285,9 +289,10 @@ def tile_attend_mqa_ownlists_gated_kernel(tc, query, keys_words, keys_scales, th
         for half in halves:
             gate(0, half)
             place(0, half)
-        nc.gpsimd.tensor_scalar(fac_tenth[:], fac_col[:], 0.1, 0.0, MULT, ADD)
-        weave_values(0)
-        weave_values(1)
+        weave_values(0, slice(0, P // 2), on_gpsimd)
+        weave_values(0, slice(P // 2, P), on_gpsimd)
+        weave_values(1, slice(0, SHARED // 2), on_gpsimd)
+        weave_values(1, slice(SHARED // 2, SHARED), on_gpsimd)
         keep_scores(1, 1, on_scalar)
         gate(1)
         place(1)
@@ -299,9 +304,11 @@ def tile_attend_mqa_ownlists_gated_kernel(tc, query, keys_words, keys_scales, th
         turn(1)
         keep_scores(3, 0, on_scalar)
         keep_scores(3, 1, on_scalar)
+        nc.scalar.activation(fac_tenth[:], fac_col[:], COPY, scale=0.1)
         gate(3, halves[0])
         place(3, halves[0])
         turn(2)
+        weave_values(1, slice(SHARED, P), on_scalar)
         for g in range(PASSES):
             weigh_on_scalar(0, g)
         for g in range(PASSES):

@@ -30,17 +30,16 @@ LAST = TILES - 1
 PASSES = T // K_PASS
 BANK = 512
 WINDOWS = 3
-SHARED = 96
 SCORE_PIECES = (
     ((0, 256, 0), (256, 256, 1), (512, 256, 2), (768, 128, 3), (896, 128, 7)),
-    ((0, BANK, 4), (BANK, BANK, 5)),
+    ((0, BANK, 4), (BANK, 256, 5), (768, 256, 0)),
     ((0, BANK, 6), (BANK, BANK, 7)),
     ((0, BANK, 0), (BANK, BANK, 1)),
 )
 TURN_BANKS = (2, 4, 6, 4)
 FACTOR_BANKS = 2
-MIX_BANKS = (0, 1)
-LATE_MIX_BANKS = (7, 2, 3, 6)
+MIX_BANKS = ((0,), (1, 3))
+LATE_MIX_BANKS = (7, 2, 4, 0, 6)
 OVERLAP_START = 11 * GROUP
 
 
@@ -76,8 +75,8 @@ def tile_attend_mqa_ownlists_gated_kernel(tc, query, keys_words, keys_scales, th
         offsets = keep.tile([P, SLOTS // GROUP], U16, name="offsets")
         nc.sync.dma_start(offsets[:], offs)
         first_values = keep.tile([P, PACK * E], F32, name="first_values", align_bytes=64)
-        second_values = keep.tile([P, SLOTS // 2 + PACK * E], F32, name="second_values", align_bytes=64)
-        v_raw = [first_values[:], second_values[:, SLOTS // 2 :]]
+        second_values = keep.tile([P, SLOTS + PACK * E], F32, name="second_values", align_bytes=64)
+        v_raw = [first_values[:], second_values[:, SLOTS // 2 : SLOTS // 2 + PACK * E]]
         for g in range(PASSES):
             nc.sync.dma_start(v_raw[g], vals[g * K_PASS : (g + 1) * K_PASS, :].rearrange("(p t) e -> p (t e)", t=PACK))
 
@@ -97,7 +96,7 @@ def tile_attend_mqa_ownlists_gated_kernel(tc, query, keys_words, keys_scales, th
             nc.vector.tensor_tensor(ident[rows, rows], column_number[rows, :], row_number[rows, :], EQUAL)
         windows = [keep.tile([P, T], F32, name="window%d" % w, tag="window%d" % w, align_bytes=64) for w in range(WINDOWS)]
         for window in windows:
-            nc.vector.memset(window[:], 0.0)
+            nc.vector.memset(window[:].bitcast(I32), 0)
 
         def own(name, width=SLOTS):
             return keep.tile([P, width], F32, name=name, align_bytes=64)[:]
@@ -115,7 +114,7 @@ def tile_attend_mqa_ownlists_gated_kernel(tc, query, keys_words, keys_scales, th
             (1, 1): last_weighted[:, OVERLAP_START : OVERLAP_START + HALF],
             (2, 1): second_values[:, 2 * SLOTS + HALF : 3 * SLOTS],
         }
-        early_woven = [own("woven0"), second_values[:, SLOTS : 2 * SLOTS]]
+        early_woven = [second_values[:, PACK * E :], second_values[:, SLOTS : 2 * SLOTS]]
         o_words = own("o_words", 2 * Q)
         o_woven = o_words.bitcast(BF16).rearrange("p (q r) -> p q r", r=PACK)
         w_woven = {(j, g): early_woven[j][:, g * HALF : (g + 1) * HALF] for j in range(2) for g in range(PASSES)}
@@ -221,13 +220,10 @@ def tile_attend_mqa_ownlists_gated_kernel(tc, query, keys_words, keys_scales, th
             cols = slice(first * P, first * P + woven.shape[1] // 2)
             nc.vector.quantize_mx(w_codes[:, cols].bitcast(FP8X4), w_scales[:, cols], woven.bitcast(BF16))
 
-        def weave_values(g, groups, weave):
+        def weave_values(g, groups):
             woven = v_woven[:, g * PACK * E : (g + 1) * PACK * E].rearrange("p (r s t) -> p s r t", r=PACK, t=PACK)
             raw = v_raw[g].rearrange("p (t s r) -> p s r t", t=PACK, r=PACK)
-            weave(woven[:, groups], raw[:, groups])
-
-        def on_gpsimd(out, in_):
-            nc.gpsimd.tensor_scalar(out, in_, 1.0, 0.0, MULT, ADD)
+            nc.gpsimd.tensor_scalar(woven[:, groups], raw[:, groups], 1.0, 0.0, MULT, ADD)
 
         def mix(sums, j, r, g):
             cols = slice((PASSES * j + g) * P, (PASSES * j + g + 1) * P)
@@ -248,26 +244,34 @@ def tile_attend_mqa_ownlists_gated_kernel(tc, query, keys_words, keys_scales, th
                 result[:].rearrange("p r (h c i) -> p h c r i", h=HEADS, i=4)[:, heads, chunks],
             )
 
-        def mix_tile(j):
-            mixed[j] = bank(MIX_BANKS[j], [P, PACK, P])
-            for r in range(PACK):
+        def mix_tile(j, part=0):
+            count = PACK // len(MIX_BANKS[j])
+            mixed[j, part] = bank(MIX_BANKS[j][part], [P, count, P])
+            for r in range(count):
                 for g in range(PASSES):
-                    mix(mixed[j][:, r, :], j, r, g)
+                    mix(mixed[j, part][:, r, :], j, part * count + r, g)
 
-        def keep_tile(j, copy):
-            copy(result_by_tile[:, j], mixed[j][:].rearrange("p r (h i) -> p r h i", h=HEADS))
+        def keep_tile(j, copy, part=0):
+            count = PACK // len(MIX_BANKS[j])
+            copy(result_by_tile[:, j, part * count : (part + 1) * count], mixed[j, part][:].rearrange("p r (h i) -> p r h i", h=HEADS))
+
+        def mix_late(number, tiles, groups):
+            sums = bank(number, [P, len(groups), len(tiles), P])
+            for b, j in enumerate(tiles):
+                for a, r in enumerate(groups):
+                    for g in range(PASSES):
+                        mix(sums[:, a, b, :], j, r, g)
+            return sums[:].rearrange("p r j (h i) -> p r j h i", h=HEADS)
 
         def mix_late_tiles():
-            late_columns = result[:].rearrange("p r (h j i) -> p r j h i", h=HEADS, j=TILES)
-            sums = [bank(LATE_MIX_BANKS[r], [P, 2, P]) for r in range(PACK)]
-            for pair in ((0, 1), (2,), (3,)):
-                for j in (2, LAST):
-                    for r in pair:
-                        for g in range(PASSES):
-                            mix(sums[r][:, j - 2, :], j, r, g)
+            columns_of = result[:].rearrange("p r (h j i) -> p r j h i", h=HEADS, j=TILES)
+            ahead = mix_late(LATE_MIX_BANKS[0], (2,), (0, 1))
+            nc.scalar.copy(columns_of[:, 0:2, 2], ahead[:, :, 0])
             for r in range(PACK):
+                tiles = (LAST,) if r < 2 else (2, LAST)
+                sums = mix_late(LATE_MIX_BANKS[1 + r], tiles, (r,))
                 empty = nc.scalar.copy if r % 2 == 0 else nc.vector.tensor_copy
-                empty(late_columns[:, r, 2:TILES], sums[r][:].rearrange("p j (h i) -> p j h i", h=HEADS))
+                empty(columns_of[:, r, tiles[0] : TILES], sums[:, 0])
 
         on_vector, on_scalar = nc.vector.tensor_copy, nc.scalar.copy
         halves = (slice(0, HALF), slice(HALF, SLOTS))
@@ -286,14 +290,14 @@ def tile_attend_mqa_ownlists_gated_kernel(tc, query, keys_words, keys_scales, th
         score(2)
         score(3)
         keep_scores(1, 0, on_vector)
+        keep_scores(1, 1, on_vector)
         for half in halves:
             gate(0, half)
             place(0, half)
-        weave_values(0, slice(0, P // 2), on_gpsimd)
-        weave_values(0, slice(P // 2, P), on_gpsimd)
-        weave_values(1, slice(0, SHARED // 2), on_gpsimd)
-        weave_values(1, slice(SHARED // 2, SHARED), on_gpsimd)
-        keep_scores(1, 1, on_scalar)
+        for g in range(PASSES):
+            for groups in (slice(0, P // 2), slice(P // 2, P)):
+                weave_values(g, groups)
+        keep_scores(1, 2, on_scalar)
         gate(1)
         place(1)
         turn(0)
@@ -308,18 +312,18 @@ def tile_attend_mqa_ownlists_gated_kernel(tc, query, keys_words, keys_scales, th
         gate(3, halves[0])
         place(3, halves[0])
         turn(2)
-        weave_values(1, slice(SHARED, P), on_scalar)
         for g in range(PASSES):
             weigh_on_scalar(0, g)
-        for g in range(PASSES):
-            weave_weights(0, g)
+        weave_weights(0, 1)
         spread = [spread_factors(g) for g in range(PASSES)]
-        quantise_weights(0, early_woven[0])
         v_codes = keep.tile([P, PASSES * E], U32, name="v_codes", align_bytes=64)
         v_scales = keep.tile([P, PASSES * E], U8, name="v_scales", align_bytes=64)
         nc.vector.quantize_mx(v_codes[:].bitcast(FP8X4), v_scales[:], v_woven[:])
         gate(3, halves[1])
-        place(3, halves[1])
+        weave_weights(0, 0)
+        place(3, slice(HALF, HALF + P))
+        quantise_weights(0, early_woven[0])
+        place(3, slice(HALF + P, SLOTS))
         mix_tile(0)
         for g in range(PASSES):
             weigh_on_scalar(1, g)
@@ -331,30 +335,34 @@ def tile_attend_mqa_ownlists_gated_kernel(tc, query, keys_words, keys_scales, th
         weigh_last(spread)
         weigh_on_vector(2, 0)
         keep_tile(0, on_scalar)
+        mix_tile(1, 0)
         turn_last()
-        mix_tile(1)
+        mix_tile(1, 1)
         quantise_weights(2 * PASSES + 1, w_woven[2, 1])
         quantise_weights(2 * PASSES, w_woven[2, 0])
         for g in range(PASSES):
             quantise_weights(LAST * PASSES + g, w_woven[LAST, g])
-        keep_tile(1, on_scalar)
+        keep_tile(1, on_scalar, 0)
+        keep_tile(1, on_scalar, 1)
         for j in range(2):
             weave_result(on_vector, slice(j, j + 1), slice(0, HEADS))
         mix_late_tiles()
-        weave_result(on_vector, slice(2, TILES), slice(0, HEADS // 2))
-        weave_result(on_scalar, slice(2, TILES), slice(HEADS // 2, HEADS))
+        for heads in (slice(0, 2), slice(2, 5)):
+            weave_result(on_vector, slice(2, TILES), heads)
+        weave_result(on_scalar, slice(2, TILES), slice(5, HEADS))
 
         out_rows = out_0.rearrange("(p r) q -> p r q", r=PACK)
-        for rows in (slice(0, 1), slice(1, 2), slice(2, PACK)):
-            nc.sync.dma_start(out_rows[:, rows], result[:, rows])
+        for r in range(PACK):
+            nc.sync.dma_start(out_rows[:, r], result[:, r])
         o_codes = keep.tile([P, Q], U32, name="o_codes", align_bytes=64)
         o_scales = keep.tile([P, Q], U8, name="o_scales", align_bytes=64)
-        for half in range(2):
-            cols = slice(half * Q // 2, (half + 1) * Q // 2)
-            nc.vector.quantize_mx(o_codes[:, cols].bitcast(FP8X4), o_scales[:, cols], o_woven[:, cols].rearrange("p q r -> p (q r)"))
+        for parts in ((slice(0, P), slice(P, 2 * P)), (slice(2 * P, Q),)):
+            for cols in parts:
+                nc.vector.quantize_mx(o_codes[:, cols].bitcast(FP8X4), o_scales[:, cols], o_woven[:, cols].rearrange("p q r -> p (q r)"))
         nc.sync.dma_start(out_1[0].rearrange("p q r -> p (q r)").bitcast(I32), o_codes[:].bitcast(I32))
         for quad in range(4):
-            nc.sync.dma_start(
+            queue = nc.sync if quad % 2 == 0 else nc.scalar
+            queue.dma_start(
                 out_2[0, quad:16:4, :].bitcast(I32),
                 o_scales[quad:P:QUAD, :].bitcast(I32),
             )

@@ -36,10 +36,10 @@ SCORE_PIECES = (
     ((0, BANK, 6), (BANK, BANK, 7)),
     ((0, BANK, 0), (BANK, BANK, 1)),
 )
-TURN_BANKS = (2, 4, 6, 4)
-FACTOR_BANKS = 2
-MIX_BANKS = ((0,), (1, 3))
-LATE_MIX_BANKS = (7, 2, 4, 0, 6)
+TURN_BANKS = (2, 6, 0, 6)
+FACTOR_BANKS = 4
+MIX_BANKS = ((2,), (3,))
+LATE_MIX_BANKS = (1, 4, 6, 2, 0)
 OVERLAP_START = 11 * GROUP
 
 
@@ -74,14 +74,13 @@ def tile_attend_mqa_ownlists_gated_kernel(tc, query, keys_words, keys_scales, th
         nc.sync.dma_start(k_words[:].bitcast(I32), keys_words[0].bitcast(I32))
         offsets = keep.tile([P, SLOTS // GROUP], U16, name="offsets")
         nc.sync.dma_start(offsets[:], offs)
+        fac_col = keep.tile([P, PASSES, PACK], F32, name="fac_col")
+        nc.sync.dma_start(fac_col[:], fac.rearrange("(g p r) o -> p g (r o)", g=PASSES, r=PACK))
         first_values = keep.tile([P, PACK * E], F32, name="first_values", align_bytes=64)
-        second_values = keep.tile([P, SLOTS + PACK * E], F32, name="second_values", align_bytes=64)
+        second_values = keep.tile([P, SLOTS // 2 + PACK * E], F32, name="second_values", align_bytes=64)
         v_raw = [first_values[:], second_values[:, SLOTS // 2 : SLOTS // 2 + PACK * E]]
         for g in range(PASSES):
             nc.sync.dma_start(v_raw[g], vals[g * K_PASS : (g + 1) * K_PASS, :].rearrange("(p t) e -> p (t e)", t=PACK))
-
-        fac_col = keep.tile([P, PASSES, PACK], F32, name="fac_col")
-        nc.sync.dma_start(fac_col[:], fac.rearrange("(g p r) o -> p g (r o)", g=PASSES, r=PACK))
 
         ones = keep.tile([P, QUAD], F32, name="ones")
         nc.vector.memset(ones[:], 1.0)
@@ -107,14 +106,15 @@ def tile_attend_mqa_ownlists_gated_kernel(tc, query, keys_words, keys_scales, th
         gates = [own("gates0"), own("gates1"), own("gates2"), second_values[:, :SLOTS]]
         last_weighted = own("last_weighted")
         first_planes = own("first_planes")
+        late_planes = keep.tile([P, HALF], F32, name="late_planes", tag="result", align_bytes=64)[:]
         planes = {
             (0, 0): first_planes[:, :HALF],
             (0, 1): first_planes[:, HALF:],
-            (1, 0): own("second_planes", HALF),
+            (1, 0): late_planes,
             (1, 1): last_weighted[:, OVERLAP_START : OVERLAP_START + HALF],
-            (2, 1): second_values[:, 2 * SLOTS + HALF : 3 * SLOTS],
+            (2, 1): late_planes,
         }
-        early_woven = [second_values[:, PACK * E :], second_values[:, SLOTS : 2 * SLOTS]]
+        early_woven = [own("woven0"), second_values[:, SLOTS : 2 * SLOTS]]
         o_words = own("o_words", 2 * Q)
         o_woven = o_words.bitcast(BF16).rearrange("p (q r) -> p q r", r=PACK)
         w_woven = {(j, g): early_woven[j][:, g * HALF : (g + 1) * HALF] for j in range(2) for g in range(PASSES)}
@@ -124,8 +124,6 @@ def tile_attend_mqa_ownlists_gated_kernel(tc, query, keys_words, keys_scales, th
         w_scales = keep.tile([P, TILES * PASSES * P], U8, name="w_scales", align_bytes=64)
         fac_tenth = keep.tile([P, PASSES, PACK], F32, name="fac_tenth")
         neg_th = keep.tile([P, TILES], F32, name="neg_th")
-        result = keep.tile([P, PACK, Q], F32, name="result")
-        result_by_tile = result[:].rearrange("p r (h j i) -> p j r h i", h=HEADS, j=TILES)
         turned, summed, columns, mixed = {}, {}, {}, {}
 
         def weave_queries(j, weave):
@@ -223,7 +221,7 @@ def tile_attend_mqa_ownlists_gated_kernel(tc, query, keys_words, keys_scales, th
         def weave_values(g, groups):
             woven = v_woven[:, g * PACK * E : (g + 1) * PACK * E].rearrange("p (r s t) -> p s r t", r=PACK, t=PACK)
             raw = v_raw[g].rearrange("p (t s r) -> p s r t", t=PACK, r=PACK)
-            nc.gpsimd.tensor_scalar(woven[:, groups], raw[:, groups], 1.0, 0.0, MULT, ADD)
+            nc.gpsimd.tensor_scalar(woven[:, :, groups], raw[:, :, groups], 1.0, 0.0, MULT, ADD)
 
         def mix(sums, j, r, g):
             cols = slice((PASSES * j + g) * P, (PASSES * j + g + 1) * P)
@@ -294,8 +292,10 @@ def tile_attend_mqa_ownlists_gated_kernel(tc, query, keys_words, keys_scales, th
         for half in halves:
             gate(0, half)
             place(0, half)
+        nc.gpsimd.tensor_scalar(fac_tenth[:], fac_col[:], 0.1, 0.0, MULT, ADD)
+        spread = [spread_factors(g) for g in range(PASSES)]
         for g in range(PASSES):
-            for groups in (slice(0, P // 2), slice(P // 2, P)):
+            for groups in (slice(0, 2), slice(2, PACK)):
                 weave_values(g, groups)
         keep_scores(1, 2, on_scalar)
         gate(1)
@@ -308,22 +308,19 @@ def tile_attend_mqa_ownlists_gated_kernel(tc, query, keys_words, keys_scales, th
         turn(1)
         keep_scores(3, 0, on_scalar)
         keep_scores(3, 1, on_scalar)
-        nc.scalar.activation(fac_tenth[:], fac_col[:], COPY, scale=0.1)
         gate(3, halves[0])
         place(3, halves[0])
         turn(2)
         for g in range(PASSES):
             weigh_on_scalar(0, g)
-        weave_weights(0, 1)
-        spread = [spread_factors(g) for g in range(PASSES)]
+        for g in range(PASSES):
+            weave_weights(0, g)
+        quantise_weights(0, early_woven[0])
         v_codes = keep.tile([P, PASSES * E], U32, name="v_codes", align_bytes=64)
         v_scales = keep.tile([P, PASSES * E], U8, name="v_scales", align_bytes=64)
         nc.vector.quantize_mx(v_codes[:].bitcast(FP8X4), v_scales[:], v_woven[:])
         gate(3, halves[1])
-        weave_weights(0, 0)
-        place(3, slice(HALF, HALF + P))
-        quantise_weights(0, early_woven[0])
-        place(3, slice(HALF + P, SLOTS))
+        place(3, halves[1])
         mix_tile(0)
         for g in range(PASSES):
             weigh_on_scalar(1, g)
@@ -334,16 +331,16 @@ def tile_attend_mqa_ownlists_gated_kernel(tc, query, keys_words, keys_scales, th
         weave_weights(2, 1)
         weigh_last(spread)
         weigh_on_vector(2, 0)
+        result = keep.tile([P, PACK, Q], F32, name="result", tag="result", align_bytes=64)
+        result_by_tile = result[:].rearrange("p r (h j i) -> p j r h i", h=HEADS, j=TILES)
         keep_tile(0, on_scalar)
-        mix_tile(1, 0)
+        mix_tile(1)
         turn_last()
-        mix_tile(1, 1)
         quantise_weights(2 * PASSES + 1, w_woven[2, 1])
         quantise_weights(2 * PASSES, w_woven[2, 0])
         for g in range(PASSES):
             quantise_weights(LAST * PASSES + g, w_woven[LAST, g])
-        keep_tile(1, on_scalar, 0)
-        keep_tile(1, on_scalar, 1)
+        keep_tile(1, on_scalar)
         for j in range(2):
             weave_result(on_vector, slice(j, j + 1), slice(0, HEADS))
         mix_late_tiles()

@@ -30,6 +30,7 @@ LAST = TILES - 1
 PASSES = T // K_PASS
 BANK = 512
 WINDOWS = 3
+SHARED = 96
 SCORE_PIECES = (
     ((0, 256, 0), (256, 256, 1), (512, 256, 2), (768, 128, 3), (896, 128, 7)),
     ((0, BANK, 4), (BANK, 256, 5), (768, 256, 0)),
@@ -75,12 +76,13 @@ def tile_attend_mqa_ownlists_gated_kernel(tc, query, keys_words, keys_scales, th
         offsets = keep.tile([P, SLOTS // GROUP], U16, name="offsets")
         nc.sync.dma_start(offsets[:], offs)
         fac_col = keep.tile([P, PASSES, PACK], F32, name="fac_col")
-        nc.sync.dma_start(fac_col[:], fac.rearrange("(g p r) o -> p g (r o)", g=PASSES, r=PACK))
         first_values = keep.tile([P, PACK * E], F32, name="first_values", align_bytes=64)
         second_values = keep.tile([P, SLOTS // 2 + PACK * E], F32, name="second_values", align_bytes=64)
         v_raw = [first_values[:], second_values[:, SLOTS // 2 : SLOTS // 2 + PACK * E]]
         for g in range(PASSES):
             nc.sync.dma_start(v_raw[g], vals[g * K_PASS : (g + 1) * K_PASS, :].rearrange("(p t) e -> p (t e)", t=PACK))
+            if g == 0:
+                nc.sync.dma_start(fac_col[:], fac.rearrange("(g p r) o -> p g (r o)", g=PASSES, r=PACK))
 
         ones = keep.tile([P, QUAD], F32, name="ones")
         nc.vector.memset(ones[:], 1.0)
@@ -105,7 +107,7 @@ def tile_attend_mqa_ownlists_gated_kernel(tc, query, keys_words, keys_scales, th
         v_woven = keep.tile([P, PASSES * PACK * E], BF16, name="v_woven", align_bytes=64)
         gates = [own("gates0"), own("gates1"), own("gates2"), second_values[:, :SLOTS]]
         last_weighted = own("last_weighted")
-        first_planes = own("first_planes")
+        first_planes = keep.tile([P, SLOTS], F32, name="first_planes", tag="first_planes", align_bytes=64)[:]
         late_planes = keep.tile([P, HALF], F32, name="late_planes", tag="result", align_bytes=64)[:]
         planes = {
             (0, 0): first_planes[:, :HALF],
@@ -218,10 +220,15 @@ def tile_attend_mqa_ownlists_gated_kernel(tc, query, keys_words, keys_scales, th
             cols = slice(first * P, first * P + woven.shape[1] // 2)
             nc.vector.quantize_mx(w_codes[:, cols].bitcast(FP8X4), w_scales[:, cols], woven.bitcast(BF16))
 
-        def weave_values(g, groups):
+        def value_views(g, columns):
             woven = v_woven[:, g * PACK * E : (g + 1) * PACK * E].rearrange("p (r s t) -> p s r t", r=PACK, t=PACK)
             raw = v_raw[g].rearrange("p (t s r) -> p s r t", t=PACK, r=PACK)
-            nc.gpsimd.tensor_scalar(woven[:, :, groups], raw[:, :, groups], 1.0, 0.0, MULT, ADD)
+            return woven[:, columns], raw[:, columns]
+
+        def weave_values(g, columns):
+            woven, raw = value_views(g, columns)
+            for r in range(PACK):
+                nc.gpsimd.tensor_scalar(woven[:, :, r], raw[:, :, r], 1.0, 0.0, MULT, ADD)
 
         def mix(sums, j, r, g):
             cols = slice((PASSES * j + g) * P, (PASSES * j + g + 1) * P)
@@ -292,14 +299,13 @@ def tile_attend_mqa_ownlists_gated_kernel(tc, query, keys_words, keys_scales, th
         for half in halves:
             gate(0, half)
             place(0, half)
-        nc.gpsimd.tensor_scalar(fac_tenth[:], fac_col[:], 0.1, 0.0, MULT, ADD)
-        spread = [spread_factors(g) for g in range(PASSES)]
-        for g in range(PASSES):
-            for groups in (slice(0, 2), slice(2, PACK)):
-                weave_values(g, groups)
+        weave_values(0, slice(0, P))
+        weave_values(1, slice(0, SHARED))
         keep_scores(1, 2, on_scalar)
         gate(1)
         place(1)
+        nc.scalar.activation(fac_tenth[:], fac_col[:], COPY, scale=0.1)
+        spread = [spread_factors(g) for g in range(PASSES)]
         turn(0)
         keep_scores(2, 0, on_scalar)
         keep_scores(2, 1, on_scalar)
@@ -311,12 +317,13 @@ def tile_attend_mqa_ownlists_gated_kernel(tc, query, keys_words, keys_scales, th
         gate(3, halves[0])
         place(3, halves[0])
         turn(2)
+        on_scalar(*value_views(1, slice(SHARED, P)))
         for g in range(PASSES):
             weigh_on_scalar(0, g)
         for g in range(PASSES):
             weave_weights(0, g)
         quantise_weights(0, early_woven[0])
-        v_codes = keep.tile([P, PASSES * E], U32, name="v_codes", align_bytes=64)
+        v_codes = keep.tile([P, PASSES * E], U32, name="v_codes", tag="first_planes", align_bytes=64)
         v_scales = keep.tile([P, PASSES * E], U8, name="v_scales", align_bytes=64)
         nc.vector.quantize_mx(v_codes[:].bitcast(FP8X4), v_scales[:], v_woven[:])
         gate(3, halves[1])

@@ -29,7 +29,7 @@ TILES = Q // P
 LAST = TILES - 1
 PASSES = T // K_PASS
 BANK = 512
-WINDOWS = 3
+WINDOWS = 2
 SHARED = 96
 SCORE_PIECES = (
     ((0, 256, 0), (256, 256, 1), (512, 256, 2), (768, 128, 3), (896, 128, 7)),

@@ -29,7 +29,8 @@ TILES = Q // P
 LAST = TILES - 1
 PASSES = T // K_PASS
 BANK = 512
-WINDOWS = 2
+WINDOWS = 3
+WINDOW_OF = (0, 1, 0, 2)
 SHARED = 96
 SCORE_PIECES = (
     ((0, 256, 0), (256, 256, 1), (512, 256, 2), (768, 128, 3), (896, 128, 7)),
@@ -88,14 +89,14 @@ def tile_attend_mqa_ownlists_gated_kernel(tc, query, keys_words, keys_scales, th
         nc.vector.memset(ones[:], 1.0)
         warm = keep.tile([P, 1], F32, name="warm")
         nc.scalar.activation(warm[:], ones[:, 0:1], SIGMOID)
-        column_number = keep.tile([P, QUAD], F32, name="column_number", tag="window0", align_bytes=64)
+        column_number = keep.tile([P, QUAD], F32, name="column_number", align_bytes=64)
         nc.vector.tensor_tensor_scan(column_number[:], ones[:], ones[:], 0.0, MULT, ADD)
-        row_number = keep.tile([P, QUAD], F32, name="row_number", tag="window1", align_bytes=64)
+        row_number = keep.tile([P, QUAD], F32, name="row_number", align_bytes=64)
         nc.vector.transpose(row_number[:], column_number[:])
         for quad in range(4):
             rows = slice(QUAD * quad, QUAD * (quad + 1))
             nc.vector.tensor_tensor(ident[rows, rows], column_number[rows, :], row_number[rows, :], EQUAL)
-        windows = [keep.tile([P, T], F32, name="window%d" % w, tag="window%d" % w, align_bytes=64) for w in range(WINDOWS)]
+        windows = [keep.tile([P, T], F32, name="window%d" % w, align_bytes=64) for w in range(WINDOWS)]
         for window in windows:
             nc.vector.memset(window[:].bitcast(I32), 0)
 
@@ -105,7 +106,8 @@ def tile_attend_mqa_ownlists_gated_kernel(tc, query, keys_words, keys_scales, th
         HALF = SLOTS // 2
         q_woven, q_codes, q_scales, scores = {}, {}, {}, {}
         v_woven = keep.tile([P, PASSES * PACK * E], BF16, name="v_woven", align_bytes=64)
-        gates = [own("gates0"), own("gates1"), own("gates2"), second_values[:, :SLOTS]]
+        gates = {(0, 0): own("gates0", HALF), (1, 0): own("gates1"), (2, 0): own("gates2")}
+        gates.update({(LAST, 0): second_values[:, :HALF], (LAST, HALF): second_values[:, HALF:SLOTS]})
         last_weighted = own("last_weighted")
         first_planes = keep.tile([P, SLOTS], F32, name="first_planes", tag="first_planes", align_bytes=64)[:]
         late_planes = keep.tile([P, HALF], F32, name="late_planes", tag="result", align_bytes=64)[:]
@@ -171,17 +173,33 @@ def tile_attend_mqa_ownlists_gated_kernel(tc, query, keys_words, keys_scales, th
 
         def gate(j, part=slice(0, SLOTS)):
             listed = offsets[:, part.start // GROUP : part.stop // GROUP]
-            nc.scalar.activation(gates[j][:, part], scores[j][:].indirect(listed), SIGMOID, bias=neg_th[:, j : j + 1])
+            nc.scalar.activation(gates[j, part.start], scores[j][:].indirect(listed), SIGMOID, bias=neg_th[:, j : j + 1])
 
-        def place(j, part=slice(0, SLOTS)):
+        def place(j, part=slice(0, SLOTS), window=None):
             listed = offsets[:, part.start // GROUP : part.stop // GROUP]
-            nc.vector.tensor_copy(windows[j % WINDOWS][:].indirect(listed), gates[j][:, part])
+            window = windows[WINDOW_OF[j]] if window is None else window
+            nc.vector.tensor_copy(window[:].indirect(listed), gates[j, part.start])
+
+        def turn_first_tile(parts):
+            for g in range(PASSES):
+                turned[0, g] = bank(TURN_BANKS[0] + g, [P, PACK, P])
+            for n, window in enumerate(parts):
+                for g in range(PASSES):
+                    for r in range(PACK):
+                        nc.tensor.matmul(
+                            turned[0, g][:, r, :],
+                            window[:, g * K_PASS + r : (g + 1) * K_PASS : PACK],
+                            ident[:],
+                            is_transpose=True,
+                            start=(n == 0 and r == 0),
+                            stop=(n == len(parts) - 1 and r == PACK - 1),
+                        )
 
         def turn(j):
             for g in range(PASSES):
                 turned[j, g] = bank(TURN_BANKS[j] + g, [P, PACK, P])
                 for r in range(PACK):
-                    nc.tensor.transpose(turned[j, g][:, r, :], windows[j % WINDOWS][:, g * K_PASS + r : (g + 1) * K_PASS : PACK], ident[:])
+                    nc.tensor.transpose(turned[j, g][:, r, :], windows[WINDOW_OF[j]][:, g * K_PASS + r : (g + 1) * K_PASS : PACK], ident[:])
 
         def weigh_on_scalar(j, g, places=range(PACK)):
             rows = planes[j, g].bitcast(BF16).rearrange("p (r q) -> p r q", r=PACK)
@@ -204,7 +222,7 @@ def tile_attend_mqa_ownlists_gated_kernel(tc, query, keys_words, keys_scales, th
 
         def weigh_last(spread):
             ordered = last_weighted.bitcast(BF16).rearrange("q (g u p e) -> q g u p e", g=PASSES, u=2, e=2)
-            placed = windows[LAST % WINDOWS][:].rearrange("q (g p u e) -> q g u p e", g=PASSES, u=2, e=2)
+            placed = windows[WINDOW_OF[LAST]][:].rearrange("q (g p u e) -> q g u p e", g=PASSES, u=2, e=2)
             nc.vector.tensor_tensor(ordered[:, 0], placed[:, 0], spread[0], MULT)
             for u in range(2):
                 nc.vector.tensor_tensor(ordered[:, 1, u], placed[:, 1, u], spread[1][:, u], MULT)
@@ -296,17 +314,20 @@ def tile_attend_mqa_ownlists_gated_kernel(tc, query, keys_words, keys_scales, th
         score(3)
         keep_scores(1, 0, on_vector)
         keep_scores(1, 1, on_vector)
-        for half in halves:
-            gate(0, half)
-            place(0, half)
+        first_parts = (windows[0], windows[2])
+        gate(0, halves[0])
+        place(0, halves[0], first_parts[0])
+        keep_scores(1, 2, on_scalar)
+        gates[0, HALF] = keep.tile([P, HALF], F32, name="late_gates0", tag="q_codes1", align_bytes=64)[:]
+        gate(0, halves[1])
+        place(0, halves[1], first_parts[1])
         weave_values(0, slice(0, P))
         weave_values(1, slice(0, SHARED))
-        keep_scores(1, 2, on_scalar)
         gate(1)
         place(1)
         nc.scalar.activation(fac_tenth[:], fac_col[:], COPY, scale=0.1)
         spread = [spread_factors(g) for g in range(PASSES)]
-        turn(0)
+        turn_first_tile(first_parts)
         keep_scores(2, 0, on_scalar)
         keep_scores(2, 1, on_scalar)
         gate(2)

@@ -31,7 +31,6 @@ PASSES = T // K_PASS
 BANK = 512
 WINDOWS = 3
 WINDOW_OF = (0, 1, 0, 2)
-SHARED = 96
 SCORE_PIECES = (
     ((0, 256, 0), (256, 256, 1), (512, 256, 2), (768, 128, 3), (896, 128, 7)),
     ((0, BANK, 4), (BANK, 256, 5), (768, 256, 0)),
@@ -41,7 +40,7 @@ SCORE_PIECES = (
 TURN_BANKS = (2, 6, 0, 6)
 FACTOR_BANKS = 4
 MIX_BANKS = ((2,), (3,))
-LATE_MIX_BANKS = (1, 4, 6, 2, 0)
+LATE_MIX_BANKS = ((1, 4, 6), (2, 0, 5))
 OVERLAP_START = 11 * GROUP
 
 
@@ -77,13 +76,13 @@ def tile_attend_mqa_ownlists_gated_kernel(tc, query, keys_words, keys_scales, th
         offsets = keep.tile([P, SLOTS // GROUP], U16, name="offsets")
         nc.sync.dma_start(offsets[:], offs)
         fac_col = keep.tile([P, PASSES, PACK], F32, name="fac_col")
-        first_values = keep.tile([P, PACK * E], F32, name="first_values", align_bytes=64)
+        first_values = [keep.tile([P, PACK, E // 2], F32, name="first_values%d" % half, align_bytes=64) for half in range(2)]
         second_values = keep.tile([P, SLOTS // 2 + PACK * E], F32, name="second_values", align_bytes=64)
-        v_raw = [first_values[:], second_values[:, SLOTS // 2 : SLOTS // 2 + PACK * E]]
-        for g in range(PASSES):
-            nc.sync.dma_start(v_raw[g], vals[g * K_PASS : (g + 1) * K_PASS, :].rearrange("(p t) e -> p (t e)", t=PACK))
-            if g == 0:
-                nc.sync.dma_start(fac_col[:], fac.rearrange("(g p r) o -> p g (r o)", g=PASSES, r=PACK))
+        second_raw = second_values[:, SLOTS // 2 :]
+        for piece, columns_of in zip(first_values, (slice(0, E // 2), slice(E // 2, E))):
+            nc.sync.dma_start(piece[:], vals[:K_PASS, columns_of].rearrange("(p t) e -> p t e", t=PACK))
+        nc.sync.dma_start(fac_col[:], fac.rearrange("(g p r) o -> p g (r o)", g=PASSES, r=PACK))
+        nc.sync.dma_start(second_raw, vals[K_PASS:, :].rearrange("(p t) e -> p (t e)", t=PACK))
 
         ones = keep.tile([P, QUAD], F32, name="ones")
         nc.vector.memset(ones[:], 1.0)
@@ -116,13 +115,13 @@ def tile_attend_mqa_ownlists_gated_kernel(tc, query, keys_words, keys_scales, th
             (0, 1): first_planes[:, HALF:],
             (1, 0): late_planes,
             (1, 1): last_weighted[:, OVERLAP_START : OVERLAP_START + HALF],
-            (2, 1): late_planes,
+            (2, 0): late_planes,
+            (2, 1): second_values[:, 2 * SLOTS : 2 * SLOTS + HALF],
         }
-        early_woven = [own("woven0"), second_values[:, SLOTS : 2 * SLOTS]]
+        early_woven = [own("woven0"), second_values[:, SLOTS : 2 * SLOTS], own("woven2")]
         o_words = own("o_words", 2 * Q)
         o_woven = o_words.bitcast(BF16).rearrange("p (q r) -> p q r", r=PACK)
-        w_woven = {(j, g): early_woven[j][:, g * HALF : (g + 1) * HALF] for j in range(2) for g in range(PASSES)}
-        w_woven.update({(2, 0): early_woven[1][:, :HALF], (2, 1): own("woven2", HALF)})
+        w_woven = {(j, g): early_woven[j][:, g * HALF : (g + 1) * HALF] for j in range(LAST) for g in range(PASSES)}
         w_woven.update({(LAST, g): o_words[:, g * HALF : (g + 1) * HALF] for g in range(PASSES)})
         w_codes = keep.tile([P, TILES * PASSES * P], U32, name="w_codes", align_bytes=64)
         w_scales = keep.tile([P, TILES * PASSES * P], U8, name="w_scales", align_bytes=64)
@@ -212,14 +211,6 @@ def tile_attend_mqa_ownlists_gated_kernel(tc, query, keys_words, keys_scales, th
                 planes[j, g].bitcast(BF16).rearrange("p (r c i) -> p c r i", r=PACK, i=4),
             )
 
-        def weigh_on_vector(j, g):
-            nc.vector.tensor_tensor(
-                w_woven[j, g].bitcast(BF16).rearrange("p (q r) -> p q r", r=PACK),
-                turned[j, g][:].rearrange("p r q -> p q r"),
-                fac_tenth[:, g : g + 1, :].to_broadcast([P, P, PACK]),
-                MULT,
-            )
-
         def weigh_last(spread):
             ordered = last_weighted.bitcast(BF16).rearrange("q (g u p e) -> q g u p e", g=PASSES, u=2, e=2)
             placed = windows[WINDOW_OF[LAST]][:].rearrange("q (g p u e) -> q g u p e", g=PASSES, u=2, e=2)
@@ -238,15 +229,11 @@ def tile_attend_mqa_ownlists_gated_kernel(tc, query, keys_words, keys_scales, th
             cols = slice(first * P, first * P + woven.shape[1] // 2)
             nc.vector.quantize_mx(w_codes[:, cols].bitcast(FP8X4), w_scales[:, cols], woven.bitcast(BF16))
 
-        def value_views(g, columns):
-            woven = v_woven[:, g * PACK * E : (g + 1) * PACK * E].rearrange("p (r s t) -> p s r t", r=PACK, t=PACK)
-            raw = v_raw[g].rearrange("p (t s r) -> p s r t", t=PACK, r=PACK)
-            return woven[:, columns], raw[:, columns]
+        def woven_values(g):
+            return v_woven[:, g * PACK * E : (g + 1) * PACK * E].rearrange("p (r s t) -> p r s t", r=PACK, t=PACK)
 
-        def weave_values(g, columns):
-            woven, raw = value_views(g, columns)
-            for r in range(PACK):
-                nc.gpsimd.tensor_scalar(woven[:, :, r], raw[:, :, r], 1.0, 0.0, MULT, ADD)
+        def weave_values(woven, raw):
+            nc.gpsimd.tensor_scalar(woven, raw, 1.0, 0.0, MULT, ADD)
 
         def mix(sums, j, r, g):
             cols = slice((PASSES * j + g) * P, (PASSES * j + g + 1) * P)
@@ -288,13 +275,13 @@ def tile_attend_mqa_ownlists_gated_kernel(tc, query, keys_words, keys_scales, th
 
         def mix_late_tiles():
             columns_of = result[:].rearrange("p r (h j i) -> p r j h i", h=HEADS, j=TILES)
-            ahead = mix_late(LATE_MIX_BANKS[0], (2,), (0, 1))
-            nc.scalar.copy(columns_of[:, 0:2, 2], ahead[:, :, 0])
-            for r in range(PACK):
-                tiles = (LAST,) if r < 2 else (2, LAST)
-                sums = mix_late(LATE_MIX_BANKS[1 + r], tiles, (r,))
-                empty = nc.scalar.copy if r % 2 == 0 else nc.vector.tensor_copy
-                empty(columns_of[:, r, tiles[0] : TILES], sums[:, 0])
+            for pair in range(2):
+                groups = (2 * pair, 2 * pair + 1)
+                ahead = mix_late(LATE_MIX_BANKS[pair][0], (2,), groups)
+                nc.scalar.copy(columns_of[:, groups[0] : groups[1] + 1, 2], ahead[:, :, 0])
+                for r, empty in zip(groups, (nc.scalar.copy, nc.vector.tensor_copy)):
+                    sums = mix_late(LATE_MIX_BANKS[pair][1 + r % 2], (LAST,), (r,))
+                    empty(columns_of[:, r, LAST], sums[:, 0, 0])
 
         on_vector, on_scalar = nc.vector.tensor_copy, nc.scalar.copy
         halves = (slice(0, HALF), slice(HALF, SLOTS))
@@ -321,8 +308,14 @@ def tile_attend_mqa_ownlists_gated_kernel(tc, query, keys_words, keys_scales, th
         gates[0, HALF] = keep.tile([P, HALF], F32, name="late_gates0", tag="q_codes1", align_bytes=64)[:]
         gate(0, halves[1])
         place(0, halves[1], first_parts[1])
-        weave_values(0, slice(0, P))
-        weave_values(1, slice(0, SHARED))
+        for half in range(2):
+            weave_values(
+                woven_values(0)[:, :, half * P // 2 : (half + 1) * P // 2],
+                first_values[half][:].rearrange("p t (s r) -> p r s t", r=PACK),
+            )
+        second_dealt = second_raw.rearrange("p (t s r) -> p r s t", t=PACK, r=PACK)
+        for groups in (slice(0, 2), slice(2, PACK)):
+            weave_values(woven_values(1)[:, groups], second_dealt[:, groups])
         gate(1)
         place(1)
         nc.scalar.activation(fac_tenth[:], fac_col[:], COPY, scale=0.1)
@@ -338,7 +331,6 @@ def tile_attend_mqa_ownlists_gated_kernel(tc, query, keys_words, keys_scales, th
         gate(3, halves[0])
         place(3, halves[0])
         turn(2)
-        on_scalar(*value_views(1, slice(SHARED, P)))
         for g in range(PASSES):
             weigh_on_scalar(0, g)
         for g in range(PASSES):
@@ -355,17 +347,17 @@ def tile_attend_mqa_ownlists_gated_kernel(tc, query, keys_words, keys_scales, th
         for g in range(PASSES):
             weave_weights(1, g)
         quantise_weights(PASSES, early_woven[1])
-        weigh_on_scalar(2, 1)
-        weave_weights(2, 1)
+        for g in range(PASSES):
+            weigh_on_scalar(2, g)
+        for g in range(PASSES):
+            weave_weights(2, g)
         weigh_last(spread)
-        weigh_on_vector(2, 0)
+        quantise_weights(2 * PASSES, early_woven[2])
         result = keep.tile([P, PACK, Q], F32, name="result", tag="result", align_bytes=64)
         result_by_tile = result[:].rearrange("p r (h j i) -> p j r h i", h=HEADS, j=TILES)
         keep_tile(0, on_scalar)
         mix_tile(1)
         turn_last()
-        quantise_weights(2 * PASSES + 1, w_woven[2, 1])
-        quantise_weights(2 * PASSES, w_woven[2, 0])
         for g in range(PASSES):
             quantise_weights(LAST * PASSES + g, w_woven[LAST, g])
         keep_tile(1, on_scalar)
@@ -377,8 +369,8 @@ def tile_attend_mqa_ownlists_gated_kernel(tc, query, keys_words, keys_scales, th
         weave_result(on_scalar, slice(2, TILES), slice(5, HEADS))
 
         out_rows = out_0.rearrange("(p r) q -> p r q", r=PACK)
-        for r in range(PACK):
-            nc.sync.dma_start(out_rows[:, r], result[:, r])
+        for rows in (slice(0, 1), slice(1, 2), slice(2, PACK)):
+            nc.sync.dma_start(out_rows[:, rows], result[:, rows])
         o_codes = keep.tile([P, Q], U32, name="o_codes", align_bytes=64)
         o_scales = keep.tile([P, Q], U8, name="o_scales", align_bytes=64)
         for parts in ((slice(0, P), slice(P, 2 * P)), (slice(2 * P, Q),)):

from contextlib import ExitStack

import concourse.mybir as mybir

D, T, Q, SLOTS, E = 512, 1024, 512, 512, 512
FLOPS = 2 * D * Q * T + 2 * T * E * Q

F32 = mybir.dt.float32
BF16 = mybir.dt.bfloat16
I32 = mybir.dt.int32
U32 = mybir.dt.uint32
U16 = mybir.dt.uint16
U8 = mybir.dt.uint8
FP8X4 = mybir.dt.float8_e4m3fn_x4
FP4X4 = mybir.dt.float4_e2m1fn_x4
MULT = mybir.AluOpType.mult
ADD = mybir.AluOpType.add
EQUAL = mybir.AluOpType.is_equal
COPY = mybir.ActivationFunctionType.Copy
SIGMOID = mybir.ActivationFunctionType.Sigmoid

P = 128
QUAD = 32
PACK = 4
K_PASS = P * PACK
HEADS = 8
GROUP = 16
TILES = Q // P
LAST = TILES - 1
PASSES = T // K_PASS
BANK = 512
WINDOWS = 3
WINDOW_OF = (0, 1, 0, 2)
SCORE_PIECES = (
    ((0, 256, 0), (256, 256, 1), (512, 256, 2), (768, 128, 3), (896, 128, 7)),
    ((0, BANK, 4), (BANK, 256, 5), (768, 256, 0)),
    ((0, BANK, 6), (BANK, BANK, 7)),
    ((0, BANK, 0), (BANK, BANK, 1)),
)
TURN_BANKS = (2, 6, 0, 6)
FACTOR_BANKS = 4
MIX_BANKS = ((2,), (3,))
LATE_MIX_BANKS = ((1, 4, 6), (2, 0, 5))
OVERLAP_START = 11 * GROUP


def tile_attend_mqa_ownlists_gated_kernel(tc, query, keys_words, keys_scales, th, fac, vals, offs, out_0, out_1, out_2):
    nc = tc.nc
    with ExitStack() as ctx:
        keep = ctx.enter_context(tc.tile_pool(name="keep", bufs=1))
        psum = ctx.enter_context(tc.psum_pool(name="psum", bufs=1))

        def bank(number, shape):
            return psum.tile(shape, F32, name="bank%d" % number)

        k_scales = keep.tile([P, T], U8, name="k_scales", align_bytes=64)
        nc.gpsimd.memset(k_scales[:].bitcast(I32), 0)
        th_rows = keep.tile([P, P], F32, name="th_rows")
        nc.gpsimd.memset(th_rows[:], 0.0)
        ident = keep.tile([P, P], F32, name="ident")
        nc.gpsimd.memset(ident[:], 0.0)

        q_raw = keep.tile([P, PACK, Q], F32, name="q_raw")
        nc.sync.dma_start(q_raw[:], query.rearrange("(p t) q -> p t q", t=PACK))
        nc.sync.dma_start(
            th_rows[0:TILES, :].rearrange("j (h r) -> j h r", r=GROUP),
            th.rearrange("(h j r) o -> j h (r o)", h=HEADS, j=TILES),
        )
        for quad in range(4):
            nc.sync.dma_start(
                k_scales[quad:P:QUAD, :].bitcast(I32),
                keys_scales[0, quad:16:4, :].bitcast(I32),
            )
        k_words = keep.tile([P, 2 * T], U8, name="k_words", align_bytes=64)
        nc.sync.dma_start(k_words[:].bitcast(I32), keys_words[0].bitcast(I32))
        offsets = keep.tile([P, SLOTS // GROUP], U16, name="offsets")
        nc.sync.dma_start(offsets[:], offs)
        fac_col = keep.tile([P, PASSES, PACK], F32, name="fac_col")
        first_values = [keep.tile([P, PACK, E // 2], F32, name="first_values%d" % half, align_bytes=64) for half in range(2)]
        second_values = keep.tile([P, SLOTS // 2 + PACK * E], F32, name="second_values", align_bytes=64)
        second_raw = second_values[:, SLOTS // 2 :]
        for piece, columns_of in zip(first_values, (slice(0, E // 2), slice(E // 2, E))):
            nc.sync.dma_start(piece[:], vals[:K_PASS, columns_of].rearrange("(p t) e -> p t e", t=PACK))
        nc.sync.dma_start(fac_col[:], fac.rearrange("(g p r) o -> p g (r o)", g=PASSES, r=PACK))
        nc.sync.dma_start(second_raw, vals[K_PASS:, :].rearrange("(p t) e -> p (t e)", t=PACK))

        ones = keep.tile([P, QUAD], F32, name="ones")
        nc.vector.memset(ones[:], 1.0)
        warm = keep.tile([P, 1], F32, name="warm")
        nc.scalar.activation(warm[:], ones[:, 0:1], SIGMOID)
        column_number = keep.tile([P, QUAD], F32, name="column_number", align_bytes=64)
        nc.vector.tensor_tensor_scan(column_number[:], ones[:], ones[:], 0.0, MULT, ADD)
        row_number = keep.tile([P, QUAD], F32, name="row_number", align_bytes=64)
        nc.vector.transpose(row_number[:], column_number[:])
        for quad in range(4):
            rows = slice(QUAD * quad, QUAD * (quad + 1))
            nc.vector.tensor_tensor(ident[rows, rows], column_number[rows, :], row_number[rows, :], EQUAL)
        windows = [keep.tile([P, T], F32, name="window%d" % w, align_bytes=64) for w in range(WINDOWS)]
        for window in windows:
            nc.vector.memset(window[:].bitcast(I32), 0)

        def own(name, width=SLOTS):
            return keep.tile([P, width], F32, name=name, align_bytes=64)[:]

        HALF = SLOTS // 2
        q_woven, q_codes, q_scales, scores = {}, {}, {}, {}
        v_woven = keep.tile([P, PASSES * PACK * E], BF16, name="v_woven", align_bytes=64)
        gates = {(0, 0): own("gates0", HALF), (1, 0): own("gates1"), (2, 0): own("gates2")}
        gates.update({(LAST, 0): second_values[:, :HALF], (LAST, HALF): second_values[:, HALF:SLOTS]})
        last_weighted = own("last_weighted")
        first_planes = keep.tile([P, SLOTS], F32, name="first_planes", tag="first_planes", align_bytes=64)[:]
        late_planes = keep.tile([P, HALF], F32, name="late_planes", tag="result", align_bytes=64)[:]
        planes = {
            (0, 0): first_planes[:, :HALF],
            (0, 1): first_planes[:, HALF:],
            (1, 0): late_planes,
            (1, 1): last_weighted[:, OVERLAP_START : OVERLAP_START + HALF],
            (2, 0): late_planes,
            (2, 1): second_values[:, 2 * SLOTS : 2 * SLOTS + HALF],
        }
        early_woven = [own("woven0"), second_values[:, SLOTS : 2 * SLOTS], own("woven2")]
        o_words = own("o_words", 2 * Q)
        o_woven = o_words.bitcast(BF16).rearrange("p (q r) -> p q r", r=PACK)
        w_woven = {(j, g): early_woven[j][:, g * HALF : (g + 1) * HALF] for j in range(LAST) for g in range(PASSES)}
        w_woven.update({(LAST, g): o_words[:, g * HALF : (g + 1) * HALF] for g in range(PASSES)})
        w_codes = keep.tile([P, TILES * PASSES * P], U32, name="w_codes", align_bytes=64)
        w_scales = keep.tile([P, TILES * PASSES * P], U8, name="w_scales", align_bytes=64)
        fac_tenth = keep.tile([P, PASSES, PACK], F32, name="fac_tenth")
        neg_th = keep.tile([P, TILES], F32, name="neg_th")
        turned, summed, columns, mixed = {}, {}, {}, {}

        def weave_queries(j, weave):
            q_woven[j] = keep.tile([P, P, PACK], BF16, name="q_woven%d" % j, tag="q_woven%d" % (j // 2 * j), align_bytes=64)
            weave(
                q_woven[j][:].rearrange("p (h c i) t -> p h c t i", h=HEADS, i=4),
                q_raw[:].rearrange("p t (h j c i) -> p j h c t i", h=HEADS, j=TILES, i=4)[:, j],
            )

        def quantise_queries(j):
            q_codes[j] = keep.tile([P, P], U32, name="q_codes%d" % j, align_bytes=64)
            q_scales[j] = keep.tile([P, P], U8, name="q_scales%d" % j, align_bytes=64)
            nc.vector.quantize_mx(q_codes[j][:].bitcast(FP8X4), q_scales[j][:], q_woven[j][:].rearrange("p q t -> p (q t)"))

        def turn_thresholds():
            rows = bank(7, [P, P])
            nc.tensor.transpose(rows[:], th_rows[:], ident[:])
            nc.scalar.activation(neg_th[:], rows[:, 0:TILES], COPY, scale=-1.0)

        def spread_factors(g):
            spread = bank(FACTOR_BANKS + g, [P, PACK, P])
            for r in range(PACK):
                nc.tensor.transpose(spread[:, r, :], fac_tenth[:, g, r : r + 1].to_broadcast([P, P]), ident[:])
            return spread[:].rearrange("m (u e) n -> m u n e", u=2)

        def score(j):
            scores[j] = keep.tile([P, T], F32, name="scores%d" % j, tag="scores%d" % j, align_bytes=64)
            for h, (first, width, number) in enumerate(SCORE_PIECES[j]):
                summed[j, h] = bank(number, [P, width])
                columns[j, h] = slice(first, first + width)
                nc.tensor.matmul_mx(
                    summed[j, h][:],
                    lhsT=q_codes[j][:].bitcast(FP8X4),
                    lhsT_scale=q_scales[j][:],
                    rhs=k_words[:, 2 * first : 2 * (first + width)].bitcast(FP4X4),
                    rhs_scale=k_scales[:, columns[j, h]],
                    start=True,
                    stop=True,
                )

        def keep_scores(j, h, copy):
            copy(scores[j][:, columns[j, h]], summed[j, h][:])

        def gate(j, part=slice(0, SLOTS)):
            listed = offsets[:, part.start // GROUP : part.stop // GROUP]
            nc.scalar.activation(gates[j, part.start], scores[j][:].indirect(listed), SIGMOID, bias=neg_th[:, j : j + 1])

        def place(j, part=slice(0, SLOTS), window=None):
            listed = offsets[:, part.start // GROUP : part.stop // GROUP]
            window = windows[WINDOW_OF[j]] if window is None else window
            nc.vector.tensor_copy(window[:].indirect(listed), gates[j, part.start])

        def turn_first_tile(parts):
            for g in range(PASSES):
                turned[0, g] = bank(TURN_BANKS[0] + g, [P, PACK, P])
            for n, window in enumerate(parts):
                for g in range(PASSES):
                    for r in range(PACK):
                        nc.tensor.matmul(
                            turned[0, g][:, r, :],
                            window[:, g * K_PASS + r : (g + 1) * K_PASS : PACK],
                            ident[:],
                            is_transpose=True,
                            start=(n == 0 and r == 0),
                            stop=(n == len(parts) - 1 and r == PACK - 1),
                        )

        def turn(j):
            for g in range(PASSES):
                turned[j, g] = bank(TURN_BANKS[j] + g, [P, PACK, P])
                for r in range(PACK):
                    nc.tensor.transpose(turned[j, g][:, r, :], windows[WINDOW_OF[j]][:, g * K_PASS + r : (g + 1) * K_PASS : PACK], ident[:])

        def weigh_on_scalar(j, g, places=range(PACK)):
            rows = planes[j, g].bitcast(BF16).rearrange("p (r q) -> p r q", r=PACK)
            for r in places:
                nc.scalar.activation(rows[:, r, :], turned[j, g][:, r, :], COPY, scale=fac_tenth[:, g, r : r + 1])

        def weave_weights(j, g):
            nc.scalar.copy(
                w_woven[j, g].bitcast(BF16).rearrange("p (c i r) -> p c r i", i=4, r=PACK),
                planes[j, g].bitcast(BF16).rearrange("p (r c i) -> p c r i", r=PACK, i=4),
            )

        def weigh_last(spread):
            ordered = last_weighted.bitcast(BF16).rearrange("q (g u p e) -> q g u p e", g=PASSES, u=2, e=2)
            placed = windows[WINDOW_OF[LAST]][:].rearrange("q (g p u e) -> q g u p e", g=PASSES, u=2, e=2)
            nc.vector.tensor_tensor(ordered[:, 0], placed[:, 0], spread[0], MULT)
            for u in range(2):
                nc.vector.tensor_tensor(ordered[:, 1, u], placed[:, 1, u], spread[1][:, u], MULT)

        def turn_last():
            for g in range(PASSES):
                pairs = bank(TURN_BANKS[LAST] + g, [P, 2, P])
                for u in range(2):
                    nc.tensor.transpose(pairs[:, u, :], last_weighted[:, (2 * g + u) * P : (2 * g + u + 1) * P], ident[:])
                nc.scalar.copy(w_woven[LAST, g].rearrange("p (q u) -> p q u", u=2), pairs[:].rearrange("p u q -> p q u"))

        def quantise_weights(first, woven):
            cols = slice(first * P, first * P + woven.shape[1] // 2)
            nc.vector.quantize_mx(w_codes[:, cols].bitcast(FP8X4), w_scales[:, cols], woven.bitcast(BF16))

        def woven_values(g):
            return v_woven[:, g * PACK * E : (g + 1) * PACK * E].rearrange("p (r s t) -> p r s t", r=PACK, t=PACK)

        def weave_values(woven, raw):
            nc.gpsimd.tensor_scalar(woven, raw, 1.0, 0.0, MULT, ADD)

        def mix(sums, j, r, g):
            cols = slice((PASSES * j + g) * P, (PASSES * j + g + 1) * P)
            nc.tensor.matmul_mx(
                sums,
                lhsT=v_codes[:, g * E + r * P : g * E + (r + 1) * P].bitcast(FP8X4),
                lhsT_scale=v_scales[:, g * E + r * P : g * E + (r + 1) * P],
                rhs=w_codes[:, cols].bitcast(FP8X4),
                rhs_scale=w_scales[:, cols],
                start=(g == 0),
                stop=(g == PASSES - 1),
            )

        def weave_result(weave, tiles, heads):
            chunks = slice(PACK * tiles.start, PACK * tiles.stop)
            weave(
                o_woven.rearrange("p (h c i) r -> p h c r i", h=HEADS, i=4)[:, heads, chunks],
                result[:].rearrange("p r (h c i) -> p h c r i", h=HEADS, i=4)[:, heads, chunks],
            )

        def mix_tile(j, part=0):
            count = PACK // len(MIX_BANKS[j])
            mixed[j, part] = bank(MIX_BANKS[j][part], [P, count, P])
            for r in range(count):
                for g in range(PASSES):
                    mix(mixed[j, part][:, r, :], j, part * count + r, g)

        def keep_tile(j, copy, part=0):
            count = PACK // len(MIX_BANKS[j])
            copy(result_by_tile[:, j, part * count : (part + 1) * count], mixed[j, part][:].rearrange("p r (h i) -> p r h i", h=HEADS))

        def mix_late(number, tiles, groups):
            sums = bank(number, [P, len(groups), len(tiles), P])
            for b, j in enumerate(tiles):
                for a, r in enumerate(groups):
                    for g in range(PASSES):
                        mix(sums[:, a, b, :], j, r, g)
            return sums[:].rearrange("p r j (h i) -> p r j h i", h=HEADS)

        def mix_late_tiles():
            columns_of = result[:].rearrange("p r (h j i) -> p r j h i", h=HEADS, j=TILES)
            for pair in range(2):
                groups = (2 * pair, 2 * pair + 1)
                ahead = mix_late(LATE_MIX_BANKS[pair][0], (2,), groups)
                nc.scalar.copy(columns_of[:, groups[0] : groups[1] + 1, 2], ahead[:, :, 0])
                for r, empty in zip(groups, (nc.scalar.copy, nc.vector.tensor_copy)):
                    sums = mix_late(LATE_MIX_BANKS[pair][1 + r % 2], (LAST,), (r,))
                    empty(columns_of[:, r, LAST], sums[:, 0, 0])

        on_vector, on_scalar = nc.vector.tensor_copy, nc.scalar.copy
        halves = (slice(0, HALF), slice(HALF, SLOTS))
        turn_thresholds()
        weave_queries(0, on_vector)
        quantise_queries(0)
        weave_queries(1, on_vector)
        weave_queries(2, on_scalar)
        weave_queries(3, on_scalar)
        for j in range(1, TILES):
            quantise_queries(j)
        score(0)
        for h in range(len(SCORE_PIECES[0])):
            keep_scores(0, h, on_scalar if h % 2 == 0 else on_vector)
        score(1)
        score(2)
        score(3)
        keep_scores(1, 0, on_vector)
        keep_scores(1, 1, on_vector)
        first_parts = (windows[0], windows[2])
        gate(0, halves[0])
        place(0, halves[0], first_parts[0])
        keep_scores(1, 2, on_scalar)
        gates[0, HALF] = keep.tile([P, HALF], F32, name="late_gates0", tag="q_codes1", align_bytes=64)[:]
        gate(0, halves[1])
        place(0, halves[1], first_parts[1])
        for half in range(2):
            weave_values(
                woven_values(0)[:, :, half * P // 2 : (half + 1) * P // 2],
                first_values[half][:].rearrange("p t (s r) -> p r s t", r=PACK),
            )
        second_dealt = second_raw.rearrange("p (t s r) -> p r s t", t=PACK, r=PACK)
        for groups in (slice(0, 2), slice(2, PACK)):
            weave_values(woven_values(1)[:, groups], second_dealt[:, groups])
        gate(1)
        place(1)
        nc.scalar.activation(fac_tenth[:], fac_col[:], COPY, scale=0.1)
        spread = [spread_factors(g) for g in range(PASSES)]
        turn_first_tile(first_parts)
        keep_scores(2, 0, on_scalar)
        keep_scores(2, 1, on_scalar)
        gate(2)
        place(2)
        turn(1)
        keep_scores(3, 0, on_scalar)
        keep_scores(3, 1, on_scalar)
        gate(3, halves[0])
        place(3, halves[0])
        turn(2)
        for g in range(PASSES):
            weigh_on_scalar(0, g)
        for g in range(PASSES):
            weave_weights(0, g)
        quantise_weights(0, early_woven[0])
        v_codes = keep.tile([P, PASSES * E], U32, name="v_codes", tag="first_planes", align_bytes=64)
        v_scales = keep.tile([P, PASSES * E], U8, name="v_scales", align_bytes=64)
        nc.vector.quantize_mx(v_codes[:].bitcast(FP8X4), v_scales[:], v_woven[:])
        gate(3, halves[1])
        place(3, halves[1])
        mix_tile(0)
        for g in range(PASSES):
            weigh_on_scalar(1, g)
        for g in range(PASSES):
            weave_weights(1, g)
        quantise_weights(PASSES, early_woven[1])
        for g in range(PASSES):
            weigh_on_scalar(2, g)
        for g in range(PASSES):
            weave_weights(2, g)
        weigh_last(spread)
        quantise_weights(2 * PASSES, early_woven[2])
        result = keep.tile([P, PACK, Q], F32, name="result", tag="result", align_bytes=64)
        result_by_tile = result[:].rearrange("p r (h j i) -> p j r h i", h=HEADS, j=TILES)
        keep_tile(0, on_scalar)
        mix_tile(1)
        turn_last()
        for g in range(PASSES):
            quantise_weights(LAST * PASSES + g, w_woven[LAST, g])
        keep_tile(1, on_scalar)
        for j in range(2):
            weave_result(on_vector, slice(j, j + 1), slice(0, HEADS))
        mix_late_tiles()
        for heads in (slice(0, 2), slice(2, 5)):
            weave_result(on_vector, slice(2, TILES), heads)
        weave_result(on_scalar, slice(2, TILES), slice(5, HEADS))

        out_rows = out_0.rearrange("(p r) q -> p r q", r=PACK)
        for rows in (slice(0, 1), slice(1, 2), slice(2, PACK)):
            nc.sync.dma_start(out_rows[:, rows], result[:, rows])
        o_codes = keep.tile([P, Q], U32, name="o_codes", align_bytes=64)
        o_scales = keep.tile([P, Q], U8, name="o_scales", align_bytes=64)
        for parts in ((slice(0, P), slice(P, 2 * P)), (slice(2 * P, Q),)):
            for cols in parts:
                nc.vector.quantize_mx(o_codes[:, cols].bitcast(FP8X4), o_scales[:, cols], o_woven[:, cols].rearrange("p q r -> p (q r)"))
        nc.sync.dma_start(out_1[0].rearrange("p q r -> p (q r)").bitcast(I32), o_codes[:].bitcast(I32))
        for quad in range(4):
            queue = nc.sync if quad % 2 == 0 else nc.scalar
            queue.dma_start(
                out_2[0, quad:16:4, :].bitcast(I32),
                o_scales[quad:P:QUAD, :].bitcast(I32),
            )
